import numpy as np, ml_dtypes
CORES = [1,5,17,21,33,37,49,53]
N = 8
import mx_ref
BF = ml_dtypes.bfloat16
def gentries(a):
    return np.ascontiguousarray(a.reshape(8, 16, -1).transpose(0, 2, 1)).reshape(8, -1)
def gtable(e):
    e = np.asarray(e); return np.ascontiguousarray(e.reshape(8, -1, 16).transpose(0, 2, 1)).reshape(128, -1).astype(np.int32)
def gcols(t, e):
    v = np.concatenate([t.reshape(8, 16, -1, 4), np.zeros((8, 16, 1, 4), BF)], axis=2)
    return np.ascontiguousarray(np.stack([v[g][:, e[g]] for g in range(8)])).reshape(128, -1)
def gpick(z, e):
    return np.concatenate([z[16 * g:16 * g + 16][:, e[g]] for g in range(8)])
def pick(q, e):
    c = np.concatenate([q[0].reshape(128, -1, 4), np.zeros((128, 1, 4), np.uint8)], axis=1); s = np.concatenate([q[1], np.ones((16, 1), np.uint8)], axis=1)
    return (np.ascontiguousarray(c[:, e].reshape(128, -1)), np.ascontiguousarray(s[:, e]))
def join(*qs):
    return (np.concatenate([q[0] for q in qs], axis=1), np.concatenate([q[1] for q in qs], axis=1))
def put(q, e, v):
    c, s = q[0].reshape(128, -1, 4).copy(), q[1].copy(); c[:, e] = v[0].reshape(128, -1, 4); s[:, e] = v[1]
    return (c.reshape(128, -1), s)
def pk(c, s):
    return (np.ascontiguousarray(c), mx_ref.live(s))
def emit(q):
    return q[0], q[1]
def packed(v, rng):
    q = [mx_ref.quantize(np.ascontiguousarray(v[r])) for r in range(N)]
    return np.stack([a for a, b in q]), np.stack([mx_ref.plane(b, rng) for a, b in q])
def values_of_codes():
    e, c = np.zeros((128, 128, 4), np.float32), np.zeros((128, 2, 4), np.uint8)
    e[np.arange(128), np.arange(128), 0] = 1
    c[:127, :, 0] = np.arange(256).reshape(2, 128).T[:127]
    return mx_ref.matmul(mx_ref.quantize(e.reshape(128, 512).astype(BF)), (c.reshape(128, 8), np.full((16, 2), 127, np.uint8))).T.reshape(-1).astype(np.float64)
CODE_VALUE, SCALE_VALUE = values_of_codes(), 2.0 ** (np.arange(256) - 127.0)
def decode(q):
    return (CODE_VALUE[q[0]].reshape(16, 8, -1, 4) * SCALE_VALUE[q[1]][:, None, :, None] + 0.0).reshape(128, -1).astype(np.float32)
def f(rng, *shape):
    return mx_ref.flush((rng.standard_normal(shape, dtype=np.float32) * np.exp2(rng.integers(-2, 3, shape[:-1] + (1,)))).astype(BF))
def wide(rng, *shape, cols=0):
    v = rng.standard_normal(shape, dtype=np.float32) * np.exp2(rng.integers(-12, 13, shape)).astype(np.float32)
    if cols: v *= np.repeat(np.exp2(rng.integers(-cols, cols + 1, shape[:-2] + (1, shape[-1] // 4))) * (rng.random(shape[:-2] + (1, shape[-1] // 4)) > 0.0625), 4, axis=-1).astype(np.float32)
    return mx_ref.flush(v.astype(BF))
V, F, K, T = 512, 1024, 128, 3
def big(v, k):
    v = v.astype(np.float32) * np.float32(k)
    v[np.abs(v) < np.float32(2.0 ** -16)] = 0
    return v.astype(BF)
def weights(rng, k=1.0, still=slice(0)):
    v = big(f(rng, N, 128, 2048), k).reshape(N, 128, 4, 128, 4)
    v[:, :, :, still] = 0
    c, s = packed(v.reshape(N, 128, 2048), rng)
    return {"wc": c, "ws": s}
def lists_of(rng):
    return rng.permuted(np.tile(np.arange(F) % V, (N, 8, 1)), axis=2)
def stored(e):
    return np.stack([gtable(e[r]) for r in range(N)])
def numbers_of(rng):
    return {"x": big(f(rng, N, 128, 4 * V), 1), "fv": stored(lists_of(rng)), "u": np.array(f(rng, N, 128, 512)), "wy": np.array(f(rng, N, 128, 512))}
def planted(rng):
    at = 16 * rng.permutation(8)[:T]
    still = np.concatenate([np.arange(p, p + 16) for p in at])
    d = numbers_of(rng)
    x = d["x"].reshape(N, 128, V, 4)
    x[:, still] = 0
    d["u"][:, :, :4 * T] = 0
    d["u"][:, at, 4 * np.arange(T)] = 1
    return {**d, **weights(rng, 1.0, still)}, x, at
def setup_inputs(rng):
    return {**numbers_of(rng), **weights(rng)}
def setup_inputs_ties(rng):
    d, x, at = planted(rng)
    o = rng.permutation(N)
    none = int(rng.integers(T))
    for i in range(N):
        zero = i < N // 2
        for t in range(T):
            v = np.full(V, 0.0 if zero else 1.0, np.float32)
            j = rng.permutation(V)
            v[j[:K // 4]] = 2
            if zero: v[j[K // 4:K // 2]] = -2
            if i == 0: v *= np.float32(2.0 ** -24)
            if i == 0 and t == none: v[:] = 0
            if i == N - 1: v *= np.float32(2.0 ** 26)
            x[o[i], at[t], :, 0] = v.astype(BF)
    d["u"][o[0], at, 4 * np.arange(T)] = 2.0 ** -30
    d["u"][o[N - 1], at, 4 * np.arange(T)] = 2.0 ** 30
    return {**d, "x": x.reshape(N, 128, 4 * V)}
def setup_inputs_near(rng):
    d, x, at = planted(rng)
    e = lists_of(rng)
    sign = (rng.permutation(N) % 2 * 2.0 - 1.0).astype(np.float32).astype(BF)
    for t in range(T):
        p = int(at[t])
        e[:, p // 16] = np.arange(F) // 2
        d["u"][:, p + 1, 4 * t] = 2.0 ** 12
        d["u"][:, p + 8:p + 11, 4 * t:4 * t + 4] = 1
        x[:, p, :, 0] = sign[:, None]
        for r in range(N):
            s = np.argsort(np.argsort(np.arange(V) + 16 * rng.random(V)))
            s = (s + int(rng.integers(1, V // 4))) % V
            v = (((s[:, None] >> np.arange(12)) & 1) * np.exp2(np.arange(12) - 23.0)).astype(np.float32).astype(BF)
            x[r, p + 8:p + 11] = v.reshape(V, 3, 4).transpose(1, 0, 2)
            j = rng.permutation(V)[:8]
            x[r, p + 1, j[:4], 0] = 2.0 ** 30
            x[r, p + 1, j[4:], 0] = -2.0 ** 30
    m = int(rng.integers(N))
    later = [int(p) for p in at[1:]]
    d["u"][m, :, :4] = 0
    for p in range(0, 128, 16):
        if p in later: continue
        d["u"][m, p, 0] = 1
        d["u"][m, p + 8:p + 16, 0] = 1
        v = rng.integers(8, 16, (16, V, 4)) * rng.choice([-1.0, 1.0], (16, V, 4))
        v[:8] *= 2.0 ** -3
        v[8:] *= 2.0 ** -27
        v[0, :, 0] = 1
        x[m, p:p + 16] = v.astype(np.float32).astype(BF)
    return {**d, "x": x.reshape(N, 128, 4 * V), "fv": stored(e)}
def setup_inputs_deep(rng):
    d = numbers_of(rng)
    e = lists_of(rng)
    line = 1.0 - 2.0 * rng.integers(0, 2, (128, 4))
    sign = np.tile((rng.permutation(N) % 2 * 2.0 - 1.0)[:, None], (1, V))
    m = int(rng.permutation(np.flatnonzero(sign[:, 0] > 0))[0])
    j, k = rng.permutation(V), rng.permutation(F)
    sign[m, j[K // 4:]] = -1
    e[m][:, k[:K // 2]] = rng.permuted(np.tile(j[:K // 4], (8, 2)), axis=1)
    e[m][:, k[K // 2:]] = rng.permuted(np.tile(j[K // 4:], (8, 2)), axis=1)
    d["u"][:, :, :4 * T] = (np.tile(line, (1, T)) * 2.0 ** 30).astype(np.float32).astype(BF)
    x = np.where(rng.random((N, 128, V, 4)) < 0.0625, 0.875, 1.0) * 2.0 ** 30
    x = x * line[:, None, :] * sign[:, None, :, None]
    return {**d, "x": x.astype(np.float32).astype(BF).reshape(N, 128, 4 * V), "fv": stored(e), **weights(rng, 2.0 ** -5)}
def setup_inputs_crowd(rng):
    d, x, at = planted(rng)
    e = np.zeros((N, 8, F), int)
    for r in range(N):
        odd = bin(r).count("1") % 2
        turn = int(rng.integers(T))
        to = rng.permuted(np.tile(np.arange(V), (8, 1)), axis=1)
        e[r] = to[:, np.arange(F) % V if odd else np.arange(F) // 2]
        for t in range(T):
            v = np.ones(V, np.float32)
            if odd:
                j = 2 * rng.permutation(V // 2)[:K // 2] + rng.integers(0, 2, K // 2)
                if t == turn: j = 8 * rng.permutation(V // 8)[:K // 2] + int(rng.integers(8))
                v[j] = 64 * (1 + 0.25 * rng.integers(0, 4, K // 2))
            else:
                j = rng.permutation(V // 2)[:K // 4]
                up = rng.permutation(K // 4) % 2
                v[j + V // 2 * up] = 1024 * (1 + 0.25 * rng.integers(0, 4, K // 4))
                v[j + V // 2 * (1 - up)] = 64 * (1 + 0.25 * rng.integers(0, 4, K // 4))
            p = int(at[t])
            x[r, p, to[p // 16], 0] = v.astype(BF)
    return {**d, "x": x.reshape(N, 128, 4 * V), "fv": stored(e)}
def setup_inputs_spread(rng):
    d = setup_inputs(rng)
    d["x"] = big(wide(rng, N, 128, 4 * V, cols=6), 1)
    return d
def check_inputs(d):
    b = []
    for k in ("x", "u", "wy"):
        v = np.abs(d[k].astype(np.float32))
        if not (np.isfinite(v).all() and ((v == 0) | (v >= 2.0 ** -30) & (v <= 2.0 ** 30)).all()): b.append("a value of " + k)
    e = [gentries(a) for a in d["fv"]]
    if any(((a < 0) | (a >= V)).any() for a in e): b.append("an entry of fv out of range")
    if any((np.sort(a, axis=1) != np.arange(F) // 2).any() for a in e): b.append("a variable that isn't exactly twice in a list of fv")
    good = True
    for r in range(N):
        try:
            w = decode(pk(d["wc"][r], d["ws"][r]))
            good = good and bool(np.isfinite(w).all() and (np.abs(w) <= 2.0 ** 31).all())
        except Exception:
            good = False
    if not good: b.append("a number that wc and ws hold")
    return b
def reference(x, fv, u, wy, wc, ws):
    now = [x[r] for r in range(N)]
    e = [gentries(fv[r]) for r in range(N)]
    qu = [mx_ref.quantize(np.ascontiguousarray(u[r])) for r in range(N)]
    qw = [pk(wc[r], ws[r]) for r in range(N)]
    fl = np.zeros((N, T, K), np.float32)
    for t in range(T):
        fired, sent = [], []
        for r in range(N):
            h = mx_ref.quantize(gcols(now[r], e[r]))
            s = mx_ref.matmul(qu[r], h)[t] + np.float32(0.0)
            o = np.argsort(-s, kind="stable")[:K]
            fired.append(o)
            sent.append(pick(h, o))
            fl[r, t] = o
        new = []
        for r in range(N):
            p = r ^ (1 << t)
            low = np.full((8, V), K)
            np.minimum.at(low, (np.arange(8)[:, None], e[r][:, fired[p]]), np.tile(np.arange(K), (8, 1)))
            v = []
            for b in range(4):
                z = mx_ref.matmul(pick(qw[r], np.arange(128 * b, 128 * b + 128)), sent[p]) * np.float32(0.03125)
                v.append(gpick(np.concatenate([z, np.zeros((128, 1), np.float32)], axis=1), low))
            v = np.stack(v, axis=2).reshape(128, -1)
            hit = np.repeat(np.repeat(low < K, 16, axis=0), 4, axis=1)
            a = now[r].astype(np.float32)
            new.append(np.where(hit, a * np.float32(0.5) + v * np.float32(0.5), a).astype(BF))
        now = new
    y = np.zeros((N, 128, V), np.float32)
    oc, osc = np.zeros((N, 128, 4 * V), np.uint8), np.zeros((N, 16, V), np.uint8)
    for r in range(N):
        q = mx_ref.quantize(np.ascontiguousarray(now[r]))
        y[r] = mx_ref.matmul(mx_ref.quantize(np.ascontiguousarray(wy[r])), q)
        oc[r], osc[r] = emit(q)
    return {"y": y, "oc": oc, "osc": osc, "fl": fl}

@@ -1,0 +1,428 @@
+from concourse.mybir import dt, AluOpType, ActivationFunctionType
+
+ROUNDS = 3
+VCH = (2, 3, 4, 5, 6)
+SCH = (0, 1, 7)
+
+F32, BF, F16, I32, U16, CODE, U8 = "float32", "bfloat16", "float16", "int32", "uint16", "float8_e4m3fn_x4", "uint8"
+SCRATCH = {
+    "XI": ("sbuf", [128, 2048], BF), "XF": ("sbuf", [128, 4096], BF), "H": ("sbuf", [128, 4096], BF),
+    "WQ": ("sbuf", [128, 512], CODE), "WSC": ("sbuf", [128, 512], U8),
+    "UB": ("sbuf", [128, 512], BF), "QU": ("sbuf", [128, 128], CODE), "SU": ("sbuf", [128, 128], U8),
+    "WYB": ("sbuf", [128, 512], BF), "QWY": ("sbuf", [128, 128], CODE), "SWY": ("sbuf", [128, 128], U8),
+    "QX": ("sbuf", [128, 512], CODE), "SX": ("sbuf", [128, 512], U8),
+    "FVT": ("sbuf", [128, 64], I32), "OFH": ("sbuf", [128, 256], U16), "OFP": ("sbuf", [128, 64], U16),
+    "FVP": ("sbuf", [128, 1024], I32), "POSL": ("sbuf", [128, 64], U16), "FVN": ("sbuf", [128, 1024], F32),
+    "CC": ("sbuf", [128, 8], F32), "NCC": ("sbuf", [128, 4], F32),
+    "EQR": ("sbuf", [128, 1024], BF), "SCB": ("sbuf", [128, 2880], F16), "JNK": ("sbuf", [128, 3480], BF),
+    "ASU": ("sbuf", [128, 4], F32), "APR": ("sbuf", [128, 4], F32),
+    "OFR": ("sbuf", [128, 8], U16), "WIN": ("sbuf", [128, 1040], F32), "TT": ("sbuf", [128, 288], F32),
+    "SA": ("sbuf", [128, 16], F32), "SB": ("sbuf", [64, 16], F32), "SC": ("sbuf", [128, 16], F32),
+    "PP": ("sbuf", [128, 18], F32), "MK": ("sbuf", [128, 18], F32),
+    "P32": ("sbuf", [128, 1], I32), "GI": ("sbuf", [128, 1], I32), "QI": ("sbuf", [128, 1], I32),
+    "HI": ("sbuf", [128, 1], I32), "HF": ("sbuf", [128, 1], F32), "NH": ("sbuf", [128, 1], F32),
+    "GF": ("sbuf", [128, 1], F32), "QF": ("sbuf", [128, 1], F32), "Q64": ("sbuf", [128, 1], F32),
+    "IV0": ("sbuf", [128, 128], F32), "IV": ("sbuf", [128, 128], F32),
+    "MD0": ("sbuf", [128, 128], F32), "MD": ("sbuf", [128, 128], F32),
+    "KM": ("sbuf", [128, 1024], F16), "IOT": ("sbuf", [128, 1024], F32),
+    "RV0": ("sbuf", [128, 8], F32), "QM": ("sbuf", [128, 8], F32), "REV": ("sbuf", [128, 8], U16),
+    "PL0": ("sbuf", [128, 128], F32),
+    "VRO": ("sbuf", [128, 128], F16), "VM": ("sbuf", [128, 128], F32), "ZR": ("sbuf", [128, 128], F32),
+    "VC": ("sbuf", [128, 144], F32), "VW": ("sbuf", [128, 8], F32), "EQ": ("sbuf", [128, 1024], F16),
+    "LOS": ("sbuf", [128, 1024], F16), "VD": ("sbuf", [128, 8], F32),
+    "OFG": ("sbuf", [128, 8], U16), "OFS": ("sbuf", [128, 8], U16), "OFX": ("sbuf", [128, 32], U16),
+    "FR": ("sbuf", [128, 128], F32),
+    "OLD": ("sbuf", [128, 512], F32), "TMP": ("sbuf", [128, 512], F32), "NV": ("sbuf", [128, 512], BF),
+    "YS": ("sbuf", [128, 512], F32),
+    "psR": ("psum", [128, 2048], F32), "psC": ("psum", [128, 2048], F32),
+}
+for _e in range(4):
+    SCRATCH["XP%d" % _e] = ("sbuf", [128, 1024], BF)
+for _c in VCH:
+    SCRATCH["CB%d" % _c] = ("sbuf", [128, 1152], BF)
+for _c in SCH:
+    SCRATCH["SG%d" % _c] = ("sbuf", [128, 1160], BF)
+for _t in range(ROUNDS):
+    SCRATCH["UO%d" % _t] = ("sbuf", [128, 8], U16)
+    SCRATCH["QUR%d" % _t] = ("sbuf", [128, 128], CODE)
+    SCRATCH["SUR%d" % _t] = ("sbuf", [128, 128], U8)
+    SCRATCH["QH%d" % _t] = ("sbuf", [128, 1024], CODE)
+    SCRATCH["SH%d" % _t] = ("sbuf", [128, 1024], U8)
+    SCRATCH["SL%d" % _t] = ("sbuf", [128, 128], CODE)
+    SCRATCH["SS%d" % _t] = ("sbuf", [128, 128], U8)
+    SCRATCH["LC%d" % _t] = ("sbuf", [128, 128], CODE)
+    SCRATCH["LS%d" % _t] = ("sbuf", [128, 128], U8)
+    SCRATCH["LR%d" % _t] = ("sbuf", [128, 8], U16)
+    SCRATCH["LST%d" % _t] = ("sbuf", [128, 8], U16)
+    SCRATCH["FLS%d" % _t] = ("sbuf", [128, 128], F32)
+
+SEMAPHORES = ["cv", "cs", "ct", "cg", "dx", "dfv", "du", "dfp", "dw", "dwy", "dout", "sent"]
+for _t in range(ROUNDS):
+    SEMAPHORES += ["arrL%d" % _t, "arrC%d" % _t, "arrS%d" % _t]
+
+
+def rank_program(g, core, T, topo):
+    rank = T.rank_of(core)
+    if rank is None:
+        return
+    A, ACT = AluOpType, ActivationFunctionType
+    V, S, TE, SY = g.vector, g.scalar, g.tensor, g.sync
+    queue = {"v": V, "s": S, "t": TE, "g": g, "y": SY}
+    own = {"v": "cv", "s": "cs", "t": "ct", "g": "cg"}
+
+    count = {k: 0 for k in own}
+    known = {k: {} for k in queue}
+    most, total = {}, {}
+    wr, rd = {}, {}
+
+    def need(e, tok):
+        sem, n = tok
+        if known[e].get(sem, 0) < n:
+            queue[e].wait_ge(T.sem[sem], n)
+            known[e][sem] = n
+            most[sem] = max(most.get(sem, 0), n)
+
+    def deps(e, reads, writes):
+        want = {}
+        for n, a, b in reads:
+            for (x, y, tok, w) in wr.get(n, []):
+                if x < b and a < y:
+                    want[tok[0]] = max(want.get(tok[0], 0), tok[1])
+        for n, a, b in writes:
+            for (x, y, tok, w) in wr.get(n, []):
+                if x < b and a < y:
+                    want[tok[0]] = max(want.get(tok[0], 0), tok[1])
+            for (x, y, tok, w) in rd.get(n, []):
+                if x < b and a < y and w != e:
+                    want[tok[0]] = max(want.get(tok[0], 0), tok[1])
+        for sem in sorted(want):
+            need(e, (sem, want[sem]))
+
+    def note(e, tok, reads, writes):
+        for n, a, b in writes:
+            wr[n] = [r for r in wr.get(n, []) if not (a <= r[0] and r[1] <= b)] + [(a, b, tok, e)]
+            rd[n] = [r for r in rd.get(n, []) if not (a <= r[0] and r[1] <= b)]
+        for n, a, b in reads:
+            rd[n] = [r for r in rd.get(n, []) if not (r[3] == e and a <= r[0] and r[1] <= b)] + [(a, b, tok, e)]
+
+    def op(e, call, reads, writes):
+        deps(e, reads, writes)
+        count[e] += 1
+        total[own[e]] = count[e]
+        call().then_inc(T.sem[own[e]], 1)
+        note(e, (own[e], count[e]), reads, writes)
+
+    def dma(e, out, in_, sem, n, reads, writes):
+        deps(e, reads, writes)
+        total[sem] = total.get(sem, 0) + 16
+        queue[e].dma_start(out, in_).then_inc(T.sem[sem], 16)
+        note("d" + sem, (sem, 16 * n), reads, writes)
+
+    def ts(out, in0, s1, s2, *ops):
+        return lambda: V.tensor_scalar(out, in0, s1, s2, *ops)
+
+    def tt(out, a, b, o):
+        return lambda: V.tensor_tensor(out, a, b, o)
+
+    def scan(out, a, b, o0, o1):
+        return lambda: V.tensor_tensor_scan(out, a, b, 0.0, o0, o1)
+
+    def cp(out, in_):
+        return lambda: V.tensor_copy(out, in_)
+
+    def ms(ap, c):
+        return lambda: V.memset(ap, c)
+
+    def act(out, in_, func, **kw):
+        return lambda: S.activation(out, in_, func, **kw)
+
+    def mm(out, a, sa, b, sb):
+        return lambda: TE.matmul_mx(out, a, sa, b, sb, True, True)
+
+    def iota(name, pattern, base, cm, a, b):
+        kw = {} if SCRATCH[name][2] == I32 else {"allow_small_or_imprecise_dtypes": True}
+        op("g", lambda: g.iota(T[name][:, a:b], pattern, base, cm, **kw), [], [(name, a, b)])
+
+    dma("y", T.XI[:], T.x[:], "dx", 1, [], [("XI", 0, 2048)])
+    dma("s", T.FVT[:], T.fv[:], "dfv", 1, [], [("FVT", 0, 64)])
+    dma("s", T.UB[:], T.u[:], "du", 1, [], [("UB", 0, 512)])
+    need("y", ("dx", 16))
+    dma("y", T.WQ[:, 0:512].bitcast(dt.uint8), T.wc[:], "dw", 2, [], [("WQ", 0, 512)])
+    dma("y", T.WSC[:, 0:512], T.ws[:], "dw", 2, [], [("WSC", 0, 512)])
+    for q in range(16):
+        dma("y", T.FVP[q:128:16, :], T.fv[:], "dfp", 16, [], [("FVP.%d" % q, 0, 1024)])
+    dma("y", T.WYB[:], T.wy[:], "dwy", 1, [], [("WYB", 0, 512)])
+
+    iota("P32", [[0, 1]], 0, 1, 0, 1)
+    iota("RV0", [[16, 8]], 0, 0, 0, 8)
+    iota("PL0", [[1, 128]], 0, 0, 0, 128)
+    iota("MD0", [[0, 8], [1, 16]], 0, 0, 0, 128)
+    col = 0
+    for first, n in ((VCH[0], len(VCH)), (SCH[0], 2), (SCH[2], 1)):
+        iota("IV0", [[128, n], [1, 16]], 128 * first, 0, col, col + 16 * n)
+        col += 16 * n
+    iota("IOT", [[1, 1024]], 0, 0, 0, 1024)
+    op("v", ms(T.WIN[:, 880:1040], 0.0), [], [("WIN", 880, 1040)])
+    op("v", ms(T.MK[:], 0.0), [], [("MK", 0, 18)])
+    op("v", ms(T.ZR[:], 0.0), [], [("ZR", 0, 128)])
+    op("v", ms(T.VC[:, 0:16], 0.0), [], [("VC", 0, 16)])
+    op("v", ts(T.GI[:], T.P32[:], 4, None, A.arith_shift_right), [("P32", 0, 1)], [("GI", 0, 1)])
+    op("v", ts(T.QI[:], T.P32[:], 15, None, A.bitwise_and), [("P32", 0, 1)], [("QI", 0, 1)])
+    op("v", ts(T.HI[:], T.GI[:], 1, None, A.bitwise_and), [("GI", 0, 1)], [("HI", 0, 1)])
+    op("v", cp(T.QF[:], T.QI[:]), [("QI", 0, 1)], [("QF", 0, 1)])
+    op("v", ts(T.GF[:], T.GI[:], 16.0, None, A.mult), [("GI", 0, 1)], [("GF", 0, 1)])
+    op("v", cp(T.HF[:], T.HI[:]), [("HI", 0, 1)], [("HF", 0, 1)])
+    op("v", ts(T.Q64[:], T.QI[:], 64.0, None, A.mult), [("QI", 0, 1)], [("Q64", 0, 1)])
+    op("v", ts(T.NH[:], T.HI[:], -1.0, 1.0, A.mult, A.add), [("HI", 0, 1)], [("NH", 0, 1)])
+    op("v", ts(T.QM[:], T.RV0[:], T.QF[:, 0:1], None, A.add), [("RV0", 0, 8), ("QF", 0, 1)], [("QM", 0, 8)])
+    for c in SCH:
+        op("v", ms(T["SG%d" % c][:, 6:7], float(128 * c - 896)), [], [("SG%d" % c, 6, 7)])
+        op("v", ts(T["SG%d" % c][:, 7:8], T.P32[:], -127.0, None, A.add), [("P32", 0, 1)], [("SG%d" % c, 7, 8)])
+    for a, s in ((0, "NH"), (4, "HF"), (9, "HF"), (14, "NH")):
+        op("v", ts(T.MK[:, a:a + 4], T.PL0[:, 0:4], 0.0, T[s][:, 0:1], A.mult, A.add), [("PL0", 0, 128), (s, 0, 1)], [("MK", a, a + 4)])
+    for e in range(4):
+        op("v", ts(T.OFH[:, 64 * e:64 * e + 64], T.FVT[:], 4.0, float(e), A.mult, A.add), [("FVT", 0, 64)], [("OFH", 64 * e, 64 * e + 64)])
+    op("v", lambda: V.quantize_mx(T.QU[:, 0:128], T.SU[:, 0:128], T.UB[:, 0:512]), [("UB", 0, 512)], [("QU", 0, 128), ("SU", 0, 128)])
+
+    def lay_u(t):
+        op("v", ms(T["UO%d" % t][:], t), [], [("UO%d" % t, 0, 8)])
+        off = T["UO%d" % t]
+        op("v", cp(T["QUR%d" % t][:, 0:128].bitcast(dt.uint32), T.QU[:, 0:128].bitcast(dt.uint32).indirect(off[:, 0:8])),
+           [("QU", 0, 128), ("UO%d" % t, 0, 8)], [("QUR%d" % t, 0, 128)])
+        op("v", cp(T["SUR%d" % t][:, 0:128], T.SU[:, 0:128].indirect(off[:, 0:8])),
+           [("SU", 0, 128), ("UO%d" % t, 0, 8)], [("SUR%d" % t, 0, 128)])
+
+    lay_u(0)
+    op("v", cp(T.OFP[:], T.FVT[:]), [("FVT", 0, 64)], [("OFP", 0, 64)])
+    op("v", ts(T.POSL[:], T.PL0[:, 0:64], T.Q64[:, 0:1], None, A.add), [("PL0", 0, 128), ("Q64", 0, 1)], [("POSL", 0, 64)])
+    op("v", ts(T.MD[:], T.MD0[:], T.QF[:, 0:1], None, A.is_equal), [("MD0", 0, 128), ("QF", 0, 1)], [("MD", 0, 128)])
+    op("v", ts(T.IV[:], T.IV0[:], T.GF[:, 0:1], None, A.add), [("IV0", 0, 128), ("GF", 0, 1)], [("IV", 0, 128)])
+    op("v", ts(T.REV[:], T.QM[:], -1.0, 127.0, A.mult, A.add), [("QM", 0, 8)], [("REV", 0, 8)])
+    for m in range(8):
+        op("v", ts(T.KM[:, 128 * m:128 * m + 128], T.PL0[:], T.QM[:, m:m + 1], None, A.is_gt), [("PL0", 0, 128), ("QM", 0, 8)], [("KM", 128 * m, 128 * m + 128)])
+
+    partners = [T.cores[rank ^ (1 << t)] for t in range(ROUNDS)]
+    common = [e for e in topo.engines(core, partners[0]) if all(e in topo.engines(core, p) for p in partners)]
+    mask, ne = sum(1 << e for e in common), len(common)
+    nout = ROUNDS + 7
+
+    def send(t, land, src, arr, reads):
+        deps("g", reads, [])
+        rid, pid = topo.addr(partners[t])[:2]
+        total["sent"] = total.get("sent", 0) + ne
+        g.remote_dma(land, src, T.sem[arr], T.sem.sent, pid, rid, mask)
+        total[arr] = ne
+
+    for t in range(ROUNDS):
+        QH, SH, QUR, SUR = T["QH%d" % t], T["SH%d" % t], T["QUR%d" % t], T["SUR%d" % t]
+        nQH, nSH = "QH%d" % t, "SH%d" % t
+        ru = [("QUR%d" % t, 0, 128), ("SUR%d" % t, 0, 128)]
+
+        def gather(e, el, lo, hi):
+            out = T.H[:, 4 * lo + el:4 * hi:4]
+            if t == 0:
+                win = T.XI[:, 0:2048].indirect(T.OFH[:, 64 * el + lo // 16:64 * el + hi // 16])
+                reads = [("XI", 0, 2048), ("OFH", 64 * el, 64 * el + 64)]
+            else:
+                win = T["XP%d" % el][:, 0:512].indirect(T.OFP[:, lo // 16:hi // 16])
+                reads = [("XP%d" % el, 0, 512), ("OFP", 0, 64)]
+            op(e, cp(out, win) if e == "v" else act(out, win, ACT.Copy), reads, [("H.%d" % el, lo, hi)])
+
+        def quant(a, b):
+            op("v", lambda: V.quantize_mx(QH[:, a:b], SH[:, a:b], T.H[:, 4 * a:4 * b]),
+               [("H.%d" % e, a, b) for e in range(4)], [(nQH, a, b), (nSH, a, b)])
+
+        def rows(h, base):
+            a = 512 * h
+            op("t", mm(T.psR[:, base + a:base + a + 512], QUR[:, 0:128], SUR[:, 0:128], QH[:, a:a + 512], SH[:, a:a + 512]),
+               ru + [(nQH, a, a + 512), (nSH, a, a + 512)], [("psR", base + a, base + a + 512)])
+
+        def cols(c):
+            k = c % 4
+            op("t", mm(T.psC[:, 512 * k:512 * k + 128], QH[:, 128 * c:128 * c + 128], SH[:, 128 * c:128 * c + 128], QUR[:, 0:128], SUR[:, 0:128]),
+               ru + [(nQH, 128 * c, 128 * c + 128), (nSH, 128 * c, 128 * c + 128)], [("psC", 512 * k, 512 * k + 512)])
+
+        if t == 0:
+            first = [("v", 0), ("s", 2), ("v", 1), ("s", 3)]
+            second = [("s", 2, 512, 1024), ("s", 3, 512, 1024), ("v", 0, 512, 1024), ("s", 1, 768, 1024), ("v", 1, 512, 768)]
+        else:
+            first = [("s", 0), ("s", 1), ("v", 2), ("v", 3)]
+            second = [("s", 0, 512, 1024), ("s", 1, 512, 1024), ("s", 2, 512, 1024), ("v", 3, 512, 768), ("s", 3, 768, 1024)]
+        for e, el in first:
+            gather(e, el, 0, 512)
+        quant(0, 512)
+        for e, el, lo, hi in second:
+            gather(e, el, lo, hi)
+        for c in range(4):
+            cols(c)
+        quant(512, 768)
+        quant(768, 1024)
+        rows(0, 0)
+        rows(0, 1024)
+        op("v", cp(T.CC[:, 0:4], T.psC[:, 0:2048:512]), [("psC", 0, 2048)], [("CC", 0, 4)])
+        op("v", ts(T.NCC[:, 0:2], T.CC[:, 0:2], -1.0, None, A.mult), [("CC", 0, 2)], [("NCC", 0, 2)])
+        rows(1, 0)
+        for c in range(4, 8):
+            cols(c)
+        rows(1, 1024)
+
+        def sign(i, h):
+            c = SCH[i]
+            op("s", act(T["SG%d" % c][:, 8 + 512 * h:520 + 512 * h], T.psR[:, 1024 + 512 * h:1536 + 512 * h], ACT.Sign, bias=T.NCC[:, i:i + 1]),
+               [("psR", 1024 + 512 * h, 1536 + 512 * h), ("NCC", i, i + 1)], [("SG%d" % c, 8 + 512 * h, 520 + 512 * h)])
+
+        def triangles(i):
+            c = SCH[i]
+            sg, nm, d = T["SG%d" % c], "SG%d" % c, 8 + 128 * c
+            op("g", lambda: g.affine_select(sg[:, 1032:1160], sg[:, d:d + 128], [[1, 128]], A.is_gt, 0.0, 0, -1),
+               [(nm, d, d + 128)], [(nm, 1032, 1160)])
+            op("g", lambda: g.affine_select(sg[:, d:d + 128], sg[:, d:d + 128], [[-1, 128]], A.is_gt, 0.0, 0, 1),
+               [(nm, d, d + 128)], [(nm, d, d + 128)])
+
+        def eq(c):
+            cb = T["CB%d" % c]
+            op("v", ts(T.EQR[:, 128 * c:128 * c + 128], T.psR[:, 128 * c:128 * c + 128], T.CC[:, c:c + 1], None, A.is_equal),
+               [("psR", 128 * c, 128 * c + 128), ("CC", c, c + 1)], [("EQR", 128 * c, 128 * c + 128)])
+            op("g", lambda: g.affine_select(cb[:, 1024:1152], T.EQR[:, 128 * c:128 * c + 128], [[1, 128]], A.is_gt, 0.0, 0, -1),
+               [("EQR", 128 * c, 128 * c + 128)], [("CB%d" % c, 1024, 1152)])
+
+        def beat(c, a, b, o):
+            op("v", ts(T["CB%d" % c][:, a:b], T.psR[:, a:b], T.CC[:, c:c + 1], None, o),
+               [("psR", a, b), ("CC", c, c + 1)], [("CB%d" % c, a, b)])
+
+        def total_of(i):
+            cb = T["CB%d" % VCH[i]]
+            op("v", scan(T.SCB[:, 576 * i:576 * i + 576], cb[:, 0:576], cb[:, 576:1152], A.add, A.add),
+               [("CB%d" % VCH[i], 0, 1152)], [("SCB", 576 * i, 576 * i + 576)])
+
+        for i in (0, 1):
+            sign(i, 0)
+            triangles(i)
+        for c in (2, 3):
+            eq(c)
+        beat(2, 0, 384, A.is_lt)
+        beat(2, 384, 512, A.is_le)
+        beat(3, 0, 512, A.is_lt)
+        op("v", ms(T.WIN[:, 896:1024], 0.0), [], [("WIN", 896, 1024)])
+        op("v", cp(T.CC[:, 4:8], T.psC[:, 0:2048:512]), [("psC", 0, 2048)], [("CC", 4, 8)])
+        op("v", ts(T.NCC[:, 2:3], T.CC[:, 7:8], -1.0, None, A.mult), [("CC", 7, 8)], [("NCC", 2, 3)])
+        for i, h in ((2, 0), (2, 1), (0, 1), (1, 1)):
+            sign(i, h)
+        triangles(2)
+        for i, c in enumerate(SCH):
+            sg, nm, d, j = T["SG%d" % c], "SG%d" % c, 136 + 128 * c, 1160 * i
+            op("s", act(T.JNK[:, j + 6:j + d], sg[:, 6:d], ACT.Relu, scale=-1.0, accum_out=T.APR[:, i:i + 1]),
+               [(nm, 6, d)], [("APR", i, i + 1), ("JNK", j + 6, j + d)])
+            op("s", act(T.JNK[:, j + d:j + 1160], sg[:, d:1160], ACT.Relu, accum_out=T.ASU[:, i:i + 1]),
+               [(nm, d, 1160)], [("ASU", i, i + 1), ("JNK", j + d, j + 1160)])
+        if t == 0:
+            op("s", act(T.FVN[:], T.FVP[:].indirect(T.POSL[:, 0:64]), ACT.Copy),
+               [("FVP.%d" % q, 0, 1024) for q in range(16)] + [("POSL", 0, 64)], [("FVN", 0, 1024)])
+        beat(2, 512, 1024, A.is_le)
+        eq(4)
+        beat(3, 512, 1024, A.is_le)
+        total_of(0)
+        for i in (2, 3, 4):
+            c = VCH[i]
+            if i > 2:
+                eq(c)
+            beat(c, 0, 128 * c + 128, A.is_lt)
+            beat(c, 128 * c + 128, 1024, A.is_le)
+            total_of(i - 1)
+        total_of(4)
+        op("v", cp(T.OFR[:, 0:5], T.SCB[:, 575:2880:576]), [("SCB", 0, 2880)], [("OFR", 0, 5)])
+        op("v", tt(T.OFR[:, 5:8], T.APR[:, 0:3], T.ASU[:, 0:3], A.subtract), [("ASU", 0, 3), ("APR", 0, 3)], [("OFR", 5, 8)])
+        op("v", cp(T.WIN[:, 0:1024].indirect(T.OFR[:, 0:8]), T.IV[:]), [("OFR", 0, 8), ("IV", 0, 128)], [("WIN", 0, 1024)])
+        op("v", lambda: V.transpose(T.TT[:, 0:128], T.WIN[:, 896:1024]), [("WIN", 896, 1024)], [("TT.0", 0, 128)])
+        op("v", lambda: V.transpose(T.TT[:, 128:288], T.WIN[:, 880:1040]), [("WIN", 880, 1040)], [("TT.1", 0, 160)])
+        op("v", tt(T.SA[:, 0:9], T.TT[:, 0:288:32], T.TT[:, 16:288:32], A.add), [("TT.0", 0, 128), ("TT.1", 0, 160)], [("SA", 0, 9)])
+        op("v", tt(T.SB[0:64, 0:9], T.SA[0:64, 0:9], T.SA[64:128, 0:9], A.add), [("SA", 0, 9)], [("SB", 0, 9)])
+        op("v", tt(T.SC[0:32, 0:9], T.SB[0:32, 0:9], T.SB[32:64, 0:9], A.add), [("SB", 0, 9)], [("SC", 0, 9)])
+        op("v", cp(T.SC[32:64, 0:9], T.SC[0:32, 0:9]), [("SC", 0, 9)], [("SC", 0, 9)])
+        op("v", cp(T.SC[64:128, 0:9], T.SC[0:64, 0:9]), [("SC", 0, 9)], [("SC", 0, 9)])
+        LST, nL = T["LST%d" % t], "LST%d" % t
+        op("v", tt(T.PP[:, 0:9], T.SC[:, 0:9], T.MK[:, 0:9], A.mult), [("SC", 0, 9), ("MK", 0, 18)], [("PP", 0, 9)])
+        op("v", tt(T.PP[:, 9:18], T.SC[:, 0:9], T.MK[:, 9:18], A.mult), [("SC", 0, 9), ("MK", 0, 18)], [("PP", 9, 18)])
+        op("v", tt(LST[:, 0:8:2], T.PP[:, 0:4], T.PP[:, 4:8], A.add), [("PP", 0, 9)], [(nL + ".0", 0, 8)])
+        op("v", tt(LST[:, 1:8:2], T.PP[:, 9:13], T.PP[:, 14:18], A.add), [("PP", 9, 18)], [(nL + ".1", 0, 8)])
+        rL = [(nL + ".0", 0, 8), (nL + ".1", 0, 8)]
+
+        send(t, T["LR%d" % t][:], LST[:], "arrL%d" % t, rL)
+        op("v", cp(T["SL%d" % t][:, 0:128].bitcast(dt.uint32), QH[:, 0:1024].bitcast(dt.uint32).indirect(LST[:, 0:8])),
+           [(nQH, 0, 1024)] + rL, [("SL%d" % t, 0, 128)])
+        op("s", act(T["SS%d" % t][:, 0:128], SH[:, 0:1024].indirect(LST[:, 0:8]), ACT.Copy),
+           [(nSH, 0, 1024)] + rL, [("SS%d" % t, 0, 128)])
+        send(t, T["LC%d" % t][:, 0:128].bitcast(dt.uint8), T["SL%d" % t][:, 0:128].bitcast(dt.uint8), "arrC%d" % t, [("SL%d" % t, 0, 128)])
+        send(t, T["LS%d" % t][:, 0:128], T["SS%d" % t][:, 0:128], "arrS%d" % t, [("SS%d" % t, 0, 128)])
+        note("a", ("arrL%d" % t, ne), [], [("LR%d" % t, 0, 8)])
+        note("a", ("arrC%d" % t, ne), [], [("LC%d" % t, 0, 128)])
+        note("a", ("arrS%d" % t, ne), [], [("LS%d" % t, 0, 128)])
+        FLS, nF = T["FLS%d" % t], "FLS%d" % t
+        op("s", act(T.FR[:], T.IOT[:].indirect(LST[:, 0:8]), ACT.Copy), [("IOT", 0, 1024)] + rL, [("FR", 0, 128)])
+        op("s", act(FLS[:], T.FR[:].indirect(T.REV[:, 0:8]), ACT.Copy), [("FR", 0, 128), ("REV", 0, 8)], [(nF, 0, 128)])
+        dma("y", T.fl[t:t + 1, :], FLS[0:1, :], "dout", nout, [(nF, 0, 128)], [])
+        if t == 0:
+            for e in range(4):
+                op("v", cp(T["XP%d" % e][:, 0:512], T.XI[:, e:2048:4]), [("XI", 0, 2048)], [("XP%d" % e, 0, 512)])
+            lay_u(1)
+        if t == 1:
+            lay_u(2)
+            op("v", lambda: V.quantize_mx(T.QWY[:, 0:128], T.SWY[:, 0:128], T.WYB[:, 0:512]), [("WYB", 0, 512)], [("QWY", 0, 128), ("SWY", 0, 128)])
+        if t == 2:
+            for e in range(4):
+                op("v", cp(T.XF[:, e:2048:4], T["XP%d" % e][:, 0:512]), [("XP%d" % e, 0, 512)], [("XF.%d" % e, 0, 4096)])
+
+        LR, nR = T["LR%d" % t], "LR%d" % t
+        op("v", tt(T.VM[:], T.FVN[:].indirect(LR[:, 0:8]), T.MD[:], A.mult), [("FVN", 0, 1024), (nR, 0, 8), ("MD", 0, 128)], [("VM", 0, 128)])
+        op("s", act(T.VRO[:], T.FVN[:].indirect(LR[:, 0:8]), ACT.Copy), [("FVN", 0, 1024), (nR, 0, 8)], [("VRO", 0, 128)])
+        op("v", scan(T.VC[:, 16:144], T.VM[:], T.ZR[:], A.add, A.add), [("VM", 0, 128), ("ZR", 0, 128)], [("VC", 16, 144)])
+        op("v", tt(T.OFG[:], T.VC[:, 31:144:16], T.VC[:, 15:128:16], A.subtract), [("VC", 0, 144)], [("OFG", 0, 8)])
+        op("v", tt(T.VW[:], T.VC[:, 31:144:16], T.VC[:, 15:128:16], A.subtract), [("VC", 0, 144)], [("VW", 0, 8)])
+        for e in range(4):
+            op("s", act(T.OLD[:, 128 * e:128 * e + 128], T["XP%d" % e][:, 0:512].indirect(T.OFG[:, 0:8]), ACT.Copy, scale=32.0),
+               [("XP%d" % e, 0, 512), ("OFG", 0, 8)], [("OLD", 128 * e, 128 * e + 128)])
+        for m in range(8):
+            a = 128 * m
+            op("v", ts(T.EQ[:, a:a + 128], T.VRO[:], T.VW[:, m:m + 1], 512.0, A.is_equal, A.mult),
+               [("VRO", 0, 128), ("VW", 0, 8)], [("EQ", a, a + 128)])
+        op("v", scan(T.LOS[:], T.EQ[:], T.KM[:], A.add, A.mult), [("EQ", 0, 1024), ("KM", 0, 1024)], [("LOS", 0, 1024)])
+        if t < 2:
+            op("v", tt(T.OFS[:], T.LOS[:, 127:1024:128], T.VW[:], A.add), [("LOS", 0, 1024), ("VW", 0, 8)], [("OFS", 0, 8)])
+        else:
+            op("v", tt(T.VD[:], T.LOS[:, 127:1024:128], T.VW[:], A.add), [("LOS", 0, 1024), ("VW", 0, 8)], [("VD", 0, 8)])
+            for e in range(4):
+                op("v", ts(T.OFX[:, 8 * e:8 * e + 8], T.VD[:], 4.0, float(e), A.mult, A.add), [("VD", 0, 8)], [("OFX", 8 * e, 8 * e + 8)])
+
+        for b in range(4):
+            op("t", mm(T.psC[:, 512 * b:512 * b + 128], T.WQ[:, 128 * b:128 * b + 128], T.WSC[:, 128 * b:128 * b + 128],
+                       T["LC%d" % t][:, 0:128], T["LS%d" % t][:, 0:128]),
+               [("WQ", 0, 512), ("WSC", 0, 512), ("LC%d" % t, 0, 128), ("LS%d" % t, 0, 128)], [("psC", 512 * b, 512 * b + 512)])
+        for b in range(4):
+            a = 128 * b
+            op("v", tt(T.TMP[:, a:a + 128], T.psC[:, 512 * b:512 * b + 128], T.OLD[:, a:a + 128], A.add),
+               [("psC", 512 * b, 512 * b + 128), ("OLD", a, a + 128)], [("TMP", a, a + 128)])
+            op("s", act(T.NV[:, a:a + 128], T.TMP[:, a:a + 128], ACT.Copy, scale=1.0 / 64), [("TMP", a, a + 128)], [("NV", a, a + 128)])
+        for b in range(4):
+            if t < 2:
+                op("v", cp(T["XP%d" % b][:, 0:1024].indirect(T.OFS[:, 0:8]), T.NV[:, 128 * b:128 * b + 128]),
+                   [("OFS", 0, 8), ("NV", 128 * b, 128 * b + 128)], [("XP%d" % b, 0, 1024)])
+            else:
+                op("v", cp(T.XF[:, 0:4096].indirect(T.OFX[:, 8 * b:8 * b + 8]), T.NV[:, 128 * b:128 * b + 128]),
+                   [("OFX", 0, 32), ("NV", 128 * b, 128 * b + 128)], [("XF.%d" % e, 0, 4096) for e in range(4)])
+
+    for h in range(2):
+        a = 256 * h
+        op("v", lambda: V.quantize_mx(T.QX[:, a:a + 256], T.SX[:, a:a + 256], T.XF[:, 4 * a:4 * a + 1024]),
+           [("XF.%d" % e, 0, 4096) for e in range(4)], [("QX", a, a + 256), ("SX", a, a + 256)])
+        op("t", mm(T.psR[:, 1024 * h:1024 * h + 256], T.QWY[:, 0:128], T.SWY[:, 0:128], T.QX[:, a:a + 256], T.SX[:, a:a + 256]),
+           [("QWY", 0, 128), ("SWY", 0, 128), ("QX", a, a + 256), ("SX", a, a + 256)], [("psR", 1024 * h, 1024 * h + 512)])
+    op("s", act(T.YS[:, 0:256], T.psR[:, 0:256], ACT.Copy), [("psR", 0, 256)], [("YS", 0, 256)])
+    op("v", cp(T.YS[:, 256:512], T.psR[:, 1024:1280]), [("psR", 1024, 1280)], [("YS", 256, 512)])
+    dma("y", T.oc[:, 0:2048], T.QX[:, 0:512].bitcast(dt.uint8), "dout", nout, [("QX", 0, 512)], [])
+    dma("s", T.y[:, 0:256], T.YS[:, 0:256], "dout", nout, [("YS", 0, 256)], [])
+    dma("y", T.y[:, 256:512], T.YS[:, 256:512], "dout", nout, [("YS", 256, 512)], [])
+    for k in range(4):
+        dma("y" if k % 2 else "s", T.osc[4 * k:4 * k + 4, :], T.SX[32 * k:32 * k + 4, 0:512], "dout", nout, [("SX", 0, 512)], [])
+    for sem in sorted(total):
+        if most.get(sem, 0) < total[sem]:
+            need("g", (sem, total[sem]))

@@ -1,8 +1,6 @@
 from concourse.mybir import dt, AluOpType, ActivationFunctionType
 
 ROUNDS = 3
-VCH = (2, 3, 4, 5, 6)
-SCH = (0, 1, 7)
 
 F32, BF, F16, I32, U16, CODE, U8 = "float32", "bfloat16", "float16", "int32", "uint16", "float8_e4m3fn_x4", "uint8"
 SCRATCH = {
@@ -14,8 +12,7 @@ SCRATCH = {
     "FVT": ("sbuf", [128, 64], I32), "OFH": ("sbuf", [128, 256], U16), "OFP": ("sbuf", [128, 64], U16),
     "FVP": ("sbuf", [128, 1024], I32), "POSL": ("sbuf", [128, 64], U16), "FVN": ("sbuf", [128, 1024], F32),
     "CC": ("sbuf", [128, 8], F32), "NCC": ("sbuf", [128, 4], F32),
-    "EQR": ("sbuf", [128, 1024], BF), "SCB": ("sbuf", [128, 2880], F16), "JNK": ("sbuf", [128, 3480], BF),
-    "ASU": ("sbuf", [128, 4], F32), "APR": ("sbuf", [128, 4], F32),
+    "SCA": ("sbuf", [128, 4608], F16), "SCB": ("sbuf", [128, 3584], F16), "XA": ("sbuf", [128, 4], F32),
     "OFR": ("sbuf", [128, 8], U16), "WIN": ("sbuf", [128, 1040], F32), "TT": ("sbuf", [128, 288], F32),
     "SA": ("sbuf", [128, 16], F32), "SB": ("sbuf", [64, 16], F32), "SC": ("sbuf", [128, 16], F32),
     "PP": ("sbuf", [128, 18], F32), "MK": ("sbuf", [128, 18], F32),
@@ -38,10 +35,10 @@ SCRATCH = {
 }
 for _e in range(4):
     SCRATCH["XP%d" % _e] = ("sbuf", [128, 1024], BF)
-for _c in VCH:
+for _c in range(8):
     SCRATCH["CB%d" % _c] = ("sbuf", [128, 1152], BF)
-for _c in SCH:
-    SCRATCH["SG%d" % _c] = ("sbuf", [128, 1160], BF)
+    if _c != 3:
+        SCRATCH["CU%d" % _c] = ("sbuf", [128, 1024], U16)
 for _t in range(ROUNDS):
     SCRATCH["UO%d" % _t] = ("sbuf", [128, 8], U16)
     SCRATCH["QUR%d" % _t] = ("sbuf", [128, 128], CODE)
@@ -157,10 +154,7 @@ def rank_program(g, core, T, topo):
     iota("RV0", [[16, 8]], 0, 0, 0, 8)
     iota("PL0", [[1, 128]], 0, 0, 0, 128)
     iota("MD0", [[0, 8], [1, 16]], 0, 0, 0, 128)
-    col = 0
-    for first, n in ((VCH[0], len(VCH)), (SCH[0], 2), (SCH[2], 1)):
-        iota("IV0", [[128, n], [1, 16]], 128 * first, 0, col, col + 16 * n)
-        col += 16 * n
+    iota("IV0", [[128, 8], [1, 16]], 0, 0, 0, 128)
     iota("IOT", [[1, 1024]], 0, 0, 0, 1024)
     op("v", ms(T.WIN[:, 880:1040], 0.0), [], [("WIN", 880, 1040)])
     op("v", ms(T.MK[:], 0.0), [], [("MK", 0, 18)])
@@ -175,9 +169,6 @@ def rank_program(g, core, T, topo):
     op("v", ts(T.Q64[:], T.QI[:], 64.0, None, A.mult), [("QI", 0, 1)], [("Q64", 0, 1)])
     op("v", ts(T.NH[:], T.HI[:], -1.0, 1.0, A.mult, A.add), [("HI", 0, 1)], [("NH", 0, 1)])
     op("v", ts(T.QM[:], T.RV0[:], T.QF[:, 0:1], None, A.add), [("RV0", 0, 8), ("QF", 0, 1)], [("QM", 0, 8)])
-    for c in SCH:
-        op("v", ms(T["SG%d" % c][:, 6:7], float(128 * c - 896)), [], [("SG%d" % c, 6, 7)])
-        op("v", ts(T["SG%d" % c][:, 7:8], T.P32[:], -127.0, None, A.add), [("P32", 0, 1)], [("SG%d" % c, 7, 8)])
     for a, s in ((0, "NH"), (4, "HF"), (9, "HF"), (14, "NH")):
         op("v", ts(T.MK[:, a:a + 4], T.PL0[:, 0:4], 0.0, T[s][:, 0:1], A.mult, A.add), [("PL0", 0, 128), (s, 0, 1)], [("MK", a, a + 4)])
     for e in range(4):
@@ -217,6 +208,8 @@ def rank_program(g, core, T, topo):
         QH, SH, QUR, SUR = T["QH%d" % t], T["SH%d" % t], T["QUR%d" % t], T["SUR%d" % t]
         nQH, nSH = "QH%d" % t, "SH%d" % t
         ru = [("QUR%d" % t, 0, 128), ("SUR%d" % t, 0, 128)]
+        if t > 0:
+            iota("WIN", [[0, 128]], 0, 0, 896, 1024)
 
         def gather(e, el, lo, hi):
             out = T.H[:, 4 * lo + el:4 * hi:4]
@@ -259,90 +252,94 @@ def rank_program(g, core, T, topo):
         quant(768, 1024)
         rows(0, 0)
         rows(0, 1024)
-        op("v", cp(T.CC[:, 0:4], T.psC[:, 0:2048:512]), [("psC", 0, 2048)], [("CC", 0, 4)])
-        op("v", ts(T.NCC[:, 0:2], T.CC[:, 0:2], -1.0, None, A.mult), [("CC", 0, 2)], [("NCC", 0, 2)])
-        rows(1, 0)
+        op("s", act(T.CC[:, 0:4], T.psC[:, 0:2048:512], ACT.Copy), [("psC", 0, 2048)], [("CC", 0, 4)])
+        op("s", act(T.NCC[:, 0:4], T.psC[:, 0:2048:512], ACT.Copy, scale=-1.0), [("psC", 0, 2048)], [("NCC", 0, 4)])
         for c in range(4, 8):
             cols(c)
+        rows(1, 0)
         rows(1, 1024)
 
-        def sign(i, h):
-            c = SCH[i]
-            op("s", act(T["SG%d" % c][:, 8 + 512 * h:520 + 512 * h], T.psR[:, 1024 + 512 * h:1536 + 512 * h], ACT.Sign, bias=T.NCC[:, i:i + 1]),
-               [("psR", 1024 + 512 * h, 1536 + 512 * h), ("NCC", i, i + 1)], [("SG%d" % c, 8 + 512 * h, 520 + 512 * h)])
-
-        def triangles(i):
-            c = SCH[i]
-            sg, nm, d = T["SG%d" % c], "SG%d" % c, 8 + 128 * c
-            op("g", lambda: g.affine_select(sg[:, 1032:1160], sg[:, d:d + 128], [[1, 128]], A.is_gt, 0.0, 0, -1),
-               [(nm, d, d + 128)], [(nm, 1032, 1160)])
-            op("g", lambda: g.affine_select(sg[:, d:d + 128], sg[:, d:d + 128], [[-1, 128]], A.is_gt, 0.0, 0, 1),
-               [(nm, d, d + 128)], [(nm, d, d + 128)])
+        def sign(c, a, b):
+            kw = {"bias": T.NCC[:, c:c + 1]} if c < 4 else {"bias": T.CC[:, c:c + 1], "scale": -1.0}
+            op("s", act(T["CU%d" % c][:, a:b], T.psR[:, 1024 + a:1024 + b], ACT.Sign, **kw),
+               [("psR", 1024 + a, 1024 + b), ("NCC" if c < 4 else "CC", c, c + 1)], [("CU%d" % c, a, b)])
 
         def eq(c):
-            cb = T["CB%d" % c]
-            op("v", ts(T.EQR[:, 128 * c:128 * c + 128], T.psR[:, 128 * c:128 * c + 128], T.CC[:, c:c + 1], None, A.is_equal),
-               [("psR", 128 * c, 128 * c + 128), ("CC", c, c + 1)], [("EQR", 128 * c, 128 * c + 128)])
-            op("g", lambda: g.affine_select(cb[:, 1024:1152], T.EQR[:, 128 * c:128 * c + 128], [[1, 128]], A.is_gt, 0.0, 0, -1),
-               [("EQR", 128 * c, 128 * c + 128)], [("CB%d" % c, 1024, 1152)])
+            cb, nm = T["CB%d" % c], "CB%d" % c
+            s = 1 if c < 4 else -1
+            d = 128 * c + 128 if c < 3 else 1024
+            op("v", ts(cb[:, d:d + 128], T.psR[:, 128 * c:128 * c + 128], T.CC[:, c:c + 1], None, A.is_equal),
+               [("psR", 128 * c, 128 * c + 128), ("CC", c, c + 1)], [(nm, d, d + 128)])
+            op("g", lambda: g.affine_select(cb[:, d:d + 128], cb[:, d:d + 128], [[-s, 128]], A.is_gt, 0.0, 0, s),
+               [(nm, d, d + 128)], [(nm, d, d + 128)])
 
         def beat(c, a, b, o):
             op("v", ts(T["CB%d" % c][:, a:b], T.psR[:, a:b], T.CC[:, c:c + 1], None, o),
                [("psR", a, b), ("CC", c, c + 1)], [("CB%d" % c, a, b)])
 
-        def total_of(i):
-            cb = T["CB%d" % VCH[i]]
-            op("v", scan(T.SCB[:, 576 * i:576 * i + 576], cb[:, 0:576], cb[:, 576:1152], A.add, A.add),
-               [("CB%d" % VCH[i], 0, 1152)], [("SCB", 576 * i, 576 * i + 576)])
+        def add_up(src, a, b, dst, end):
+            n = (b - a) // 2
+            op("v", scan(T[dst][:, end - n:end], T[src][:, a:a + n], T[src][:, a + n:b], A.add, A.add),
+               [(src, a, b)], [(dst, end - n, end)])
 
-        for i in (0, 1):
-            sign(i, 0)
-            triangles(i)
-        for c in (2, 3):
+        def short(c):
+            a, b = (0, 128 * c + 256) if c < 3 else (0 if c == 3 else 128 * c, 1152)
+            add_up("CB%d" % c, a, b, "SCA", 576 * c + 576)
+
+        def long(c):
+            a, b = (128 * c + 128, 1024) if c < 4 else (0, 128 * c)
+            add_up("CU%d" % c, a, b, "SCB", 448 * c + 448)
+
+        for c in range(3):
+            sign(c, 128 * c + 128, 512)
+        for c in range(4):
             eq(c)
-        beat(2, 0, 384, A.is_lt)
-        beat(2, 384, 512, A.is_le)
-        beat(3, 0, 512, A.is_lt)
-        op("v", ms(T.WIN[:, 896:1024], 0.0), [], [("WIN", 896, 1024)])
-        op("v", cp(T.CC[:, 4:8], T.psC[:, 0:2048:512]), [("psC", 0, 2048)], [("CC", 4, 8)])
-        op("v", ts(T.NCC[:, 2:3], T.CC[:, 7:8], -1.0, None, A.mult), [("CC", 7, 8)], [("NCC", 2, 3)])
-        for i, h in ((2, 0), (2, 1), (0, 1), (1, 1)):
-            sign(i, h)
-        triangles(2)
-        for i, c in enumerate(SCH):
-            sg, nm, d, j = T["SG%d" % c], "SG%d" % c, 136 + 128 * c, 1160 * i
-            op("s", act(T.JNK[:, j + 6:j + d], sg[:, 6:d], ACT.Relu, scale=-1.0, accum_out=T.APR[:, i:i + 1]),
-               [(nm, 6, d)], [("APR", i, i + 1), ("JNK", j + 6, j + d)])
-            op("s", act(T.JNK[:, j + d:j + 1160], sg[:, d:1160], ACT.Relu, accum_out=T.ASU[:, i:i + 1]),
-               [(nm, d, 1160)], [("ASU", i, i + 1), ("JNK", j + d, j + 1160)])
+        for c in range(4):
+            beat(c, 128 * c, 128 * c + 128, A.is_gt)
+            if c:
+                beat(c, 0, 128 * c, A.is_ge)
+        for c in range(3):
+            short(c)
+        op("s", act(T.CC[:, 4:8], T.psC[:, 0:2048:512], ACT.Copy), [("psC", 0, 2048)], [("CC", 4, 8)])
+        for c in (4, 7, 6, 5):
+            sign(c, 0, 512)
+        for c in (5, 6, 7):
+            sign(c, 512, 128 * c)
+        for c in range(3):
+            sign(c, 512, 1024)
         if t == 0:
             op("s", act(T.FVN[:], T.FVP[:].indirect(T.POSL[:, 0:64]), ACT.Copy),
                [("FVP.%d" % q, 0, 1024) for q in range(16)] + [("POSL", 0, 64)], [("FVN", 0, 1024)])
-        beat(2, 512, 1024, A.is_le)
-        eq(4)
-        beat(3, 512, 1024, A.is_le)
-        total_of(0)
-        for i in (2, 3, 4):
-            c = VCH[i]
-            if i > 2:
-                eq(c)
-            beat(c, 0, 128 * c + 128, A.is_lt)
-            beat(c, 128 * c + 128, 1024, A.is_le)
-            total_of(i - 1)
-        total_of(4)
-        op("v", cp(T.OFR[:, 0:5], T.SCB[:, 575:2880:576]), [("SCB", 0, 2880)], [("OFR", 0, 5)])
-        op("v", tt(T.OFR[:, 5:8], T.APR[:, 0:3], T.ASU[:, 0:3], A.subtract), [("ASU", 0, 3), ("APR", 0, 3)], [("OFR", 5, 8)])
+        for c in range(4, 8):
+            eq(c)
+        beat(3, 512, 1024, A.is_gt)
+        for c in range(4, 8):
+            beat(c, 128 * c, 128 * c + 128, A.is_lt)
+            if c < 7:
+                beat(c, 128 * c + 128, 1024, A.is_le)
+        for c in range(3, 8):
+            short(c)
+        long(4)
+        op("v", ts(T.XA[:, 0:3], T.SCA[:, 575:1728:576], -1.0, 1023.0, A.mult, A.add), [("SCA", 0, 1728)], [("XA", 0, 3)])
+        op("v", ts(T.OFR[:, 3:4], T.SCA[:, 2303:2304], -1.0, 1023.0, A.mult, A.add), [("SCA", 1728, 2304)], [("OFR", 3, 4)])
+        for c in (5, 6, 7, 0):
+            long(c)
+        op("v", tt(T.OFR[:, 4:8], T.SCA[:, 2879:4608:576], T.SCB[:, 2239:3584:448], A.add),
+           [("SCA", 2304, 4608), ("SCB", 1792, 3584)], [("OFR", 4, 8)])
+        for c in (1, 2):
+            long(c)
+        op("v", tt(T.OFR[:, 0:3], T.XA[:, 0:3], T.SCB[:, 447:1344:448], A.subtract), [("XA", 0, 3), ("SCB", 0, 1344)], [("OFR", 0, 3)])
         op("v", cp(T.WIN[:, 0:1024].indirect(T.OFR[:, 0:8]), T.IV[:]), [("OFR", 0, 8), ("IV", 0, 128)], [("WIN", 0, 1024)])
         op("v", lambda: V.transpose(T.TT[:, 0:128], T.WIN[:, 896:1024]), [("WIN", 896, 1024)], [("TT.0", 0, 128)])
         op("v", lambda: V.transpose(T.TT[:, 128:288], T.WIN[:, 880:1040]), [("WIN", 880, 1040)], [("TT.1", 0, 160)])
         op("v", tt(T.SA[:, 0:9], T.TT[:, 0:288:32], T.TT[:, 16:288:32], A.add), [("TT.0", 0, 128), ("TT.1", 0, 160)], [("SA", 0, 9)])
         op("v", tt(T.SB[0:64, 0:9], T.SA[0:64, 0:9], T.SA[64:128, 0:9], A.add), [("SA", 0, 9)], [("SB", 0, 9)])
-        op("v", tt(T.SC[0:32, 0:9], T.SB[0:32, 0:9], T.SB[32:64, 0:9], A.add), [("SB", 0, 9)], [("SC", 0, 9)])
-        op("v", cp(T.SC[32:64, 0:9], T.SC[0:32, 0:9]), [("SC", 0, 9)], [("SC", 0, 9)])
-        op("v", cp(T.SC[64:128, 0:9], T.SC[0:64, 0:9]), [("SC", 0, 9)], [("SC", 0, 9)])
+        for k in range(4):
+            op("v", tt(T.SC[32 * k:32 * k + 32, 0:9], T.SB[0:32, 0:9], T.SB[32:64, 0:9], A.add), [("SB", 0, 9)], [("SC.%d" % k, 0, 9)])
+        rC = [("SC.%d" % k, 0, 9) for k in range(4)]
         LST, nL = T["LST%d" % t], "LST%d" % t
-        op("v", tt(T.PP[:, 0:9], T.SC[:, 0:9], T.MK[:, 0:9], A.mult), [("SC", 0, 9), ("MK", 0, 18)], [("PP", 0, 9)])
-        op("v", tt(T.PP[:, 9:18], T.SC[:, 0:9], T.MK[:, 9:18], A.mult), [("SC", 0, 9), ("MK", 0, 18)], [("PP", 9, 18)])
+        op("v", tt(T.PP[:, 0:9], T.SC[:, 0:9], T.MK[:, 0:9], A.mult), rC + [("MK", 0, 18)], [("PP", 0, 9)])
+        op("v", tt(T.PP[:, 9:18], T.SC[:, 0:9], T.MK[:, 9:18], A.mult), rC + [("MK", 0, 18)], [("PP", 9, 18)])
         op("v", tt(LST[:, 0:8:2], T.PP[:, 0:4], T.PP[:, 4:8], A.add), [("PP", 0, 9)], [(nL + ".0", 0, 8)])
         op("v", tt(LST[:, 1:8:2], T.PP[:, 9:13], T.PP[:, 14:18], A.add), [("PP", 9, 18)], [(nL + ".1", 0, 8)])
         rL = [(nL + ".0", 0, 8), (nL + ".1", 0, 8)]

@@ -1,6 +1,7 @@
 from concourse.mybir import dt, AluOpType, ActivationFunctionType
 
 ROUNDS = 3
+UW, WW = 1666, 770
 
 F32, BF, F16, I32, U16, CODE, U8 = "float32", "bfloat16", "float16", "int32", "uint16", "float8_e4m3fn_x4", "uint8"
 SCRATCH = {
@@ -12,21 +13,19 @@ SCRATCH = {
     "FVT": ("sbuf", [128, 64], I32), "OFH": ("sbuf", [128, 256], U16), "OFP": ("sbuf", [128, 64], U16),
     "FVP": ("sbuf", [128, 1024], I32), "POSL": ("sbuf", [128, 64], U16), "FVN": ("sbuf", [128, 1024], F32),
     "CC": ("sbuf", [128, 8], F32), "NCC": ("sbuf", [128, 4], F32),
-    "SCA": ("sbuf", [128, 4608], F16), "SCB": ("sbuf", [128, 3584], F16), "XA": ("sbuf", [128, 4], F32),
-    "OFR": ("sbuf", [128, 8], U16), "WIN": ("sbuf", [128, 1040], F32), "TT": ("sbuf", [128, 288], F32),
-    "SA": ("sbuf", [128, 16], F32), "SB": ("sbuf", [64, 16], F32), "SC": ("sbuf", [128, 16], F32),
-    "PP": ("sbuf", [128, 18], F32), "MK": ("sbuf", [128, 18], F32),
-    "P32": ("sbuf", [128, 1], I32), "GI": ("sbuf", [128, 1], I32), "QI": ("sbuf", [128, 1], I32),
-    "HI": ("sbuf", [128, 1], I32), "HF": ("sbuf", [128, 1], F32), "NH": ("sbuf", [128, 1], F32),
-    "GF": ("sbuf", [128, 1], F32), "QF": ("sbuf", [128, 1], F32), "Q64": ("sbuf", [128, 1], F32),
+    "UA": ("sbuf", [128, 8 * UW], U16), "WA": ("sbuf", [128, 8 * WW], F16),
+    "SCL": ("sbuf", [128, 1028], U16), "OU": ("sbuf", [128, 330], U16),
+    "WIN": ("sbuf", [128, 1040], F32), "TT": ("sbuf", [128, 288], F32),
+    "GL": ("sbuf", [128, 2], U16), "G0": ("sbuf", [128, 16], F32), "G1": ("sbuf", [64, 16], F32), "G2": ("sbuf", [64, 8], F32),
+    "P32": ("sbuf", [128, 1], I32), "PI": ("sbuf", [128, 8], I32), "PF": ("sbuf", [128, 16], F32),
     "IV0": ("sbuf", [128, 128], F32), "IV": ("sbuf", [128, 128], F32),
     "MD0": ("sbuf", [128, 128], F32), "MD": ("sbuf", [128, 128], F32),
-    "KM": ("sbuf", [128, 1024], F16), "IOT": ("sbuf", [128, 1024], F32),
+    "KM": ("sbuf", [128, 768], F16), "IOT": ("sbuf", [128, 1024], F32),
     "RV0": ("sbuf", [128, 8], F32), "QM": ("sbuf", [128, 8], F32), "REV": ("sbuf", [128, 8], U16),
-    "PL0": ("sbuf", [128, 128], F32),
-    "VRO": ("sbuf", [128, 128], F16), "VM": ("sbuf", [128, 128], F32), "ZR": ("sbuf", [128, 128], F32),
-    "VC": ("sbuf", [128, 144], F32), "VW": ("sbuf", [128, 8], F32), "EQ": ("sbuf", [128, 1024], F16),
-    "LOS": ("sbuf", [128, 1024], F16), "VD": ("sbuf", [128, 8], F32),
+    "PL0": ("sbuf", [128, 128], BF),
+    "VRO": ("sbuf", [128, 128], F16), "VM": ("sbuf", [128, 128], F32),
+    "VC": ("sbuf", [128, 72], F32), "VW": ("sbuf", [128, 8], F32), "EQ": ("sbuf", [128, 768], F16),
+    "LOS": ("sbuf", [128, 768], F16), "VD": ("sbuf", [128, 8], F32),
     "OFG": ("sbuf", [128, 8], U16), "OFS": ("sbuf", [128, 8], U16), "OFX": ("sbuf", [128, 32], U16),
     "FR": ("sbuf", [128, 128], F32),
     "OLD": ("sbuf", [128, 512], F32), "TMP": ("sbuf", [128, 512], F32), "NV": ("sbuf", [128, 512], BF),
@@ -35,10 +34,6 @@ SCRATCH = {
 }
 for _e in range(4):
     SCRATCH["XP%d" % _e] = ("sbuf", [128, 1024], BF)
-for _c in range(8):
-    SCRATCH["CB%d" % _c] = ("sbuf", [128, 1152], BF)
-    if _c != 3:
-        SCRATCH["CU%d" % _c] = ("sbuf", [128, 1024], U16)
 for _t in range(ROUNDS):
     SCRATCH["UO%d" % _t] = ("sbuf", [128, 8], U16)
     SCRATCH["QUR%d" % _t] = ("sbuf", [128, 128], CODE)
@@ -56,6 +51,21 @@ for _t in range(ROUNDS):
 SEMAPHORES = ["cv", "cs", "ct", "cg", "dx", "dfv", "du", "dfp", "dw", "dwy", "dout", "sent"]
 for _t in range(ROUNDS):
     SEMAPHORES += ["arrL%d" % _t, "arrC%d" % _t, "arrS%d" % _t]
+
+LOSERS = "d0 d1 d2 d3 d4 d5 d6 d7 o0 o1 "
+FIRST = {"v": "g0.0.512 g1.0.512 u i0 q0.512 g1.512.1024 g0.512.768 q768.1024 q512.768 e0 s1.128.512 l2 e2 l1 e1 v0 e3 e7 e4 l4 l5 e6 v2 a6 "
+              "e5 l3 s3.512.1024 v3 v1 a4 l6 a2 a1 a7 a5 s0.896.1024 a3 v7 a0 b1 v5 b3 v4 v6 b0 b7 b2 b6 low b5 b4 z0.8",
+         "s": "g0.768.1024 g3.0.512 g2.0.512 g3.512.1024 g2.512.1024 k0 m0 s2.256.512 s3.384.512 s0.0.512 k1 s6.0.512 s4.0.512 s7.0.512 "
+              "s0.512.896 s5.0.512 s7.512.1024 s1.512.1024 s2.512.1024 s6.512.896 s5.512.768 s4.512.640",
+         "t": "c0 c1 r0.0 c2 c3 r0.1 c4 c5 c6 c7 r1.0 r1.1"}
+LATER = {"v": LOSERS + "t0 p0 p1 t1 t2 t3 x0 x1 x2 x3 g2.0.512 g3.0.256 q256.512 q0.256 g3.512.768 g2.512.1024 q512.768 q768.1024 "
+              "l2 e1 e0 l1 e2 s1.128.512 l4 e3 l3 v1 e5 e7 l5 v2 e4 v0 e6 a1 a7 v3 a6 v7 a3 a4 s0.896.1024 a0 a2 b1 v4 l6 a5 s3.512.1024 "
+              "v6 b2 b7 v5 b0 b3 b6 b5 low b4 z0.8",
+         "s": "h0 h1 h2 h3 n0.128 n128.256 n256.512 g0.0.512 g1.0.512 g3.256.512 g0.512.1024 g1.512.1024 g3.768.1024 k0 m0 s2.256.512 "
+              "s3.384.512 s0.0.512 k1 s7.0.512 s5.0.512 s6.0.512 s0.512.896 s4.0.512 s1.512.1024 s7.512.1024 s2.512.1024 s5.512.768 "
+              "s6.512.896 s4.512.640",
+         "t": "w0 w1 w2 w3 c2 c3 c0 c1 r0.1 r0.0 c4 c5 c6 c7 r1.0 r1.1"}
+LAST = {"v": LOSERS + "p0 p1 t0 t1 f0 f1 t2 t3 f2 f3 y0 y1", "s": "h0 h1 h2 h3 n0.128 n128.256 n256.384 n384.512", "t": "w0 w1 w2 w3"}
 
 
 def rank_program(g, core, T, topo):
@@ -133,6 +143,9 @@ def rank_program(g, core, T, topo):
     def act(out, in_, func, **kw):
         return lambda: S.activation(out, in_, func, **kw)
 
+    def move(e, out, in_):
+        return cp(out, in_) if e == "v" else act(out, in_, ACT.Copy)
+
     def mm(out, a, sa, b, sb):
         return lambda: TE.matmul_mx(out, a, sa, b, sb, True, True)
 
@@ -142,60 +155,75 @@ def rank_program(g, core, T, topo):
 
     dma("y", T.XI[:], T.x[:], "dx", 1, [], [("XI", 0, 2048)])
     dma("s", T.FVT[:], T.fv[:], "dfv", 1, [], [("FVT", 0, 64)])
-    dma("s", T.UB[:], T.u[:], "du", 1, [], [("UB", 0, 512)])
+    dma("y", T.UB[:], T.u[:], "du", 1, [], [("UB", 0, 512)])
     need("y", ("dx", 16))
-    dma("y", T.WQ[:, 0:512].bitcast(dt.uint8), T.wc[:], "dw", 2, [], [("WQ", 0, 512)])
-    dma("y", T.WSC[:, 0:512], T.ws[:], "dw", 2, [], [("WSC", 0, 512)])
     for q in range(16):
         dma("y", T.FVP[q:128:16, :], T.fv[:], "dfp", 16, [], [("FVP.%d" % q, 0, 1024)])
+    dma("y", T.WQ[:, 0:512].bitcast(dt.uint8), T.wc[:], "dw", 2, [], [("WQ", 0, 512)])
+    dma("y", T.WSC[:, 0:512], T.ws[:], "dw", 2, [], [("WSC", 0, 512)])
     dma("y", T.WYB[:], T.wy[:], "dwy", 1, [], [("WYB", 0, 512)])
 
     iota("P32", [[0, 1]], 0, 1, 0, 1)
-    iota("RV0", [[16, 8]], 0, 0, 0, 8)
     iota("PL0", [[1, 128]], 0, 0, 0, 128)
+    iota("RV0", [[16, 8]], 0, 0, 0, 8)
+    iota("IV0", [[128, 4], [1, 16]], 512, 0, 0, 64)
+    iota("IV0", [[128, 4], [1, 16]], 0, 0, 64, 128)
     iota("MD0", [[0, 8], [1, 16]], 0, 0, 0, 128)
-    iota("IV0", [[128, 8], [1, 16]], 0, 0, 0, 128)
+    iota("WIN", [[0, 160]], 0, 0, 880, 1040)
     iota("IOT", [[1, 1024]], 0, 0, 0, 1024)
-    op("v", ms(T.WIN[:, 880:1040], 0.0), [], [("WIN", 880, 1040)])
-    op("v", ms(T.MK[:], 0.0), [], [("MK", 0, 18)])
-    op("v", ms(T.ZR[:], 0.0), [], [("ZR", 0, 128)])
-    op("v", ms(T.VC[:, 0:16], 0.0), [], [("VC", 0, 16)])
-    op("v", ts(T.GI[:], T.P32[:], 4, None, A.arith_shift_right), [("P32", 0, 1)], [("GI", 0, 1)])
-    op("v", ts(T.QI[:], T.P32[:], 15, None, A.bitwise_and), [("P32", 0, 1)], [("QI", 0, 1)])
-    op("v", ts(T.HI[:], T.GI[:], 1, None, A.bitwise_and), [("GI", 0, 1)], [("HI", 0, 1)])
-    op("v", cp(T.QF[:], T.QI[:]), [("QI", 0, 1)], [("QF", 0, 1)])
-    op("v", ts(T.GF[:], T.GI[:], 16.0, None, A.mult), [("GI", 0, 1)], [("GF", 0, 1)])
-    op("v", cp(T.HF[:], T.HI[:]), [("HI", 0, 1)], [("HF", 0, 1)])
-    op("v", ts(T.Q64[:], T.QI[:], 64.0, None, A.mult), [("QI", 0, 1)], [("Q64", 0, 1)])
-    op("v", ts(T.NH[:], T.HI[:], -1.0, 1.0, A.mult, A.add), [("HI", 0, 1)], [("NH", 0, 1)])
-    op("v", ts(T.QM[:], T.RV0[:], T.QF[:, 0:1], None, A.add), [("RV0", 0, 8), ("QF", 0, 1)], [("QM", 0, 8)])
-    for a, s in ((0, "NH"), (4, "HF"), (9, "HF"), (14, "NH")):
-        op("v", ts(T.MK[:, a:a + 4], T.PL0[:, 0:4], 0.0, T[s][:, 0:1], A.mult, A.add), [("PL0", 0, 128), (s, 0, 1)], [("MK", a, a + 4)])
-    for e in range(4):
-        op("v", ts(T.OFH[:, 64 * e:64 * e + 64], T.FVT[:], 4.0, float(e), A.mult, A.add), [("FVT", 0, 64)], [("OFH", 64 * e, 64 * e + 64)])
-    op("v", lambda: V.quantize_mx(T.QU[:, 0:128], T.SU[:, 0:128], T.UB[:, 0:512]), [("UB", 0, 512)], [("QU", 0, 128), ("SU", 0, 128)])
-
-    def lay_u(t):
+    op("v", ms(T.VC[:, 0:8], 0.0), [], [("VC", 0, 8)])
+    for t in range(ROUNDS):
         op("v", ms(T["UO%d" % t][:], t), [], [("UO%d" % t, 0, 8)])
-        off = T["UO%d" % t]
-        op("v", cp(T["QUR%d" % t][:, 0:128].bitcast(dt.uint32), T.QU[:, 0:128].bitcast(dt.uint32).indirect(off[:, 0:8])),
-           [("QU", 0, 128), ("UO%d" % t, 0, 8)], [("QUR%d" % t, 0, 128)])
-        op("v", cp(T["SUR%d" % t][:, 0:128], T.SU[:, 0:128].indirect(off[:, 0:8])),
-           [("SU", 0, 128), ("UO%d" % t, 0, 8)], [("SUR%d" % t, 0, 128)])
 
-    lay_u(0)
-    op("v", cp(T.OFP[:], T.FVT[:]), [("FVT", 0, 64)], [("OFP", 0, 64)])
-    op("v", ts(T.POSL[:], T.PL0[:, 0:64], T.Q64[:, 0:1], None, A.add), [("PL0", 0, 128), ("Q64", 0, 1)], [("POSL", 0, 64)])
-    op("v", ts(T.MD[:], T.MD0[:], T.QF[:, 0:1], None, A.is_equal), [("MD0", 0, 128), ("QF", 0, 1)], [("MD", 0, 128)])
-    op("v", ts(T.IV[:], T.IV0[:], T.GF[:, 0:1], None, A.add), [("IV0", 0, 128), ("GF", 0, 1)], [("IV", 0, 128)])
+    def bits(k, *a):
+        op("v", ts(T.PI[:, k:k + 1], T.P32[:], *a), [("P32", 0, 1)], [("PI", k, k + 1)])
+
+    def col(k, j, *a):
+        reads = [("PI", j, j + 1)] + [("PF", 0, 16) for s in a[:2] if not isinstance(s, (float, int)) and s is not None]
+        op("v", ts(T.PF[:, k:k + 1], T.PI[:, j:j + 1], *a), reads, [("PF", k, k + 1)])
+
+    bits(0, 15, None, A.bitwise_and)
+    bits(1, 112, None, A.bitwise_and)
+    bits(2, 4, 1, A.arith_shift_right, A.bitwise_and)
+    bits(3, 1, None, A.bitwise_and)
+    bits(4, 6, None, A.bitwise_and)
+    bits(5, 8, None, A.bitwise_and)
+    col(0, 0, 1.0, None, A.mult)
+    col(1, 1, 1.0, None, A.mult)
+    col(2, 0, 64.0, None, A.mult)
+    col(3, 2, 1.0, None, A.mult)
+    col(4, 2, -32.0, 160.0, A.mult, A.add)
+    col(5, 4, 16.0, None, A.mult)
+    col(6, 3, T.PF[:, 3:4], T.PF[:, 4:5], A.not_equal, A.mult)
+    col(7, 5, 2.0, T.PF[:, 5:6], A.mult, A.add)
+    QF, GF, Q64 = T.PF[:, 0:1], T.PF[:, 1:2], T.PF[:, 2:3]
+    rP = [("PF", 0, 3)]
+    op("v", ts(T.QM[:], T.RV0[:], QF, None, A.add), [("RV0", 0, 8)] + rP, [("QM", 0, 8)])
+    op("v", ts(T.GL[:, 0:1], T.PF[:, 6:7], T.PF[:, 7:8], None, A.add), [("PF", 0, 16)], [("GL", 0, 1)])
+    op("v", ts(T.POSL[:], T.PL0[:, 0:64], Q64, None, A.add), [("PL0", 0, 128)] + rP, [("POSL", 0, 64)])
     op("v", ts(T.REV[:], T.QM[:], -1.0, 127.0, A.mult, A.add), [("QM", 0, 8)], [("REV", 0, 8)])
-    for m in range(8):
-        op("v", ts(T.KM[:, 128 * m:128 * m + 128], T.PL0[:], T.QM[:, m:m + 1], None, A.is_gt), [("PL0", 0, 128), ("QM", 0, 8)], [("KM", 128 * m, 128 * m + 128)])
+    for nm, c0, z, s in (("UA", 0, 832, -128), ("UA", 0, 1664, 0), ("UA", 4, 768, 128), ("WA", 4, 1280, -128)):
+        d = (UW if nm == "UA" else WW) + s
+        op("s", act(T[nm][:, z + d * c0:z + d * (c0 + 3) + 1:d], T.PL0[:, 0:4], ACT.Copy, scale=0.0), [("PL0", 0, 128)],
+           [(nm, z + d * c, z + d * c + 1) for c in range(c0, c0 + 4)])
+    op("v", ts(T.IV[:], T.IV0[:], GF, None, A.add), [("IV0", 0, 128)] + rP, [("IV", 0, 128)])
+    op("v", ts(T.MD[:], T.MD0[:], QF, None, A.is_equal), [("MD0", 0, 128)] + rP, [("MD", 0, 128)])
+    for e in (0, 3, 2, 1):
+        op("v", ts(T.OFH[:, 64 * e:64 * e + 64], T.FVT[:], 4.0, float(e), A.mult, A.add), [("FVT", 0, 64)], [("OFH", 64 * e, 64 * e + 64)])
+    segs = [(128 * m, 0) if m < 4 else (256 + 64 * m, 64) for m in range(8)]
+
+    def lay_codes(t):
+        op("v", cp(T["QUR%d" % t][:, 0:128].bitcast(dt.uint32), T.QU[:, 0:128].bitcast(dt.uint32).indirect(T["UO%d" % t][:, 0:8])),
+           [("QU", 0, 128), ("UO%d" % t, 0, 8)], [("QUR%d" % t, 0, 128)])
+
+    def lay_scales(t, e):
+        op(e, move(e, T["SUR%d" % t][:, 0:128], T.SU[:, 0:128].indirect(T["UO%d" % t][:, 0:8])),
+           [("SU", 0, 128), ("UO%d" % t, 0, 8)], [("SUR%d" % t, 0, 128)])
 
     partners = [T.cores[rank ^ (1 << t)] for t in range(ROUNDS)]
     common = [e for e in topo.engines(core, partners[0]) if all(e in topo.engines(core, p) for p in partners)]
     mask, ne = sum(1 << e for e in common), len(common)
-    nout = ROUNDS + 7
+    nout = ROUNDS + 12
 
     def send(t, land, src, arr, reads):
         deps("g", reads, [])
@@ -204,145 +232,202 @@ def rank_program(g, core, T, topo):
         g.remote_dma(land, src, T.sem[arr], T.sem.sent, pid, rid, mask)
         total[arr] = ne
 
-    for t in range(ROUNDS):
-        QH, SH, QUR, SUR = T["QH%d" % t], T["SH%d" % t], T["QUR%d" % t], T["SUR%d" % t]
-        nQH, nSH = "QH%d" % t, "SH%d" % t
-        ru = [("QUR%d" % t, 0, 128), ("SUR%d" % t, 0, 128)]
-        if t > 0:
-            iota("WIN", [[0, 128]], 0, 0, 896, 1024)
-
-        def gather(e, el, lo, hi):
-            out = T.H[:, 4 * lo + el:4 * hi:4]
+    def step(t, e, name):
+        kind, n = name[0], [int(x) for x in name[1:].split(".")] if name[1:2].isdigit() else []
+        if t < ROUNDS:
+            QH, SH, QUR, SUR = T["QH%d" % t], T["SH%d" % t], T["QUR%d" % t], T["SUR%d" % t]
+            nQH, nSH = "QH%d" % t, "SH%d" % t
+            ru = [("QUR%d" % t, 0, 128), ("SUR%d" % t, 0, 128)]
+        if name == "low":
+            op("v", ts(T.OU[:, 326:330], T.SCL[:, 256:1028:257], -1.0, 1023.0, A.mult, A.add), [("SCL", 0, 1028)], [("OU", 326, 330)])
+        elif name == "u":
+            op("v", lambda: V.quantize_mx(T.QU[:, 0:128], T.SU[:, 0:128], T.UB[:, 0:512]), [("UB", 0, 512)], [("QU", 0, 128), ("SU", 0, 128)])
+            lay_codes(0)
+        elif kind == "i":
+            lay_scales(0, e)
+        elif kind == "w":
+            b = n[0]
+            op("t", mm(T.psC[:, 512 * b:512 * b + 128], T.WQ[:, 128 * b:128 * b + 128], T.WSC[:, 128 * b:128 * b + 128],
+                       T["LC%d" % (t - 1)][:, 0:128], T["LS%d" % (t - 1)][:, 0:128]),
+               [("WQ", 0, 512), ("WSC", 0, 512), ("LC%d" % (t - 1), 0, 128), ("LS%d" % (t - 1), 0, 128)], [("psC", 512 * b, 512 * b + 512)])
+        elif kind == "t":
+            a = 128 * n[0]
+            op("v", tt(T.TMP[:, a:a + 128], T.psC[:, 4 * a:4 * a + 128], T.OLD[:, a:a + 128], A.add),
+               [("psC", 4 * a, 4 * a + 128), ("OLD", a, a + 128)], [("TMP", a, a + 128)])
+        elif kind == "n":
+            a, b = n
+            out, in_ = T.NV[:, a:b], T.TMP[:, a:b]
+            op(e, act(out, in_, ACT.Copy, scale=1.0 / 64) if e == "s" else ts(out, in_, 1.0 / 64, None, A.mult), [("TMP", a, b)], [("NV", a, b)])
+        elif kind == "h":
+            a = 128 * n[0]
+            out, in_ = T.OLD[:, a:a + 128], T["XP%d" % n[0]][:, 0:512].indirect(T.OFG[:, 0:8])
+            op(e, act(out, in_, ACT.Copy, scale=32.0) if e == "s" else ts(out, in_, 32.0, None, A.mult),
+               [("XP%d" % n[0], 0, 512), ("OFG", 0, 8)], [("OLD", a, a + 128)])
+        elif kind == "d":
+            a, j = segs[n[0]]
+            op("v", ts(T.EQ[:, a:a + 128 - j], T.VRO[:, j:128], T.VW[:, n[0]:n[0] + 1], 512.0, A.is_equal, A.mult),
+               [("VRO", 0, 128), ("VW", 0, 8)], [("EQ", a, a + 128 - j)])
+        elif kind == "o":
+            a, b = ((0, 512), (512, 768))[n[0]]
+            op("v", scan(T.LOS[:, a:b], T.EQ[:, a:b], T.KM[:, a:b], A.add, A.mult), [("EQ", a, b), ("KM", a, b)], [("LOS", a, b)])
+        elif kind == "p":
+            to, a = "OFS" if t < ROUNDS else "VD", 4 * n[0]
+            ends = (T.LOS[:, 127:512:128], T.LOS[:, 575:768:64])[n[0]]
+            op("v", tt(T[to][:, a:a + 4], ends, T.VW[:, a:a + 4], A.add), [("LOS", 512 * n[0], 512 * n[0] + 512), ("VW", 0, 8)], [(to, a, a + 4)])
+        elif kind == "f":
+            a = 8 * n[0]
+            op("v", ts(T.OFX[:, a:a + 8], T.VD[:], 4.0, float(n[0]), A.mult, A.add), [("VD", 0, 8)], [("OFX", a, a + 8)])
+        elif kind == "z":
+            a, b = n
+            op("v", cp(T.WIN[:, 0:1024].indirect(T.OU[:, 322 + a:322 + b]), T.IV[:, 16 * a:16 * b]),
+               [("OU", 322 + a, 322 + b), ("IV", 0, 128)], [("WIN", 0, 1024)])
+        elif kind == "x":
+            a = 128 * n[0]
+            op("v", cp(T["XP%d" % n[0]][:, 0:1024].indirect(T.OFS[:, 0:8]), T.NV[:, a:a + 128]),
+               [("OFS", 0, 8), ("NV", a, a + 128)], [("XP%d" % n[0], 0, 1024)])
+        elif kind == "y":
+            a = 256 * n[0]
+            op("v", cp(T.XF[:, 0:4096].indirect(T.OFX[:, 16 * n[0]:16 * n[0] + 16]), T.NV[:, a:a + 256]),
+               [("OFX", 16 * n[0], 16 * n[0] + 16), ("NV", a, a + 256)], [("XF.%d" % k, 0, 4096) for k in range(4)])
+        elif kind == "g":
+            el, lo, hi = n
             if t == 0:
                 win = T.XI[:, 0:2048].indirect(T.OFH[:, 64 * el + lo // 16:64 * el + hi // 16])
                 reads = [("XI", 0, 2048), ("OFH", 64 * el, 64 * el + 64)]
             else:
                 win = T["XP%d" % el][:, 0:512].indirect(T.OFP[:, lo // 16:hi // 16])
                 reads = [("XP%d" % el, 0, 512), ("OFP", 0, 64)]
-            op(e, cp(out, win) if e == "v" else act(out, win, ACT.Copy), reads, [("H.%d" % el, lo, hi)])
-
-        def quant(a, b):
+            op(e, move(e, T.H[:, 4 * lo + el:4 * hi:4], win), reads, [("H.%d" % el, lo, hi)])
+        elif kind == "q":
+            a, b = n
             op("v", lambda: V.quantize_mx(QH[:, a:b], SH[:, a:b], T.H[:, 4 * a:4 * b]),
-               [("H.%d" % e, a, b) for e in range(4)], [(nQH, a, b), (nSH, a, b)])
-
-        def rows(h, base):
-            a = 512 * h
+               [("H.%d" % k, a, b) for k in range(4)], [(nQH, a, b), (nSH, a, b)])
+        elif kind == "r":
+            a, base = 512 * n[0], 1024 * n[1]
             op("t", mm(T.psR[:, base + a:base + a + 512], QUR[:, 0:128], SUR[:, 0:128], QH[:, a:a + 512], SH[:, a:a + 512]),
                ru + [(nQH, a, a + 512), (nSH, a, a + 512)], [("psR", base + a, base + a + 512)])
+        elif kind == "c":
+            a, k = 128 * n[0], 512 * (n[0] % 4)
+            op("t", mm(T.psC[:, k:k + 128], QH[:, a:a + 128], SH[:, a:a + 128], QUR[:, 0:128], SUR[:, 0:128]),
+               ru + [(nQH, a, a + 128), (nSH, a, a + 128)], [("psC", k, k + 512)])
+        elif kind == "k":
+            a = 4 * n[0]
+            op(e, move(e, T.CC[:, a:a + 4], T.psC[:, 0:2048:512]), [("psC", 0, 2048)], [("CC", a, a + 4)])
+        elif kind == "m":
+            out, in_ = T.NCC[:, 0:4], T.CC[:, 0:4]
+            op(e, act(out, in_, ACT.Copy, scale=-1.0) if e == "s" else ts(out, in_, -1.0, None, A.mult), [("CC", 0, 4)], [("NCC", 0, 4)])
+        elif kind in "sl":
+            c = n[0]
+            if kind == "s":
+                a, b = n[1:]
+                nm, d = "UA", UW * c + (a + 640 if a >= 512 else a + (320 - 128 * c if c < 4 else 0))
+            else:
+                a, b, d = (0, 128 * c, WW * c + 128) if c < 4 else (128 * c + 128, 1024, WW * c + 384)
+                nm = "WA"
+            out, w = T[nm][:, d:d + b - a], [(nm, d, d + b - a)]
+            if e == "s":
+                kw = {"bias": T.NCC[:, c:c + 1]} if c < 4 else {"bias": T.CC[:, c:c + 1], "scale": -1.0}
+                op("s", act(out, T.psR[:, 1024 + a:1024 + b], ACT.Sign, **kw),
+                   [("psR", 1024 + a, 1024 + b), ("NCC" if c < 4 else "CC", c, c + 1)], w)
+            else:
+                o = {"s": (A.is_gt, A.is_lt), "l": (A.is_ge, A.is_le)}[kind][c // 4]
+                op("v", ts(out, T.psR[:, a:b], T.CC[:, c:c + 1], None, o), [("psR", a, b), ("CC", c, c + 1)], w)
+        elif kind == "e":
+            c = n[0]
+            s, d = (1, WW * c) if c < 4 else (-1, WW * c + 256)
+            cb = T.WA[:, d:d + 128]
+            op("v", ts(cb, T.psR[:, 128 * c:128 * c + 128], T.CC[:, c:c + 1], None, A.is_equal),
+               [("psR", 128 * c, 128 * c + 128), ("CC", c, c + 1)], [("WA", d, d + 128)])
+            op("g", lambda: g.affine_select(cb, cb, [[-s, 128]], A.is_gt, 0.0, 0, s), [("WA", d, d + 128)], [("WA", d, d + 128)])
+        elif kind in "vab":
+            c = n[0]
+            u, w = UW * c, WW * c
+            if c < 4:
+                src, a, h, dst, end = {"v": ("WA", w, 64 + 64 * c, "UA", u + 320), "a": ("UA", u + 319, 257 - 64 * c, "UA", u + 1152),
+                                       "b": ("UA", u + 1151, 257, "SCL", 257 * c + 257)}[kind]
+            else:
+                src, a, h, dst, end = {"a": ("UA", u, 256, "WA", w + 256), "v": ("WA", w + 255, 513 - 64 * c, "UA", u + 1152),
+                                       "b": ("UA", u + 1151, 64 * c - 191, "OU", 319 + c)}[kind]
+            op("v", scan(T[dst][:, end - h:end], T[src][:, a:a + h], T[src][:, a + h:a + 2 * h], A.add, A.add),
+               [(src, a, a + 2 * h)], [(dst, end - h, end)])
 
-        def cols(c):
-            k = c % 4
-            op("t", mm(T.psC[:, 512 * k:512 * k + 128], QH[:, 128 * c:128 * c + 128], SH[:, 128 * c:128 * c + 128], QUR[:, 0:128], SUR[:, 0:128]),
-               ru + [(nQH, 128 * c, 128 * c + 128), (nSH, 128 * c, 128 * c + 128)], [("psC", 512 * k, 512 * k + 512)])
+    def after(name, plan):
+        kind, n = name[0], [int(x) for x in name[1:].split(".")] if name[1:2].isdigit() else []
+        every = " ".join(plan.values()).split()
 
-        if t == 0:
-            first = [("v", 0), ("s", 2), ("v", 1), ("s", 3)]
-            second = [("s", 2, 512, 1024), ("s", 3, 512, 1024), ("v", 0, 512, 1024), ("s", 1, 768, 1024), ("v", 1, 512, 768)]
-        else:
-            first = [("s", 0), ("s", 1), ("v", 2), ("v", 3)]
-            second = [("s", 0, 512, 1024), ("s", 1, 512, 1024), ("s", 2, 512, 1024), ("v", 3, 512, 768), ("s", 3, 768, 1024)]
-        for e, el in first:
-            gather(e, el, 0, 512)
-        quant(0, 512)
-        for e, el, lo, hi in second:
-            gather(e, el, lo, hi)
-        for c in range(4):
-            cols(c)
-        quant(512, 768)
-        quant(768, 1024)
-        rows(0, 0)
-        rows(0, 1024)
-        op("s", act(T.CC[:, 0:4], T.psC[:, 0:2048:512], ACT.Copy), [("psC", 0, 2048)], [("CC", 0, 4)])
-        op("s", act(T.NCC[:, 0:4], T.psC[:, 0:2048:512], ACT.Copy, scale=-1.0), [("psC", 0, 2048)], [("NCC", 0, 4)])
-        for c in range(4, 8):
-            cols(c)
-        rows(1, 0)
-        rows(1, 1024)
+        def some(k, test):
+            return [x for x in every if x[0] == k and x[1:2].isdigit() and test([int(y) for y in x[1:].split(".")])]
+        if name == "low":
+            return ["b0", "b1", "b2", "b3"]
+        if kind == "t":
+            return ["w" + name[1], "h" + name[1]]
+        if kind == "n":
+            return some("t", lambda m: n[0] <= 128 * m[0] < n[1])
+        if kind == "x":
+            return some("n", lambda m: m[0] <= 128 * n[0] < m[1]) + ["p0", "p1"]
+        if kind == "y":
+            return some("n", lambda m: m[0] < 256 * n[0] + 256 and 256 * n[0] < m[1]) + ["f%d" % (2 * n[0]), "f%d" % (2 * n[0] + 1)]
+        if kind == "o":
+            return ["d%d" % (4 * n[0] + k) for k in range(4)]
+        if kind == "p":
+            return ["o" + name[1]]
+        if kind == "f":
+            return ["p0", "p1"]
+        if kind == "i":
+            return ["u"]
+        if kind == "m":
+            return ["k0"]
+        if kind == "z":
+            return (["b4"] if n[0] < 4 else []) + (["low"] if n[1] > 4 else [])
+        if kind == "g":
+            return some("x", lambda m: m[0] == n[0])
+        if kind == "q":
+            return some("g", lambda m: m[1] < n[1] and n[0] < m[2])
+        if kind == "r":
+            return some("q", lambda m: m[0] // 512 == n[0]) + [x for x in every if x in ("u", "i0")]
+        if kind == "c":
+            return (some("q", lambda m: m[0] < 128 * n[0] + 128 and 128 * n[0] < m[1]) + some("t", lambda m: True)
+                    + [x for x in every if x in ("u", "i0")] + (["k0"] if n[0] > 3 else []))
+        if kind == "k":
+            return ["c%d" % (4 * n[0] + k) for k in range(4)]
+        if kind in "el":
+            return ["k%d" % (n[0] // 4), "r%d.0" % (n[0] // 4)]
+        if kind == "s":
+            return ["k1" if n[0] > 3 else "m0", "r%d.%d" % (n[1] // 512, name in plan["s"].split())]
+        if kind in "vab":
+            chain = "vab" if n[0] < 4 else "avb"
+            k = chain.index(kind)
+            mine = [chain[k - 1] + name[1]] if k else []
+            if kind == "v":
+                return mine + some("e", lambda m: m[0] == n[0]) + some("l", lambda m: m[0] == n[0])
+            if kind == "b" and 4 <= n[0] < 7:
+                mine.append("b%d" % (n[0] + 1))
+            return mine + some("s", lambda m: m[0] == n[0] and m[1] // 512 == "ab".index(kind))
+        return []
 
-        def sign(c, a, b):
-            kw = {"bias": T.NCC[:, c:c + 1]} if c < 4 else {"bias": T.CC[:, c:c + 1], "scale": -1.0}
-            op("s", act(T["CU%d" % c][:, a:b], T.psR[:, 1024 + a:1024 + b], ACT.Sign, **kw),
-               [("psR", 1024 + a, 1024 + b), ("NCC" if c < 4 else "CC", c, c + 1)], [("CU%d" % c, a, b)])
+    def play(t, plan):
+        left, done = {e: plan[e].split() for e in plan}, set()
+        while any(left.values()):
+            ready = [e for e in left if left[e] and all(x in done for x in after(left[e][0], plan))]
+            name = left[ready[0]].pop(0)
+            step(t, ready[0], name)
+            done.add(name)
 
-        def eq(c):
-            cb, nm = T["CB%d" % c], "CB%d" % c
-            s = 1 if c < 4 else -1
-            d = 128 * c + 128 if c < 3 else 1024
-            op("v", ts(cb[:, d:d + 128], T.psR[:, 128 * c:128 * c + 128], T.CC[:, c:c + 1], None, A.is_equal),
-               [("psR", 128 * c, 128 * c + 128), ("CC", c, c + 1)], [(nm, d, d + 128)])
-            op("g", lambda: g.affine_select(cb[:, d:d + 128], cb[:, d:d + 128], [[-s, 128]], A.is_gt, 0.0, 0, s),
-               [(nm, d, d + 128)], [(nm, d, d + 128)])
-
-        def beat(c, a, b, o):
-            op("v", ts(T["CB%d" % c][:, a:b], T.psR[:, a:b], T.CC[:, c:c + 1], None, o),
-               [("psR", a, b), ("CC", c, c + 1)], [("CB%d" % c, a, b)])
-
-        def add_up(src, a, b, dst, end):
-            n = (b - a) // 2
-            op("v", scan(T[dst][:, end - n:end], T[src][:, a:a + n], T[src][:, a + n:b], A.add, A.add),
-               [(src, a, b)], [(dst, end - n, end)])
-
-        def short(c):
-            a, b = (0, 128 * c + 256) if c < 3 else (0 if c == 3 else 128 * c, 1152)
-            add_up("CB%d" % c, a, b, "SCA", 576 * c + 576)
-
-        def long(c):
-            a, b = (128 * c + 128, 1024) if c < 4 else (0, 128 * c)
-            add_up("CU%d" % c, a, b, "SCB", 448 * c + 448)
-
-        for c in range(3):
-            sign(c, 128 * c + 128, 512)
-        for c in range(4):
-            eq(c)
-        for c in range(4):
-            beat(c, 128 * c, 128 * c + 128, A.is_gt)
-            if c:
-                beat(c, 0, 128 * c, A.is_ge)
-        for c in range(3):
-            short(c)
-        op("s", act(T.CC[:, 4:8], T.psC[:, 0:2048:512], ACT.Copy), [("psC", 0, 2048)], [("CC", 4, 8)])
-        for c in (4, 7, 6, 5):
-            sign(c, 0, 512)
-        for c in (5, 6, 7):
-            sign(c, 512, 128 * c)
-        for c in range(3):
-            sign(c, 512, 1024)
+    for t in range(ROUNDS):
+        QH, SH, nQH, nSH = T["QH%d" % t], T["SH%d" % t], "QH%d" % t, "SH%d" % t
+        play(t, LATER if t else FIRST)
         if t == 0:
             op("s", act(T.FVN[:], T.FVP[:].indirect(T.POSL[:, 0:64]), ACT.Copy),
                [("FVP.%d" % q, 0, 1024) for q in range(16)] + [("POSL", 0, 64)], [("FVN", 0, 1024)])
-        for c in range(4, 8):
-            eq(c)
-        beat(3, 512, 1024, A.is_gt)
-        for c in range(4, 8):
-            beat(c, 128 * c, 128 * c + 128, A.is_lt)
-            if c < 7:
-                beat(c, 128 * c + 128, 1024, A.is_le)
-        for c in range(3, 8):
-            short(c)
-        long(4)
-        op("v", ts(T.XA[:, 0:3], T.SCA[:, 575:1728:576], -1.0, 1023.0, A.mult, A.add), [("SCA", 0, 1728)], [("XA", 0, 3)])
-        op("v", ts(T.OFR[:, 3:4], T.SCA[:, 2303:2304], -1.0, 1023.0, A.mult, A.add), [("SCA", 1728, 2304)], [("OFR", 3, 4)])
-        for c in (5, 6, 7, 0):
-            long(c)
-        op("v", tt(T.OFR[:, 4:8], T.SCA[:, 2879:4608:576], T.SCB[:, 2239:3584:448], A.add),
-           [("SCA", 2304, 4608), ("SCB", 1792, 3584)], [("OFR", 4, 8)])
-        for c in (1, 2):
-            long(c)
-        op("v", tt(T.OFR[:, 0:3], T.XA[:, 0:3], T.SCB[:, 447:1344:448], A.subtract), [("XA", 0, 3), ("SCB", 0, 1344)], [("OFR", 0, 3)])
-        op("v", cp(T.WIN[:, 0:1024].indirect(T.OFR[:, 0:8]), T.IV[:]), [("OFR", 0, 8), ("IV", 0, 128)], [("WIN", 0, 1024)])
-        op("v", lambda: V.transpose(T.TT[:, 0:128], T.WIN[:, 896:1024]), [("WIN", 896, 1024)], [("TT.0", 0, 128)])
-        op("v", lambda: V.transpose(T.TT[:, 128:288], T.WIN[:, 880:1040]), [("WIN", 880, 1040)], [("TT.1", 0, 160)])
-        op("v", tt(T.SA[:, 0:9], T.TT[:, 0:288:32], T.TT[:, 16:288:32], A.add), [("TT.0", 0, 128), ("TT.1", 0, 160)], [("SA", 0, 9)])
-        op("v", tt(T.SB[0:64, 0:9], T.SA[0:64, 0:9], T.SA[64:128, 0:9], A.add), [("SA", 0, 9)], [("SB", 0, 9)])
-        for k in range(4):
-            op("v", tt(T.SC[32 * k:32 * k + 32, 0:9], T.SB[0:32, 0:9], T.SB[32:64, 0:9], A.add), [("SB", 0, 9)], [("SC.%d" % k, 0, 9)])
-        rC = [("SC.%d" % k, 0, 9) for k in range(4)]
+        op("v", lambda: V.transpose(T.TT[:, 0:128], T.WIN[:, 896:1024]), [("WIN", 896, 1024)], [("TT", 0, 128)])
+        op("v", lambda: V.transpose(T.TT[:, 128:288], T.WIN[:, 880:1040]), [("WIN", 880, 1040)], [("TT", 128, 288)])
+        op("v", cp(T.G0[:], T.TT[:].indirect(T.GL[:, 0:1])), [("TT", 0, 288), ("GL", 0, 1)], [("G0", 0, 16)])
+        op("v", tt(T.G1[0:64, :], T.G0[0:64, :], T.G0[64:128, :], A.add), [("G0", 0, 16)], [("G1", 0, 16)])
+        op("v", tt(T.G2[0:64, :], T.G1[0:64, 0:8], T.G1[0:64, 8:16], A.add), [("G1", 0, 16)], [("G2", 0, 8)])
         LST, nL = T["LST%d" % t], "LST%d" % t
-        op("v", tt(T.PP[:, 0:9], T.SC[:, 0:9], T.MK[:, 0:9], A.mult), rC + [("MK", 0, 18)], [("PP", 0, 9)])
-        op("v", tt(T.PP[:, 9:18], T.SC[:, 0:9], T.MK[:, 9:18], A.mult), rC + [("MK", 0, 18)], [("PP", 9, 18)])
-        op("v", tt(LST[:, 0:8:2], T.PP[:, 0:4], T.PP[:, 4:8], A.add), [("PP", 0, 9)], [(nL + ".0", 0, 8)])
-        op("v", tt(LST[:, 1:8:2], T.PP[:, 9:13], T.PP[:, 14:18], A.add), [("PP", 9, 18)], [(nL + ".1", 0, 8)])
-        rL = [(nL + ".0", 0, 8), (nL + ".1", 0, 8)]
+        for k in range(4):
+            op("v", tt(LST[32 * k:32 * k + 32, :], T.G2[0:32, :], T.G2[32:64, :], A.add), [("G2", 0, 8)], [(nL + ".%d" % k, 0, 8)])
+        rL = [(nL + ".%d" % k, 0, 8) for k in range(4)]
 
         send(t, T["LR%d" % t][:], LST[:], "arrL%d" % t, rL)
         op("v", cp(T["SL%d" % t][:, 0:128].bitcast(dt.uint32), QH[:, 0:1024].bitcast(dt.uint32).indirect(LST[:, 0:8])),
@@ -354,16 +439,25 @@ def rank_program(g, core, T, topo):
         note("a", ("arrL%d" % t, ne), [], [("LR%d" % t, 0, 8)])
         note("a", ("arrC%d" % t, ne), [], [("LC%d" % t, 0, 128)])
         note("a", ("arrS%d" % t, ne), [], [("LS%d" % t, 0, 128)])
+        if t + 1 < ROUNDS:
+            iota("WIN", [[0, 128]], 0, 0, 896, 1024)
         FLS, nF = T["FLS%d" % t], "FLS%d" % t
         op("s", act(T.FR[:], T.IOT[:].indirect(LST[:, 0:8]), ACT.Copy), [("IOT", 0, 1024)] + rL, [("FR", 0, 128)])
+        if t + 1 < ROUNDS:
+            lay_scales(t + 1, "s")
         op("s", act(FLS[:], T.FR[:].indirect(T.REV[:, 0:8]), ACT.Copy), [("FR", 0, 128), ("REV", 0, 8)], [(nF, 0, 128)])
         dma("y", T.fl[t:t + 1, :], FLS[0:1, :], "dout", nout, [(nF, 0, 128)], [])
         if t == 0:
             for e in range(4):
-                op("v", cp(T["XP%d" % e][:, 0:512], T.XI[:, e:2048:4]), [("XI", 0, 2048)], [("XP%d" % e, 0, 512)])
-            lay_u(1)
+                k = "s" if e == 3 else "v"
+                op(k, move(k, T["XP%d" % e][:, 0:512], T.XI[:, e:2048:4]), [("XI", 0, 2048)], [("XP%d" % e, 0, 512)])
+            op("v", cp(T.OFP[:], T.FVT[:]), [("FVT", 0, 64)], [("OFP", 0, 64)])
+            for m, (a, j) in enumerate(segs):
+                op("v", ts(T.KM[:, a:a + 128 - j], T.PL0[:, j:128], T.QM[:, m:m + 1], None, A.is_gt),
+                   [("PL0", 0, 128), ("QM", 0, 8)], [("KM", a, a + 128 - j)])
+            lay_codes(1)
         if t == 1:
-            lay_u(2)
+            lay_codes(2)
             op("v", lambda: V.quantize_mx(T.QWY[:, 0:128], T.SWY[:, 0:128], T.WYB[:, 0:512]), [("WYB", 0, 512)], [("QWY", 0, 128), ("SWY", 0, 128)])
         if t == 2:
             for e in range(4):
@@ -372,54 +466,26 @@ def rank_program(g, core, T, topo):
         LR, nR = T["LR%d" % t], "LR%d" % t
         op("v", tt(T.VM[:], T.FVN[:].indirect(LR[:, 0:8]), T.MD[:], A.mult), [("FVN", 0, 1024), (nR, 0, 8), ("MD", 0, 128)], [("VM", 0, 128)])
         op("s", act(T.VRO[:], T.FVN[:].indirect(LR[:, 0:8]), ACT.Copy), [("FVN", 0, 1024), (nR, 0, 8)], [("VRO", 0, 128)])
-        op("v", scan(T.VC[:, 16:144], T.VM[:], T.ZR[:], A.add, A.add), [("VM", 0, 128), ("ZR", 0, 128)], [("VC", 16, 144)])
-        op("v", tt(T.OFG[:], T.VC[:, 31:144:16], T.VC[:, 15:128:16], A.subtract), [("VC", 0, 144)], [("OFG", 0, 8)])
-        op("v", tt(T.VW[:], T.VC[:, 31:144:16], T.VC[:, 15:128:16], A.subtract), [("VC", 0, 144)], [("VW", 0, 8)])
-        for e in range(4):
-            op("s", act(T.OLD[:, 128 * e:128 * e + 128], T["XP%d" % e][:, 0:512].indirect(T.OFG[:, 0:8]), ACT.Copy, scale=32.0),
-               [("XP%d" % e, 0, 512), ("OFG", 0, 8)], [("OLD", 128 * e, 128 * e + 128)])
-        for m in range(8):
-            a = 128 * m
-            op("v", ts(T.EQ[:, a:a + 128], T.VRO[:], T.VW[:, m:m + 1], 512.0, A.is_equal, A.mult),
-               [("VRO", 0, 128), ("VW", 0, 8)], [("EQ", a, a + 128)])
-        op("v", scan(T.LOS[:], T.EQ[:], T.KM[:], A.add, A.mult), [("EQ", 0, 1024), ("KM", 0, 1024)], [("LOS", 0, 1024)])
-        if t < 2:
-            op("v", tt(T.OFS[:], T.LOS[:, 127:1024:128], T.VW[:], A.add), [("LOS", 0, 1024), ("VW", 0, 8)], [("OFS", 0, 8)])
+        op("v", scan(T.VC[:, 8:72], T.VM[:, 0:128:2], T.VM[:, 1:128:2], A.add, A.add), [("VM", 0, 128)], [("VC", 8, 72)])
+        op("v", tt(T.VW[:], T.VC[:, 15:72:8], T.VC[:, 7:64:8], A.subtract), [("VC", 0, 72)], [("VW", 0, 8)])
+        op("v", tt(T.OFG[:], T.VC[:, 15:72:8], T.VC[:, 7:64:8], A.subtract), [("VC", 0, 72)], [("OFG", 0, 8)])
+    play(ROUNDS, LAST)
+
+    for h in range(4):
+        a, e = 128 * h, "s" if h < 3 else "v"
+        op("v", lambda: V.quantize_mx(T.QX[:, a:a + 128], T.SX[:, a:a + 128], T.XF[:, 4 * a:4 * a + 512]),
+           [("XF.%d" % k, 0, 4096) for k in range(4)], [("QX", a, a + 128), ("SX", a, a + 128)])
+        op("t", mm(T.psR[:, 4 * a:4 * a + 128], T.QWY[:, 0:128], T.SWY[:, 0:128], T.QX[:, a:a + 128], T.SX[:, a:a + 128]),
+           [("QWY", 0, 128), ("SWY", 0, 128), ("QX", a, a + 128), ("SX", a, a + 128)], [("psR", 4 * a, 4 * a + 512)])
+        op(e, move(e, T.YS[:, a:a + 128], T.psR[:, 4 * a:4 * a + 128]), [("psR", 4 * a, 4 * a + 128)], [("YS", a, a + 128)])
+    for k in "c0 c1 y0 c2 c3 y1 y2 y3".split():
+        a = 128 * int(k[1])
+        if k[0] == "c":
+            dma("y", T.oc[:, 4 * a:4 * a + 512], T.QX[:, a:a + 128].bitcast(dt.uint8), "dout", nout, [("QX", a, a + 128)], [])
         else:
-            op("v", tt(T.VD[:], T.LOS[:, 127:1024:128], T.VW[:], A.add), [("LOS", 0, 1024), ("VW", 0, 8)], [("VD", 0, 8)])
-            for e in range(4):
-                op("v", ts(T.OFX[:, 8 * e:8 * e + 8], T.VD[:], 4.0, float(e), A.mult, A.add), [("VD", 0, 8)], [("OFX", 8 * e, 8 * e + 8)])
-
-        for b in range(4):
-            op("t", mm(T.psC[:, 512 * b:512 * b + 128], T.WQ[:, 128 * b:128 * b + 128], T.WSC[:, 128 * b:128 * b + 128],
-                       T["LC%d" % t][:, 0:128], T["LS%d" % t][:, 0:128]),
-               [("WQ", 0, 512), ("WSC", 0, 512), ("LC%d" % t, 0, 128), ("LS%d" % t, 0, 128)], [("psC", 512 * b, 512 * b + 512)])
-        for b in range(4):
-            a = 128 * b
-            op("v", tt(T.TMP[:, a:a + 128], T.psC[:, 512 * b:512 * b + 128], T.OLD[:, a:a + 128], A.add),
-               [("psC", 512 * b, 512 * b + 128), ("OLD", a, a + 128)], [("TMP", a, a + 128)])
-            op("s", act(T.NV[:, a:a + 128], T.TMP[:, a:a + 128], ACT.Copy, scale=1.0 / 64), [("TMP", a, a + 128)], [("NV", a, a + 128)])
-        for b in range(4):
-            if t < 2:
-                op("v", cp(T["XP%d" % b][:, 0:1024].indirect(T.OFS[:, 0:8]), T.NV[:, 128 * b:128 * b + 128]),
-                   [("OFS", 0, 8), ("NV", 128 * b, 128 * b + 128)], [("XP%d" % b, 0, 1024)])
-            else:
-                op("v", cp(T.XF[:, 0:4096].indirect(T.OFX[:, 8 * b:8 * b + 8]), T.NV[:, 128 * b:128 * b + 128]),
-                   [("OFX", 0, 32), ("NV", 128 * b, 128 * b + 128)], [("XF.%d" % e, 0, 4096) for e in range(4)])
-
-    for h in range(2):
-        a = 256 * h
-        op("v", lambda: V.quantize_mx(T.QX[:, a:a + 256], T.SX[:, a:a + 256], T.XF[:, 4 * a:4 * a + 1024]),
-           [("XF.%d" % e, 0, 4096) for e in range(4)], [("QX", a, a + 256), ("SX", a, a + 256)])
-        op("t", mm(T.psR[:, 1024 * h:1024 * h + 256], T.QWY[:, 0:128], T.SWY[:, 0:128], T.QX[:, a:a + 256], T.SX[:, a:a + 256]),
-           [("QWY", 0, 128), ("SWY", 0, 128), ("QX", a, a + 256), ("SX", a, a + 256)], [("psR", 1024 * h, 1024 * h + 512)])
-    op("s", act(T.YS[:, 0:256], T.psR[:, 0:256], ACT.Copy), [("psR", 0, 256)], [("YS", 0, 256)])
-    op("v", cp(T.YS[:, 256:512], T.psR[:, 1024:1280]), [("psR", 1024, 1280)], [("YS", 256, 512)])
-    dma("y", T.oc[:, 0:2048], T.QX[:, 0:512].bitcast(dt.uint8), "dout", nout, [("QX", 0, 512)], [])
-    dma("s", T.y[:, 0:256], T.YS[:, 0:256], "dout", nout, [("YS", 0, 256)], [])
-    dma("y", T.y[:, 256:512], T.YS[:, 256:512], "dout", nout, [("YS", 256, 512)], [])
+            dma("y", T.y[:, a:a + 128], T.YS[:, a:a + 128], "dout", nout, [("YS", a, a + 128)], [])
     for k in range(4):
-        dma("y" if k % 2 else "s", T.osc[4 * k:4 * k + 4, :], T.SX[32 * k:32 * k + 4, 0:512], "dout", nout, [("SX", 0, 512)], [])
+        dma("s", T.osc[4 * k:4 * k + 4, :], T.SX[32 * k:32 * k + 4, 0:512], "dout", nout, [("SX", 0, 512)], [])
     for sem in sorted(total):
         if most.get(sem, 0) < total[sem]:
             need("g", (sem, total[sem]))

@@ -1,7 +1,7 @@
 from concourse.mybir import dt, AluOpType, ActivationFunctionType
 
 ROUNDS = 3
-UW, WW = 1666, 770
+UW = 1282
 
 F32, BF, F16, I32, U16, CODE, U8 = "float32", "bfloat16", "float16", "int32", "uint16", "float8_e4m3fn_x4", "uint8"
 SCRATCH = {
@@ -12,20 +12,19 @@ SCRATCH = {
     "QX": ("sbuf", [128, 512], CODE), "SX": ("sbuf", [128, 512], U8),
     "FVT": ("sbuf", [128, 64], I32), "OFH": ("sbuf", [128, 256], U16), "OFP": ("sbuf", [128, 64], U16),
     "FVP": ("sbuf", [128, 1024], I32), "POSL": ("sbuf", [128, 64], U16), "FVN": ("sbuf", [128, 1024], F32),
-    "CC": ("sbuf", [128, 8], F32), "NCC": ("sbuf", [128, 4], F32),
-    "UA": ("sbuf", [128, 8 * UW], U16), "WA": ("sbuf", [128, 8 * WW], F16),
-    "SCL": ("sbuf", [128, 1028], U16), "OU": ("sbuf", [128, 330], U16),
-    "WIN": ("sbuf", [128, 1040], F32), "TT": ("sbuf", [128, 288], F32),
+    "CC": ("sbuf", [128, 8], F32), "AB": ("sbuf", [128, 8], F32), "UP": ("sbuf", [128, 8], F32),
+    "UA": ("sbuf", [128, 8 * UW], U16), "CM": ("sbuf", [128, 1024], F32), "LT": ("sbuf", [128, 128], BF),
+    "OU": ("sbuf", [128, 2056], U16), "WIN": ("sbuf", [128, 1040], F32), "TT": ("sbuf", [128, 288], F32),
     "GL": ("sbuf", [128, 2], U16), "G0": ("sbuf", [128, 16], F32), "G1": ("sbuf", [64, 16], F32), "G2": ("sbuf", [64, 8], F32),
     "P32": ("sbuf", [128, 1], I32), "PI": ("sbuf", [128, 8], I32), "PF": ("sbuf", [128, 16], F32),
     "IV0": ("sbuf", [128, 128], F32), "IV": ("sbuf", [128, 128], F32),
-    "MD0": ("sbuf", [128, 128], F32), "MD": ("sbuf", [128, 128], F32),
+    "MD0": ("sbuf", [128, 128], F32), "MD": ("sbuf", [128, 128], F32), "RM": ("sbuf", [128, 128], F32),
     "KM": ("sbuf", [128, 768], F16), "IOT": ("sbuf", [128, 1024], F32),
     "RV0": ("sbuf", [128, 8], F32), "QM": ("sbuf", [128, 8], F32), "REV": ("sbuf", [128, 8], U16),
     "PL0": ("sbuf", [128, 128], BF),
     "VRO": ("sbuf", [128, 128], F16), "VM": ("sbuf", [128, 128], F32),
-    "VC": ("sbuf", [128, 72], F32), "VW": ("sbuf", [128, 8], F32), "EQ": ("sbuf", [128, 768], F16),
-    "LOS": ("sbuf", [128, 768], F16), "VD": ("sbuf", [128, 8], F32),
+    "VC": ("sbuf", [128, 128], F32), "VE": ("sbuf", [128, 32], F32), "EQ": ("sbuf", [128, 768], F16),
+    "LOS": ("sbuf", [128, 768], F16),
     "OFG": ("sbuf", [128, 8], U16), "OFS": ("sbuf", [128, 8], U16), "OFX": ("sbuf", [128, 32], U16),
     "FR": ("sbuf", [128, 128], F32),
     "OLD": ("sbuf", [128, 512], F32), "TMP": ("sbuf", [128, 512], F32), "NV": ("sbuf", [128, 512], BF),
@@ -52,20 +51,21 @@ SEMAPHORES = ["cv", "cs", "ct", "cg", "dx", "dfv", "du", "dfp", "dw", "dwy", "do
 for _t in range(ROUNDS):
     SEMAPHORES += ["arrL%d" % _t, "arrC%d" % _t, "arrS%d" % _t]
 
-LOSERS = "d0 d1 d2 d3 d4 d5 d6 d7 o0 o1 "
-FIRST = {"v": "g0.0.512 g1.0.512 u i0 q0.512 g1.512.1024 g0.512.768 q768.1024 q512.768 e0 s1.128.512 l2 e2 l1 e1 v0 e3 e7 e4 l4 l5 e6 v2 a6 "
-              "e5 l3 s3.512.1024 v3 v1 a4 l6 a2 a1 a7 a5 s0.896.1024 a3 v7 a0 b1 v5 b3 v4 v6 b0 b7 b2 b6 low b5 b4 z0.8",
-         "s": "g0.768.1024 g3.0.512 g2.0.512 g3.512.1024 g2.512.1024 k0 m0 s2.256.512 s3.384.512 s0.0.512 k1 s6.0.512 s4.0.512 s7.0.512 "
-              "s0.512.896 s5.0.512 s7.512.1024 s1.512.1024 s2.512.1024 s6.512.896 s5.512.768 s4.512.640",
-         "t": "c0 c1 r0.0 c2 c3 r0.1 c4 c5 c6 c7 r1.0 r1.1"}
-LATER = {"v": LOSERS + "t0 p0 p1 t1 t2 t3 x0 x1 x2 x3 g2.0.512 g3.0.256 q256.512 q0.256 g3.512.768 g2.512.1024 q512.768 q768.1024 "
-              "l2 e1 e0 l1 e2 s1.128.512 l4 e3 l3 v1 e5 e7 l5 v2 e4 v0 e6 a1 a7 v3 a6 v7 a3 a4 s0.896.1024 a0 a2 b1 v4 l6 a5 s3.512.1024 "
-              "v6 b2 b7 v5 b0 b3 b6 b5 low b4 z0.8",
-         "s": "h0 h1 h2 h3 n0.128 n128.256 n256.512 g0.0.512 g1.0.512 g3.256.512 g0.512.1024 g1.512.1024 g3.768.1024 k0 m0 s2.256.512 "
-              "s3.384.512 s0.0.512 k1 s7.0.512 s5.0.512 s6.0.512 s0.512.896 s4.0.512 s1.512.1024 s7.512.1024 s2.512.1024 s5.512.768 "
-              "s6.512.896 s4.512.640",
-         "t": "w0 w1 w2 w3 c2 c3 c0 c1 r0.1 r0.0 c4 c5 c6 c7 r1.0 r1.1"}
-LAST = {"v": LOSERS + "p0 p1 t0 t1 f0 f1 t2 t3 f2 f3 y0 y1", "s": "h0 h1 h2 h3 n0.128 n128.256 n256.384 n384.512", "t": "w0 w1 w2 w3"}
+FIRST = {"v": "g1.0.1024 u g2.512.768 q256.512 q0.256 g3.512.1024 q512.768 q768.1024 l1.256.512 D1 M0 l0.128.512 e2 s1.0.128 "
+              "l2.384.512 e1 e0 e3 k1 a2 a1 s7.0.512 l6.896.1024 D4 a7 D7 M1 s5.512.640 s5.128.512 D6 a3 a4 e6 b2 e4 a0 b3 e7 a5 "
+              "s6.512.768 b7 a6 e5 b1 b6 b5 b0 b4 z0.8",
+         "s": "g0.0.512 g2.256.512 g3.0.512 g2.0.256 i0 g0.512.1024 g2.768.1024 k0 m0 s2.0.256 D0 D2 D3 s3.0.384 l1.512.1024 l2.512.1024 m1 "
+              "s4.0.512 l3.512.1024 s7.512.896 s5.0.128 l5.768.1024 D5 s6.0.512 l0.512.1024 l4.640.1024",
+         "t": "c3 c2 c0 c1 r0.1 r0.0 c5 r1.1 c4 c6 c7 r1.0"}
+LATER = {"v": "Va Vb d4 d5 d6 d7 d0 d1 d2 d3 o1 o0 t0 p1 t3 p0 t2 t1 x0 x3 x1 x2 g1.0.256 g2.0.256 g2.256.640 q0.256 q256.512 g1.512.896 "
+              "g0.896.1024 k0 q512.640 q640.768 q768.896 q896.1024 M0 D2 l0.128.512 e3 e2 k1 s3.0.256 s5.0.512 a2 l1.256.384 e1 s6.0.512 "
+              "D4 b2 e0 M1 a6 D7 a1 a5 s5.512.640 e7 e4 s7.512.896 a0 b1 a7 l6.896.1024 a4 e6 a3 e5 b7 b0 b3 b5 b6 b4 z0.8",
+         "s": "Vr Vc h0 h3 h2 h1 n0.128 n384.512 n128.256 n256.384 g0.0.896 g3.0.512 g1.256.512 g3.512.1024 g2.640.1024 g1.896.1024 m0 "
+              "s2.0.256 D3 s3.256.384 s1.0.128 D0 l1.384.512 D1 l2.384.512 l1.512.1024 m1 l2.512.1024 s4.0.512 l0.512.1024 l5.768.1024 "
+              "s7.0.512 D6 D5 l3.512.1024 s6.512.768 l4.640.1024",
+         "t": "w0 w3 w2 w1 c0 c1 c2 c3 r0.1 r0.0 c4 c5 c6 c7 r1.1 r1.0"}
+LAST = {"v": "Va Vb d4 d5 d6 d7 d0 d1 d2 d3 E3 o1 o0 p1.1 p1.3 t1 t0 p1.0 t3 p0.1 p0.0 p1.2 p0.2 p0.3 t2 y0 y1",
+        "s": "Vr Vc E1 E0 h1 E2 h0 h3 h2 n128.256 n0.128 n256.512", "t": "w1 w0 w3 w2"}
 
 
 def rank_program(g, core, T, topo):
@@ -166,59 +166,42 @@ def rank_program(g, core, T, topo):
     iota("P32", [[0, 1]], 0, 1, 0, 1)
     iota("PL0", [[1, 128]], 0, 0, 0, 128)
     iota("RV0", [[16, 8]], 0, 0, 0, 8)
-    iota("IV0", [[128, 4], [1, 16]], 512, 0, 0, 64)
-    iota("IV0", [[128, 4], [1, 16]], 0, 0, 64, 128)
+    iota("IV0", [[128, 8], [1, 16]], 0, 0, 0, 128)
     iota("MD0", [[0, 8], [1, 16]], 0, 0, 0, 128)
     iota("WIN", [[0, 160]], 0, 0, 880, 1040)
     iota("IOT", [[1, 1024]], 0, 0, 0, 1024)
-    op("v", ms(T.VC[:, 0:8], 0.0), [], [("VC", 0, 8)])
+    op("v", ms(T.PF[:, 12:13], 2.0 ** -126), [], [("PF", 12, 13)])
     for t in range(ROUNDS):
         op("v", ms(T["UO%d" % t][:], t), [], [("UO%d" % t, 0, 8)])
-
-    def bits(k, *a):
+    for k, a in enumerate([(15, None, A.bitwise_and), (112, None, A.bitwise_and), (4, 1, A.arith_shift_right, A.bitwise_and),
+                           (1, None, A.bitwise_and), (6, None, A.bitwise_and), (8, None, A.bitwise_and)]):
         op("v", ts(T.PI[:, k:k + 1], T.P32[:], *a), [("P32", 0, 1)], [("PI", k, k + 1)])
-
-    def col(k, j, *a):
-        reads = [("PI", j, j + 1)] + [("PF", 0, 16) for s in a[:2] if not isinstance(s, (float, int)) and s is not None]
-        op("v", ts(T.PF[:, k:k + 1], T.PI[:, j:j + 1], *a), reads, [("PF", k, k + 1)])
-
-    bits(0, 15, None, A.bitwise_and)
-    bits(1, 112, None, A.bitwise_and)
-    bits(2, 4, 1, A.arith_shift_right, A.bitwise_and)
-    bits(3, 1, None, A.bitwise_and)
-    bits(4, 6, None, A.bitwise_and)
-    bits(5, 8, None, A.bitwise_and)
-    col(0, 0, 1.0, None, A.mult)
-    col(1, 1, 1.0, None, A.mult)
-    col(2, 0, 64.0, None, A.mult)
-    col(3, 2, 1.0, None, A.mult)
-    col(4, 2, -32.0, 160.0, A.mult, A.add)
-    col(5, 4, 16.0, None, A.mult)
-    col(6, 3, T.PF[:, 3:4], T.PF[:, 4:5], A.not_equal, A.mult)
-    col(7, 5, 2.0, T.PF[:, 5:6], A.mult, A.add)
-    QF, GF, Q64 = T.PF[:, 0:1], T.PF[:, 1:2], T.PF[:, 2:3]
-    rP = [("PF", 0, 3)]
-    op("v", ts(T.QM[:], T.RV0[:], QF, None, A.add), [("RV0", 0, 8)] + rP, [("QM", 0, 8)])
-    op("v", ts(T.GL[:, 0:1], T.PF[:, 6:7], T.PF[:, 7:8], None, A.add), [("PF", 0, 16)], [("GL", 0, 1)])
-    op("v", ts(T.POSL[:], T.PL0[:, 0:64], Q64, None, A.add), [("PL0", 0, 128)] + rP, [("POSL", 0, 64)])
-    op("v", ts(T.REV[:], T.QM[:], -1.0, 127.0, A.mult, A.add), [("QM", 0, 8)], [("REV", 0, 8)])
-    for nm, c0, z, s in (("UA", 0, 832, -128), ("UA", 0, 1664, 0), ("UA", 4, 768, 128), ("WA", 4, 1280, -128)):
-        d = (UW if nm == "UA" else WW) + s
-        op("s", act(T[nm][:, z + d * c0:z + d * (c0 + 3) + 1:d], T.PL0[:, 0:4], ACT.Copy, scale=0.0), [("PL0", 0, 128)],
-           [(nm, z + d * c, z + d * c + 1) for c in range(c0, c0 + 4)])
-    op("v", ts(T.IV[:], T.IV0[:], GF, None, A.add), [("IV0", 0, 128)] + rP, [("IV", 0, 128)])
-    op("v", ts(T.MD[:], T.MD0[:], QF, None, A.is_equal), [("MD0", 0, 128)] + rP, [("MD", 0, 128)])
-    for e in (0, 3, 2, 1):
+    op("v", cp(T.PF[:, 13:14], T.P32[:]), [("P32", 0, 1)], [("PF", 13, 14)])
+    op("v", cp(T.PF[:, 0:6], T.PI[:, 0:6]), [("PI", 0, 6)], [("PF", 0, 6)])
+    op("v", ts(T.LT[:], T.PL0[:], T.PF[:, 13:14], None, A.is_gt), [("PL0", 0, 128), ("PF", 13, 14)], [("LT", 0, 128)])
+    op("v", ts(T.PF[:, 6:7], T.PF[:, 2:3], -32.0, 160.0, A.mult, A.add), [("PF", 0, 6)], [("PF", 6, 7)])
+    op("v", ts(T.PF[:, 8:9], T.PF[:, 4:5], 8.0, T.PF[:, 5:6], A.mult, A.add), [("PF", 0, 6)], [("PF", 8, 9)])
+    QF, GF, Q64 = T.PF[:, 0:1], T.PF[:, 1:2], T.PF[:, 10:11]
+    rP = [("PF", 0, 2)]
+    op("s", act(T.UA[:, 1280:8 * UW:UW], T.PL0[:, 0:8], ACT.Copy, scale=0.0), [("PL0", 0, 128)],
+       [("UA", 1280 + UW * c, 1281 + UW * c) for c in range(8)])
+    op("s", act(Q64, QF, ACT.Copy, scale=64.0), rP, [("PF", 10, 11)])
+    op("s", act(T.QM[:], T.RV0[:], ACT.Identity, bias=QF), [("RV0", 0, 8)] + rP, [("QM", 0, 8)])
+    op("s", act(T.IV[:], T.IV0[:], ACT.Identity, bias=GF), [("IV0", 0, 128)] + rP, [("IV", 0, 128)])
+    op("s", act(T.POSL[:], T.PL0[:, 0:64], ACT.Identity, bias=Q64), [("PL0", 0, 128), ("PF", 10, 11)], [("POSL", 0, 64)])
+    op("v", ts(T.PF[:, 7:8], T.PF[:, 3:4], T.PF[:, 2:3], T.PF[:, 6:7], A.not_equal, A.mult), [("PF", 0, 7)], [("PF", 7, 8)])
+    for e in (0, 1, 2, 3):
         op("v", ts(T.OFH[:, 64 * e:64 * e + 64], T.FVT[:], 4.0, float(e), A.mult, A.add), [("FVT", 0, 64)], [("OFH", 64 * e, 64 * e + 64)])
+    op("v", ts(T.GL[:, 0:1], T.PF[:, 8:9], 2.0, T.PF[:, 7:8], A.mult, A.add), [("PF", 7, 9)], [("GL", 0, 1)])
+    op("v", ts(T.REV[:], T.QM[:], -1.0, 127.0, A.mult, A.add), [("QM", 0, 8)], [("REV", 0, 8)])
     segs = [(128 * m, 0) if m < 4 else (256 + 64 * m, 64) for m in range(8)]
 
-    def lay_codes(t):
-        op("v", cp(T["QUR%d" % t][:, 0:128].bitcast(dt.uint32), T.QU[:, 0:128].bitcast(dt.uint32).indirect(T["UO%d" % t][:, 0:8])),
-           [("QU", 0, 128), ("UO%d" % t, 0, 8)], [("QUR%d" % t, 0, 128)])
+    def pick_codes(out, src, n, off, reads):
+        op("v", cp(T[out][:, 0:128].bitcast(dt.uint32), T[src][:, 0:n].bitcast(dt.uint32).indirect(T[off][:, 0:8])),
+           [(src, 0, n)] + reads, [(out, 0, 128)])
 
-    def lay_scales(t, e):
-        op(e, move(e, T["SUR%d" % t][:, 0:128], T.SU[:, 0:128].indirect(T["UO%d" % t][:, 0:8])),
-           [("SU", 0, 128), ("UO%d" % t, 0, 8)], [("SUR%d" % t, 0, 128)])
+    def pick_scales(e, out, src, n, off, reads):
+        op(e, move(e, T[out][:, 0:128], T[src][:, 0:n].indirect(T[off][:, 0:8])), [(src, 0, n)] + reads, [(out, 0, 128)])
 
     partners = [T.cores[rank ^ (1 << t)] for t in range(ROUNDS)]
     common = [e for e in topo.engines(core, partners[0]) if all(e in topo.engines(core, p) for p in partners)]
@@ -235,16 +218,25 @@ def rank_program(g, core, T, topo):
     def step(t, e, name):
         kind, n = name[0], [int(x) for x in name[1:].split(".")] if name[1:2].isdigit() else []
         if t < ROUNDS:
-            QH, SH, QUR, SUR = T["QH%d" % t], T["SH%d" % t], T["QUR%d" % t], T["SUR%d" % t]
+            QH, SH, QUR, SUR = T["QH%d" % t], T["SH%d" % t], T["QUR%d" % t][:, 0:128], T["SUR%d" % t][:, 0:128]
             nQH, nSH = "QH%d" % t, "SH%d" % t
             ru = [("QUR%d" % t, 0, 128), ("SUR%d" % t, 0, 128)]
-        if name == "low":
-            op("v", ts(T.OU[:, 326:330], T.SCL[:, 256:1028:257], -1.0, 1023.0, A.mult, A.add), [("SCL", 0, 1028)], [("OU", 326, 330)])
+        if kind == "V":
+            nR = "LR%d" % (t - 1)
+            hit, rH = T.FVN[:].indirect(T[nR][:, 0:8]), [("FVN", 0, 1024), (nR, 0, 8)]
+            if name == "Va":
+                op("v", tt(T.VM[:], hit, T.MD[:], A.mult), rH + [("MD", 0, 128)], [("VM", 0, 128)])
+            elif name == "Vr":
+                op(e, move(e, T.VRO[:], hit), rH, [("VRO", 0, 128)])
+            elif name == "Vb":
+                op("v", scan(T.VC[:], T.RM[:], T.VM[:], A.mult, A.add), [("VM", 0, 128), ("RM", 0, 128)], [("VC", 0, 128)])
+            else:
+                op(e, move(e, T.OFG[:], T.VC[:, 15:128:16]), [("VC", 0, 128)], [("OFG", 0, 8)])
         elif name == "u":
             op("v", lambda: V.quantize_mx(T.QU[:, 0:128], T.SU[:, 0:128], T.UB[:, 0:512]), [("UB", 0, 512)], [("QU", 0, 128), ("SU", 0, 128)])
-            lay_codes(0)
+            pick_codes("QUR0", "QU", 128, "UO0", [("UO0", 0, 8)])
         elif kind == "i":
-            lay_scales(0, e)
+            pick_scales(e, "SUR0", "SU", 128, "UO0", [("UO0", 0, 8)])
         elif kind == "w":
             b = n[0]
             op("t", mm(T.psC[:, 512 * b:512 * b + 128], T.WQ[:, 128 * b:128 * b + 128], T.WSC[:, 128 * b:128 * b + 128],
@@ -265,22 +257,28 @@ def rank_program(g, core, T, topo):
                [("XP%d" % n[0], 0, 512), ("OFG", 0, 8)], [("OLD", a, a + 128)])
         elif kind == "d":
             a, j = segs[n[0]]
-            op("v", ts(T.EQ[:, a:a + 128 - j], T.VRO[:, j:128], T.VW[:, n[0]:n[0] + 1], 512.0, A.is_equal, A.mult),
-               [("VRO", 0, 128), ("VW", 0, 8)], [("EQ", a, a + 128 - j)])
+            k = 16 * n[0] + 15
+            op("v", ts(T.EQ[:, a:a + 128 - j], T.VRO[:, j:128], T.VC[:, k:k + 1], 512.0 if t < ROUNDS else 2048.0, A.is_equal, A.mult),
+               [("VRO", 0, 128), ("VC", 0, 128)], [("EQ", a, a + 128 - j)])
         elif kind == "o":
             a, b = ((0, 512), (512, 768))[n[0]]
             op("v", scan(T.LOS[:, a:b], T.EQ[:, a:b], T.KM[:, a:b], A.add, A.mult), [("EQ", a, b), ("KM", a, b)], [("LOS", a, b)])
+        elif kind == "E":
+            out, in_ = T.VE[:, 8 * n[0]:8 * n[0] + 8], T.VC[:, 15:128:16]
+            op(e, act(out, in_, ACT.Identity, scale=4.0, bias=T.PL0[:, n[0]:n[0] + 1]) if e == "s" else ts(out, in_, 4.0, float(n[0]), A.mult, A.add),
+               [("VC", 0, 128), ("PL0", 0, 128)], [("VE", 8 * n[0], 8 * n[0] + 8)])
         elif kind == "p":
-            to, a = "OFS" if t < ROUNDS else "VD", 4 * n[0]
-            ends = (T.LOS[:, 127:512:128], T.LOS[:, 575:768:64])[n[0]]
-            op("v", tt(T[to][:, a:a + 4], ends, T.VW[:, a:a + 4], A.add), [("LOS", 512 * n[0], 512 * n[0] + 512), ("VW", 0, 8)], [(to, a, a + 4)])
-        elif kind == "f":
-            a = 8 * n[0]
-            op("v", ts(T.OFX[:, a:a + 8], T.VD[:], 4.0, float(n[0]), A.mult, A.add), [("VD", 0, 8)], [("OFX", a, a + 8)])
+            a = 4 * n[0]
+            ends, rE = (T.LOS[:, 127:512:128], T.LOS[:, 575:768:64])[n[0]], ("LOS", 512 * n[0], 512 * n[0] + 512)
+            if t < ROUNDS:
+                op("v", tt(T.OFS[:, a:a + 4], ends, T.VC[:, 16 * a + 15:16 * a + 64:16], A.add), [rE, ("VC", 0, 128)], [("OFS", a, a + 4)])
+            else:
+                a += 8 * n[1]
+                op("v", tt(T.OFX[:, a:a + 4], ends, T.VE[:, a:a + 4], A.add), [rE, ("VE", a, a + 4)], [("OFX", a, a + 4)])
         elif kind == "z":
             a, b = n
-            op("v", cp(T.WIN[:, 0:1024].indirect(T.OU[:, 322 + a:322 + b]), T.IV[:, 16 * a:16 * b]),
-               [("OU", 322 + a, 322 + b), ("IV", 0, 128)], [("WIN", 0, 1024)])
+            op("v", cp(T.WIN[:, 0:1024].indirect(T.OU[:, 2048 + a:2048 + b]), T.IV[:, 16 * a:16 * b]),
+               [("OU.%d" % c, 0, 1) for c in range(a, b)] + [("IV", 0, 128)], [("WIN", 0, 1024)])
         elif kind == "x":
             a = 128 * n[0]
             op("v", cp(T["XP%d" % n[0]][:, 0:1024].indirect(T.OFS[:, 0:8]), T.NV[:, a:a + 128]),
@@ -303,53 +301,49 @@ def rank_program(g, core, T, topo):
             op("v", lambda: V.quantize_mx(QH[:, a:b], SH[:, a:b], T.H[:, 4 * a:4 * b]),
                [("H.%d" % k, a, b) for k in range(4)], [(nQH, a, b), (nSH, a, b)])
         elif kind == "r":
-            a, base = 512 * n[0], 1024 * n[1]
-            op("t", mm(T.psR[:, base + a:base + a + 512], QUR[:, 0:128], SUR[:, 0:128], QH[:, a:a + 512], SH[:, a:a + 512]),
-               ru + [(nQH, a, a + 512), (nSH, a, a + 512)], [("psR", base + a, base + a + 512)])
+            a = 512 * n[0]
+            b = 1024 * n[1] + a
+            op("t", mm(T.psR[:, b:b + 512], QUR, SUR, QH[:, a:a + 512], SH[:, a:a + 512]),
+               ru + [(nQH, a, a + 512), (nSH, a, a + 512)], [("psR", b, b + 512)])
         elif kind == "c":
             a, k = 128 * n[0], 512 * (n[0] % 4)
-            op("t", mm(T.psC[:, k:k + 128], QH[:, a:a + 128], SH[:, a:a + 128], QUR[:, 0:128], SUR[:, 0:128]),
+            op("t", mm(T.psC[:, k:k + 128], QH[:, a:a + 128], SH[:, a:a + 128], QUR, SUR),
                ru + [(nQH, a, a + 128), (nSH, a, a + 128)], [("psC", k, k + 512)])
         elif kind == "k":
             a = 4 * n[0]
             op(e, move(e, T.CC[:, a:a + 4], T.psC[:, 0:2048:512]), [("psC", 0, 2048)], [("CC", a, a + 4)])
         elif kind == "m":
-            out, in_ = T.NCC[:, 0:4], T.CC[:, 0:4]
-            op(e, act(out, in_, ACT.Copy, scale=-1.0) if e == "s" else ts(out, in_, -1.0, None, A.mult), [("CC", 0, 4)], [("NCC", 0, 4)])
+            a = 4 * n[0]
+            op("s", act(T.AB[:, a:a + 4], T.CC[:, a:a + 4], ACT.Abs, scale=0.625 * 2.0 ** -23, bias=T.PF[:, 12:13]),
+               [("CC", a, a + 4), ("PF", 12, 13)], [("AB", a, a + 4)])
+        elif kind == "M":
+            a = 4 * n[0]
+            op("v", tt(T.UP[:, a:a + 4], T.CC[:, a:a + 4], T.AB[:, a:a + 4], A.add), [("CC", a, a + 4), ("AB", a, a + 4)], [("UP", a, a + 4)])
         elif kind in "sl":
-            c = n[0]
-            if kind == "s":
-                a, b = n[1:]
-                nm, d = "UA", UW * c + (a + 640 if a >= 512 else a + (320 - 128 * c if c < 4 else 0))
-            else:
-                a, b, d = (0, 128 * c, WW * c + 128) if c < 4 else (128 * c + 128, 1024, WW * c + 384)
-                nm = "WA"
-            out, w = T[nm][:, d:d + b - a], [(nm, d, d + b - a)]
+            c, a, b = n
+            d, j = UW * c + a + 256 * (a // 512), a + (1024 if e == "s" else 0)
+            out, in_ = T.UA[:, d:d + b - a], T.psR[:, j:j + b - a]
+            mine = "UP" if kind == "l" and e == "s" else "CC"
             if e == "s":
-                kw = {"bias": T.NCC[:, c:c + 1]} if c < 4 else {"bias": T.CC[:, c:c + 1], "scale": -1.0}
-                op("s", act(out, T.psR[:, 1024 + a:1024 + b], ACT.Sign, **kw),
-                   [("psR", 1024 + a, 1024 + b), ("NCC" if c < 4 else "CC", c, c + 1)], w)
+                call = act(out, in_, ACT.Sign, bias=T[mine][:, c:c + 1], scale=-1.0)
             else:
-                o = {"s": (A.is_gt, A.is_lt), "l": (A.is_ge, A.is_le)}[kind][c // 4]
-                op("v", ts(out, T.psR[:, a:b], T.CC[:, c:c + 1], None, o), [("psR", a, b), ("CC", c, c + 1)], w)
+                call = ts(out, in_, T.CC[:, c:c + 1], None, A.is_lt if kind == "s" else A.is_le)
+            op(e, call, [("psR", j, j + b - a), (mine, c, c + 1)], [("UA", d, d + b - a)])
+        elif kind == "D":
+            c = n[0]
+            out, s1, s2 = T.CM[:, 128 * c:128 * c + 128], T.AB[:, c:c + 1], T.CC[:, c:c + 1]
+            op(e, act(out, T.LT[:], ACT.Identity, scale=s1, bias=s2) if e == "s" else ts(out, T.LT[:], s1, s2, A.mult, A.add),
+               [("LT", 0, 128), ("AB", c, c + 1), ("CC", c, c + 1)], [("CM", 128 * c, 128 * c + 128)])
         elif kind == "e":
-            c = n[0]
-            s, d = (1, WW * c) if c < 4 else (-1, WW * c + 256)
-            cb = T.WA[:, d:d + 128]
-            op("v", ts(cb, T.psR[:, 128 * c:128 * c + 128], T.CC[:, c:c + 1], None, A.is_equal),
-               [("psR", 128 * c, 128 * c + 128), ("CC", c, c + 1)], [("WA", d, d + 128)])
-            op("g", lambda: g.affine_select(cb, cb, [[-s, 128]], A.is_gt, 0.0, 0, s), [("WA", d, d + 128)], [("WA", d, d + 128)])
-        elif kind in "vab":
-            c = n[0]
-            u, w = UW * c, WW * c
-            if c < 4:
-                src, a, h, dst, end = {"v": ("WA", w, 64 + 64 * c, "UA", u + 320), "a": ("UA", u + 319, 257 - 64 * c, "UA", u + 1152),
-                                       "b": ("UA", u + 1151, 257, "SCL", 257 * c + 257)}[kind]
-            else:
-                src, a, h, dst, end = {"a": ("UA", u, 256, "WA", w + 256), "v": ("WA", w + 255, 513 - 64 * c, "UA", u + 1152),
-                                       "b": ("UA", u + 1151, 64 * c - 191, "OU", 319 + c)}[kind]
-            op("v", scan(T[dst][:, end - h:end], T[src][:, a:a + h], T[src][:, a + h:a + 2 * h], A.add, A.add),
-               [(src, a, a + 2 * h)], [(dst, end - h, end)])
+            a = 128 * n[0]
+            d = UW * n[0] + a + 256 * (a // 512)
+            op("v", tt(T.UA[:, d:d + 128], T.psR[:, a:a + 128], T.CM[:, a:a + 128], A.is_lt), [("psR", a, a + 128), ("CM", a, a + 128)], [("UA", d, d + 128)])
+        elif kind == "a":
+            u = UW * n[0]
+            op("v", scan(T.UA[:, u + 512:u + 768], T.UA[:, u:u + 256], T.UA[:, u + 256:u + 512], A.add, A.add), [("UA", u, u + 512)], [("UA", u + 512, u + 768)])
+        elif kind == "b":
+            u = UW * n[0] + 767
+            op("v", scan(T.OU[:, n[0]:2056:8], T.UA[:, u:u + 257], T.UA[:, u + 257:u + 514], A.add, A.add), [("UA", u, u + 514)], [("OU.%d" % n[0], 0, 1)])
 
     def after(name, plan):
         kind, n = name[0], [int(x) for x in name[1:].split(".")] if name[1:2].isdigit() else []
@@ -357,8 +351,9 @@ def rank_program(g, core, T, topo):
 
         def some(k, test):
             return [x for x in every if x[0] == k and x[1:2].isdigit() and test([int(y) for y in x[1:].split(".")])]
-        if name == "low":
-            return ["b0", "b1", "b2", "b3"]
+        fixed = {"i": "u", "d": "Vb Vr", "h": "Vc", "E": "Vb", "Vb": "Va", "Vc": "Vb"}
+        if name in fixed or kind in fixed:
+            return fixed.get(name, fixed.get(kind)).split()
         if kind == "t":
             return ["w" + name[1], "h" + name[1]]
         if kind == "n":
@@ -366,19 +361,11 @@ def rank_program(g, core, T, topo):
         if kind == "x":
             return some("n", lambda m: m[0] <= 128 * n[0] < m[1]) + ["p0", "p1"]
         if kind == "y":
-            return some("n", lambda m: m[0] < 256 * n[0] + 256 and 256 * n[0] < m[1]) + ["f%d" % (2 * n[0]), "f%d" % (2 * n[0] + 1)]
+            return some("n", lambda m: m[0] < 256 * n[0] + 256 and 256 * n[0] < m[1]) + some("p", lambda m: m[1] // 2 == n[0])
         if kind == "o":
             return ["d%d" % (4 * n[0] + k) for k in range(4)]
         if kind == "p":
-            return ["o" + name[1]]
-        if kind == "f":
-            return ["p0", "p1"]
-        if kind == "i":
-            return ["u"]
-        if kind == "m":
-            return ["k0"]
-        if kind == "z":
-            return (["b4"] if n[0] < 4 else []) + (["low"] if n[1] > 4 else [])
+            return ["o" + name[1]] + ["E%d" % k for k in n[1:]]
         if kind == "g":
             return some("x", lambda m: m[0] == n[0])
         if kind == "q":
@@ -390,19 +377,21 @@ def rank_program(g, core, T, topo):
                     + [x for x in every if x in ("u", "i0")] + (["k0"] if n[0] > 3 else []))
         if kind == "k":
             return ["c%d" % (4 * n[0] + k) for k in range(4)]
-        if kind in "el":
-            return ["k%d" % (n[0] // 4), "r%d.0" % (n[0] // 4)]
-        if kind == "s":
-            return ["k1" if n[0] > 3 else "m0", "r%d.%d" % (n[1] // 512, name in plan["s"].split())]
-        if kind in "vab":
-            chain = "vab" if n[0] < 4 else "avb"
-            k = chain.index(kind)
-            mine = [chain[k - 1] + name[1]] if k else []
-            if kind == "v":
-                return mine + some("e", lambda m: m[0] == n[0]) + some("l", lambda m: m[0] == n[0])
-            if kind == "b" and 4 <= n[0] < 7:
-                mine.append("b%d" % (n[0] + 1))
-            return mine + some("s", lambda m: m[0] == n[0] and m[1] // 512 == "ab".index(kind))
+        if kind == "D":
+            return ["m%d" % (n[0] // 4)]
+        if kind == "e":
+            return ["D" + name[1], "r%d.0" % (n[0] // 4)]
+        if kind in "mM":
+            return [("k%d" if kind == "m" else "m%d") % n[0]]
+        if kind in "sl":
+            on = name in plan["s"].split()
+            return [("M%d" if kind == "l" and on else "k%d") % (n[0] // 4), "r%d.%d" % (n[1] // 512, on)]
+        if kind in "ab":
+            h = "ab".index(kind)
+            mine = some("s", lambda m: m[0] == n[0] and m[1] // 512 == h) + some("l", lambda m: m[0] == n[0] and m[1] // 512 == h)
+            return mine + (["e" + name[1]] if n[0] // 4 == h else []) + (["a" + name[1]] if h else [])
+        if kind == "z":
+            return ["b%d" % c for c in range(n[0], n[1])]
         return []
 
     def play(t, plan):
@@ -414,26 +403,23 @@ def rank_program(g, core, T, topo):
             done.add(name)
 
     for t in range(ROUNDS):
-        QH, SH, nQH, nSH = T["QH%d" % t], T["SH%d" % t], "QH%d" % t, "SH%d" % t
         play(t, LATER if t else FIRST)
         if t == 0:
             op("s", act(T.FVN[:], T.FVP[:].indirect(T.POSL[:, 0:64]), ACT.Copy),
                [("FVP.%d" % q, 0, 1024) for q in range(16)] + [("POSL", 0, 64)], [("FVN", 0, 1024)])
+        nL = "LST%d" % t
+        LST, rL = T[nL], [(nL + ".%d" % k, 0, 8) for k in range(4)]
         op("v", lambda: V.transpose(T.TT[:, 0:128], T.WIN[:, 896:1024]), [("WIN", 896, 1024)], [("TT", 0, 128)])
         op("v", lambda: V.transpose(T.TT[:, 128:288], T.WIN[:, 880:1040]), [("WIN", 880, 1040)], [("TT", 128, 288)])
         op("v", cp(T.G0[:], T.TT[:].indirect(T.GL[:, 0:1])), [("TT", 0, 288), ("GL", 0, 1)], [("G0", 0, 16)])
         op("v", tt(T.G1[0:64, :], T.G0[0:64, :], T.G0[64:128, :], A.add), [("G0", 0, 16)], [("G1", 0, 16)])
         op("v", tt(T.G2[0:64, :], T.G1[0:64, 0:8], T.G1[0:64, 8:16], A.add), [("G1", 0, 16)], [("G2", 0, 8)])
-        LST, nL = T["LST%d" % t], "LST%d" % t
         for k in range(4):
-            op("v", tt(LST[32 * k:32 * k + 32, :], T.G2[0:32, :], T.G2[32:64, :], A.add), [("G2", 0, 8)], [(nL + ".%d" % k, 0, 8)])
-        rL = [(nL + ".%d" % k, 0, 8) for k in range(4)]
+            op("v", tt(LST[32 * k:32 * k + 32, :], T.G2[0:32, :], T.G2[32:64, :], A.add), [("G2", 0, 8)], [rL[k]])
 
         send(t, T["LR%d" % t][:], LST[:], "arrL%d" % t, rL)
-        op("v", cp(T["SL%d" % t][:, 0:128].bitcast(dt.uint32), QH[:, 0:1024].bitcast(dt.uint32).indirect(LST[:, 0:8])),
-           [(nQH, 0, 1024)] + rL, [("SL%d" % t, 0, 128)])
-        op("s", act(T["SS%d" % t][:, 0:128], SH[:, 0:1024].indirect(LST[:, 0:8]), ACT.Copy),
-           [(nSH, 0, 1024)] + rL, [("SS%d" % t, 0, 128)])
+        pick_codes("SL%d" % t, "QH%d" % t, 1024, nL, rL)
+        pick_scales("s", "SS%d" % t, "SH%d" % t, 1024, nL, rL)
         send(t, T["LC%d" % t][:, 0:128].bitcast(dt.uint8), T["SL%d" % t][:, 0:128].bitcast(dt.uint8), "arrC%d" % t, [("SL%d" % t, 0, 128)])
         send(t, T["LS%d" % t][:, 0:128], T["SS%d" % t][:, 0:128], "arrS%d" % t, [("SS%d" % t, 0, 128)])
         note("a", ("arrL%d" % t, ne), [], [("LR%d" % t, 0, 8)])
@@ -444,31 +430,26 @@ def rank_program(g, core, T, topo):
         FLS, nF = T["FLS%d" % t], "FLS%d" % t
         op("s", act(T.FR[:], T.IOT[:].indirect(LST[:, 0:8]), ACT.Copy), [("IOT", 0, 1024)] + rL, [("FR", 0, 128)])
         if t + 1 < ROUNDS:
-            lay_scales(t + 1, "s")
+            pick_scales("s", "SUR%d" % (t + 1), "SU", 128, "UO%d" % (t + 1), [("UO%d" % (t + 1), 0, 8)])
         op("s", act(FLS[:], T.FR[:].indirect(T.REV[:, 0:8]), ACT.Copy), [("FR", 0, 128), ("REV", 0, 8)], [(nF, 0, 128)])
         dma("y", T.fl[t:t + 1, :], FLS[0:1, :], "dout", nout, [(nF, 0, 128)], [])
         if t == 0:
             for e in range(4):
                 k = "s" if e == 3 else "v"
                 op(k, move(k, T["XP%d" % e][:, 0:512], T.XI[:, e:2048:4]), [("XI", 0, 2048)], [("XP%d" % e, 0, 512)])
+            op("v", ts(T.MD[:], T.MD0[:], QF, None, A.is_equal), [("MD0", 0, 128)] + rP, [("MD", 0, 128)])
+            op("v", ts(T.RM[:], T.MD0[:], 0.0, None, A.is_gt), [("MD0", 0, 128)], [("RM", 0, 128)])
             op("v", cp(T.OFP[:], T.FVT[:]), [("FVT", 0, 64)], [("OFP", 0, 64)])
             for m, (a, j) in enumerate(segs):
                 op("v", ts(T.KM[:, a:a + 128 - j], T.PL0[:, j:128], T.QM[:, m:m + 1], None, A.is_gt),
                    [("PL0", 0, 128), ("QM", 0, 8)], [("KM", a, a + 128 - j)])
-            lay_codes(1)
+        if t + 1 < ROUNDS:
+            pick_codes("QUR%d" % (t + 1), "QU", 128, "UO%d" % (t + 1), [("UO%d" % (t + 1), 0, 8)])
         if t == 1:
-            lay_codes(2)
             op("v", lambda: V.quantize_mx(T.QWY[:, 0:128], T.SWY[:, 0:128], T.WYB[:, 0:512]), [("WYB", 0, 512)], [("QWY", 0, 128), ("SWY", 0, 128)])
         if t == 2:
             for e in range(4):
                 op("v", cp(T.XF[:, e:2048:4], T["XP%d" % e][:, 0:512]), [("XP%d" % e, 0, 512)], [("XF.%d" % e, 0, 4096)])
-
-        LR, nR = T["LR%d" % t], "LR%d" % t
-        op("v", tt(T.VM[:], T.FVN[:].indirect(LR[:, 0:8]), T.MD[:], A.mult), [("FVN", 0, 1024), (nR, 0, 8), ("MD", 0, 128)], [("VM", 0, 128)])
-        op("s", act(T.VRO[:], T.FVN[:].indirect(LR[:, 0:8]), ACT.Copy), [("FVN", 0, 1024), (nR, 0, 8)], [("VRO", 0, 128)])
-        op("v", scan(T.VC[:, 8:72], T.VM[:, 0:128:2], T.VM[:, 1:128:2], A.add, A.add), [("VM", 0, 128)], [("VC", 8, 72)])
-        op("v", tt(T.VW[:], T.VC[:, 15:72:8], T.VC[:, 7:64:8], A.subtract), [("VC", 0, 72)], [("VW", 0, 8)])
-        op("v", tt(T.OFG[:], T.VC[:, 15:72:8], T.VC[:, 7:64:8], A.subtract), [("VC", 0, 72)], [("OFG", 0, 8)])
     play(ROUNDS, LAST)
 
     for h in range(4):

@@ -15,17 +15,16 @@ SCRATCH = {
     "CC": ("sbuf", [128, 8], F32), "AB": ("sbuf", [128, 8], F32), "UP": ("sbuf", [128, 8], F32),
     "UA": ("sbuf", [128, 8 * UW], U16), "CM": ("sbuf", [128, 1024], F32), "LT": ("sbuf", [128, 128], BF),
     "OU": ("sbuf", [128, 2056], U16), "WIN": ("sbuf", [128, 1040], F32), "TT": ("sbuf", [128, 288], F32),
-    "GL": ("sbuf", [128, 2], U16), "G0": ("sbuf", [128, 16], F32), "G1": ("sbuf", [64, 16], F32), "G2": ("sbuf", [64, 8], F32),
+    "GL": ("sbuf", [128, 2], U16), "SG": ("sbuf", [128, 32], F32), "G0": ("sbuf", [128, 32], F32), "G1": ("sbuf", [64, 32], F32),
     "P32": ("sbuf", [128, 1], I32), "PI": ("sbuf", [128, 8], I32), "PF": ("sbuf", [128, 16], F32),
     "IV0": ("sbuf", [128, 128], F32), "IV": ("sbuf", [128, 128], F32),
     "MD0": ("sbuf", [128, 128], F32), "MD": ("sbuf", [128, 128], F32), "RM": ("sbuf", [128, 128], F32),
-    "KM": ("sbuf", [128, 768], F16), "IOT": ("sbuf", [128, 1024], F32),
+    "KM": ("sbuf", [128, 1040], F16), "IOT": ("sbuf", [128, 1024], F32),
     "RV0": ("sbuf", [128, 8], F32), "QM": ("sbuf", [128, 8], F32), "REV": ("sbuf", [128, 8], U16),
     "PL0": ("sbuf", [128, 128], BF),
-    "VRO": ("sbuf", [128, 128], F16), "VM": ("sbuf", [128, 128], F32),
-    "VC": ("sbuf", [128, 128], F32), "VE": ("sbuf", [128, 32], F32), "EQ": ("sbuf", [128, 768], F16),
-    "LOS": ("sbuf", [128, 768], F16),
-    "OFG": ("sbuf", [128, 8], U16), "OFS": ("sbuf", [128, 8], U16), "OFX": ("sbuf", [128, 32], U16),
+    "VRO": ("sbuf", [128, 128], F16), "VM": ("sbuf", [128, 128], F32), "VC": ("sbuf", [128, 128], F32),
+    "EQ": ("sbuf", [128, 1040], F16), "OS": ("sbuf", [128, 1032], U16),
+    "OFG": ("sbuf", [128, 8], U16), "OFX": ("sbuf", [128, 32], U16),
     "FR": ("sbuf", [128, 128], F32),
     "OLD": ("sbuf", [128, 512], F32), "TMP": ("sbuf", [128, 512], F32), "NV": ("sbuf", [128, 512], BF),
     "YS": ("sbuf", [128, 512], F32),
@@ -51,21 +50,21 @@ SEMAPHORES = ["cv", "cs", "ct", "cg", "dx", "dfv", "du", "dfp", "dw", "dwy", "do
 for _t in range(ROUNDS):
     SEMAPHORES += ["arrL%d" % _t, "arrC%d" % _t, "arrS%d" % _t]
 
-FIRST = {"v": "g1.0.1024 u g2.512.768 q256.512 q0.256 g3.512.1024 q512.768 q768.1024 l1.256.512 D1 M0 l0.128.512 e2 s1.0.128 "
-              "l2.384.512 e1 e0 e3 k1 a2 a1 s7.0.512 l6.896.1024 D4 a7 D7 M1 s5.512.640 s5.128.512 D6 a3 a4 e6 b2 e4 a0 b3 e7 a5 "
-              "s6.512.768 b7 a6 e5 b1 b6 b5 b0 b4 z0.8",
-         "s": "g0.0.512 g2.256.512 g3.0.512 g2.0.256 i0 g0.512.1024 g2.768.1024 k0 m0 s2.0.256 D0 D2 D3 s3.0.384 l1.512.1024 l2.512.1024 m1 "
-              "s4.0.512 l3.512.1024 s7.512.896 s5.0.128 l5.768.1024 D5 s6.0.512 l0.512.1024 l4.640.1024",
-         "t": "c3 c2 c0 c1 r0.1 r0.0 c5 r1.1 c4 c6 c7 r1.0"}
-LATER = {"v": "Va Vb d4 d5 d6 d7 d0 d1 d2 d3 o1 o0 t0 p1 t3 p0 t2 t1 x0 x3 x1 x2 g1.0.256 g2.0.256 g2.256.640 q0.256 q256.512 g1.512.896 "
-              "g0.896.1024 k0 q512.640 q640.768 q768.896 q896.1024 M0 D2 l0.128.512 e3 e2 k1 s3.0.256 s5.0.512 a2 l1.256.384 e1 s6.0.512 "
-              "D4 b2 e0 M1 a6 D7 a1 a5 s5.512.640 e7 e4 s7.512.896 a0 b1 a7 l6.896.1024 a4 e6 a3 e5 b7 b0 b3 b5 b6 b4 z0.8",
-         "s": "Vr Vc h0 h3 h2 h1 n0.128 n384.512 n128.256 n256.384 g0.0.896 g3.0.512 g1.256.512 g3.512.1024 g2.640.1024 g1.896.1024 m0 "
+FIRST = {"v": "g0.0.768 u g1.0.512 U0 q128.384 q0.128 q384.512 g1.512.896 k0 g1.896.1024 q512.768 q768.896 q896.1024 l2.384.512 D2 M0 "
+              "e3 l1.256.512 k1 e1 l0.128.256 s6.0.512 s4.0.512 s1.0.128 D7 D4 a3 M1 e0 a5 a4 D6 e2 l5.768.1024 e6 l6.896.1024 s5.512.640 "
+              "a2 a0 e5 a7 e4 a6 e7 b5 b3 a1 b0 b6 b7 b1 b2 b4 z0.8",
+         "s": "g2.0.512 g3.0.512 i0 g3.512.1024 g2.512.1024 g0.768.1024 m0 s2.0.256 D3 D1 s3.0.384 D0 l0.256.512 m1 s7.0.512 s5.0.512 D5 "
+              "s6.512.768 l1.512.1024 l3.512.1024 s7.512.896 l0.512.1024 l2.512.1024 l4.640.1024",
+         "t": "c2 c1 c0 c3 r0.1 r0.0 c5 c4 c6 c7 r1.0 r1.1"}
+LATER = {"v": "Va Vb d3 d1 d2 d4 d6 d5 d7 d0 o3 o1 o6 o5 o2 o4 o7 o0 t0 t3 x0 t2 t1 x3 x1 x2 g1.0.256 g2.0.256 g2.256.640 q0.256 q256.512 "
+              "g1.512.896 g0.896.1024 k0 q512.640 q640.768 q768.896 q896.1024 M0 D2 l0.128.512 e3 e2 k1 s3.0.256 s5.0.512 a2 l1.256.384 e1 "
+              "s6.0.512 D4 b2 e0 M1 a6 D7 a1 a5 s5.512.640 e7 e4 s7.512.896 a0 b1 a7 l6.896.1024 a4 e6 a3 e5 b7 b0 b3 b5 b6 b4 z0.8",
+         "s": "Vr Vc W0 h0 h3 h2 h1 g0.0.896 g3.0.512 g1.256.512 g3.512.1024 g2.640.1024 g1.896.1024 m0 "
               "s2.0.256 D3 s3.256.384 s1.0.128 D0 l1.384.512 D1 l2.384.512 l1.512.1024 m1 l2.512.1024 s4.0.512 l0.512.1024 l5.768.1024 "
               "s7.0.512 D6 D5 l3.512.1024 s6.512.768 l4.640.1024",
          "t": "w0 w3 w2 w1 c0 c1 c2 c3 r0.1 r0.0 c4 c5 c6 c7 r1.1 r1.0"}
-LAST = {"v": "Va Vb d4 d5 d6 d7 d0 d1 d2 d3 E3 o1 o0 p1.1 p1.3 t1 t0 p1.0 t3 p0.1 p0.0 p1.2 p0.2 p0.3 t2 y0 y1",
-        "s": "Vr Vc E1 E0 h1 E2 h0 h3 h2 n128.256 n0.128 n256.512", "t": "w1 w0 w3 w2"}
+LAST = {"v": "Va Vb d4 d1 d0 d5 d2 d7 d6 d3 o4 o0 o2 o7 o5 o6 o1 o3 t0 t1 f0 f1 f2 f3 n128.256 t2 t3 y0 y1",
+        "s": "Vr Vc W0 h0 h1 h2 h3 n0.128 n256.384 n384.512", "t": "w0 w1 w2 w3"}
 
 
 def rank_program(g, core, T, topo):
@@ -143,8 +142,10 @@ def rank_program(g, core, T, topo):
     def act(out, in_, func, **kw):
         return lambda: S.activation(out, in_, func, **kw)
 
-    def move(e, out, in_):
-        return cp(out, in_) if e == "v" else act(out, in_, ACT.Copy)
+    def move(e, out, in_, by=None):
+        if by is None:
+            return cp(out, in_) if e == "v" else act(out, in_, ACT.Copy)
+        return ts(out, in_, by, None, A.mult) if e == "v" else act(out, in_, ACT.Copy, scale=by)
 
     def mm(out, a, sa, b, sb):
         return lambda: TE.matmul_mx(out, a, sa, b, sb, True, True)
@@ -164,23 +165,24 @@ def rank_program(g, core, T, topo):
     dma("y", T.WYB[:], T.wy[:], "dwy", 1, [], [("WYB", 0, 512)])
 
     iota("P32", [[0, 1]], 0, 1, 0, 1)
-    iota("PL0", [[1, 128]], 0, 0, 0, 128)
     iota("RV0", [[16, 8]], 0, 0, 0, 8)
+    iota("PL0", [[1, 128]], 0, 0, 0, 128)
     iota("IV0", [[128, 8], [1, 16]], 0, 0, 0, 128)
     iota("MD0", [[0, 8], [1, 16]], 0, 0, 0, 128)
+    iota("SG", [[0, 8], [-2, 2], [0, 2]], 1, 0, 0, 32)
     iota("WIN", [[0, 160]], 0, 0, 880, 1040)
     iota("IOT", [[1, 1024]], 0, 0, 0, 1024)
     op("v", ms(T.PF[:, 12:13], 2.0 ** -126), [], [("PF", 12, 13)])
     for t in range(ROUNDS):
         op("v", ms(T["UO%d" % t][:], t), [], [("UO%d" % t, 0, 8)])
     for k, a in enumerate([(15, None, A.bitwise_and), (112, None, A.bitwise_and), (4, 1, A.arith_shift_right, A.bitwise_and),
-                           (1, None, A.bitwise_and), (6, None, A.bitwise_and), (8, None, A.bitwise_and)]):
+                           (2, 1, A.arith_shift_right, A.bitwise_and), (1, None, A.bitwise_and), (8, None, A.bitwise_and)]):
         op("v", ts(T.PI[:, k:k + 1], T.P32[:], *a), [("P32", 0, 1)], [("PI", k, k + 1)])
     op("v", cp(T.PF[:, 13:14], T.P32[:]), [("P32", 0, 1)], [("PF", 13, 14)])
     op("v", cp(T.PF[:, 0:6], T.PI[:, 0:6]), [("PI", 0, 6)], [("PF", 0, 6)])
     op("v", ts(T.LT[:], T.PL0[:], T.PF[:, 13:14], None, A.is_gt), [("PL0", 0, 128), ("PF", 13, 14)], [("LT", 0, 128)])
     op("v", ts(T.PF[:, 6:7], T.PF[:, 2:3], -32.0, 160.0, A.mult, A.add), [("PF", 0, 6)], [("PF", 6, 7)])
-    op("v", ts(T.PF[:, 8:9], T.PF[:, 4:5], 8.0, T.PF[:, 5:6], A.mult, A.add), [("PF", 0, 6)], [("PF", 8, 9)])
+    op("v", ts(T.PF[:, 8:9], T.PF[:, 4:5], 4.0, T.PF[:, 5:6], A.mult, A.add), [("PF", 0, 6)], [("PF", 8, 9)])
     QF, GF, Q64 = T.PF[:, 0:1], T.PF[:, 1:2], T.PF[:, 10:11]
     rP = [("PF", 0, 2)]
     op("s", act(T.UA[:, 1280:8 * UW:UW], T.PL0[:, 0:8], ACT.Copy, scale=0.0), [("PL0", 0, 128)],
@@ -190,11 +192,11 @@ def rank_program(g, core, T, topo):
     op("s", act(T.IV[:], T.IV0[:], ACT.Identity, bias=GF), [("IV0", 0, 128)] + rP, [("IV", 0, 128)])
     op("s", act(T.POSL[:], T.PL0[:, 0:64], ACT.Identity, bias=Q64), [("PL0", 0, 128), ("PF", 10, 11)], [("POSL", 0, 64)])
     op("v", ts(T.PF[:, 7:8], T.PF[:, 3:4], T.PF[:, 2:3], T.PF[:, 6:7], A.not_equal, A.mult), [("PF", 0, 7)], [("PF", 7, 8)])
-    for e in (0, 1, 2, 3):
+    op("v", ts(T.PF[:, 14:16], T.RV0[:, 0:2], T.PF[:, 8:9], 4.0, A.add, A.mult), [("RV0", 0, 8), ("PF", 8, 9)], [("PF", 14, 16)])
+    for e in (0, 2, 3, 1):
         op("v", ts(T.OFH[:, 64 * e:64 * e + 64], T.FVT[:], 4.0, float(e), A.mult, A.add), [("FVT", 0, 64)], [("OFH", 64 * e, 64 * e + 64)])
-    op("v", ts(T.GL[:, 0:1], T.PF[:, 8:9], 2.0, T.PF[:, 7:8], A.mult, A.add), [("PF", 7, 9)], [("GL", 0, 1)])
+    op("v", ts(T.GL[:], T.PF[:, 14:16], T.PF[:, 7:8], None, A.add), [("PF", 7, 8), ("PF", 14, 16)], [("GL", 0, 2)])
     op("v", ts(T.REV[:], T.QM[:], -1.0, 127.0, A.mult, A.add), [("QM", 0, 8)], [("REV", 0, 8)])
-    segs = [(128 * m, 0) if m < 4 else (256 + 64 * m, 64) for m in range(8)]
 
     def pick_codes(out, src, n, off, reads):
         op("v", cp(T[out][:, 0:128].bitcast(dt.uint32), T[src][:, 0:n].bitcast(dt.uint32).indirect(T[off][:, 0:8])),
@@ -203,10 +205,14 @@ def rank_program(g, core, T, topo):
     def pick_scales(e, out, src, n, off, reads):
         op(e, move(e, T[out][:, 0:128], T[src][:, 0:n].indirect(T[off][:, 0:8])), [(src, 0, n)] + reads, [(out, 0, 128)])
 
+    def plane(k):
+        op("v", move("v", T["XP%d" % k][:, 0:512], T.XI[:, k:2048:4], 64.0), [("XI", 0, 2048)], [("XP%d" % k, 0, 512)])
+
     partners = [T.cores[rank ^ (1 << t)] for t in range(ROUNDS)]
     common = [e for e in topo.engines(core, partners[0]) if all(e in topo.engines(core, p) for p in partners)]
     mask, ne = sum(1 << e for e in common), len(common)
     nout = ROUNDS + 12
+    rS = [("OS.%d" % m, 0, 1) for m in range(8)]
 
     def send(t, land, src, arr, reads):
         deps("g", reads, [])
@@ -232,8 +238,11 @@ def rank_program(g, core, T, topo):
                 op("v", scan(T.VC[:], T.RM[:], T.VM[:], A.mult, A.add), [("VM", 0, 128), ("RM", 0, 128)], [("VC", 0, 128)])
             else:
                 op(e, move(e, T.OFG[:], T.VC[:, 15:128:16]), [("VC", 0, 128)], [("OFG", 0, 8)])
+        elif kind == "W":
+            op(e, move(e, T.EQ[:, 128:1040:130], T.VC[:, 15:128:16]), [("VC", 0, 128)], [("EQ.W", 0, 8)])
         elif name == "u":
             op("v", lambda: V.quantize_mx(T.QU[:, 0:128], T.SU[:, 0:128], T.UB[:, 0:512]), [("UB", 0, 512)], [("QU", 0, 128), ("SU", 0, 128)])
+        elif kind == "U":
             pick_codes("QUR0", "QU", 128, "UO0", [("UO0", 0, 8)])
         elif kind == "i":
             pick_scales(e, "SUR0", "SU", 128, "UO0", [("UO0", 0, 8)])
@@ -243,46 +252,36 @@ def rank_program(g, core, T, topo):
                        T["LC%d" % (t - 1)][:, 0:128], T["LS%d" % (t - 1)][:, 0:128]),
                [("WQ", 0, 512), ("WSC", 0, 512), ("LC%d" % (t - 1), 0, 128), ("LS%d" % (t - 1), 0, 128)], [("psC", 512 * b, 512 * b + 512)])
         elif kind == "t":
-            a = 128 * n[0]
-            op("v", tt(T.TMP[:, a:a + 128], T.psC[:, 4 * a:4 * a + 128], T.OLD[:, a:a + 128], A.add),
-               [("psC", 4 * a, 4 * a + 128), ("OLD", a, a + 128)], [("TMP", a, a + 128)])
+            a, to = 128 * n[0], "NV" if t < ROUNDS else "TMP"
+            op("v", tt(T[to][:, a:a + 128], T.psC[:, 4 * a:4 * a + 128], T.OLD[:, a:a + 128], A.add),
+               [("psC", 4 * a, 4 * a + 128), ("OLD", a, a + 128)], [(to, a, a + 128)])
         elif kind == "n":
             a, b = n
-            out, in_ = T.NV[:, a:b], T.TMP[:, a:b]
-            op(e, act(out, in_, ACT.Copy, scale=1.0 / 64) if e == "s" else ts(out, in_, 1.0 / 64, None, A.mult), [("TMP", a, b)], [("NV", a, b)])
+            op(e, move(e, T.NV[:, a:b], T.TMP[:, a:b], 1.0 / 64), [("TMP", a, b)], [("NV", a, b)])
         elif kind == "h":
             a = 128 * n[0]
-            out, in_ = T.OLD[:, a:a + 128], T["XP%d" % n[0]][:, 0:512].indirect(T.OFG[:, 0:8])
-            op(e, act(out, in_, ACT.Copy, scale=32.0) if e == "s" else ts(out, in_, 32.0, None, A.mult),
+            op(e, move(e, T.OLD[:, a:a + 128], T["XP%d" % n[0]][:, 0:512].indirect(T.OFG[:, 0:8]), 0.5),
                [("XP%d" % n[0], 0, 512), ("OFG", 0, 8)], [("OLD", a, a + 128)])
         elif kind == "d":
-            a, j = segs[n[0]]
-            k = 16 * n[0] + 15
-            op("v", ts(T.EQ[:, a:a + 128 - j], T.VRO[:, j:128], T.VC[:, k:k + 1], 512.0 if t < ROUNDS else 2048.0, A.is_equal, A.mult),
-               [("VRO", 0, 128), ("VC", 0, 128)], [("EQ", a, a + 128 - j)])
+            m = n[0]
+            op("v", ts(T.EQ[:, 146 * m:130 * m + 128], T.VRO[:, 16 * m:128], T.VC[:, 16 * m + 15:16 * m + 16], 512.0, A.is_equal, A.mult),
+               [("VRO", 0, 128), ("VC", 0, 128)], [("EQ", 146 * m, 130 * m + 128)])
         elif kind == "o":
-            a, b = ((0, 512), (512, 768))[n[0]]
-            op("v", scan(T.LOS[:, a:b], T.EQ[:, a:b], T.KM[:, a:b], A.add, A.mult), [("EQ", a, b), ("KM", a, b)], [("LOS", a, b)])
-        elif kind == "E":
-            out, in_ = T.VE[:, 8 * n[0]:8 * n[0] + 8], T.VC[:, 15:128:16]
-            op(e, act(out, in_, ACT.Identity, scale=4.0, bias=T.PL0[:, n[0]:n[0] + 1]) if e == "s" else ts(out, in_, 4.0, float(n[0]), A.mult, A.add),
-               [("VC", 0, 128), ("PL0", 0, 128)], [("VE", 8 * n[0], 8 * n[0] + 8)])
-        elif kind == "p":
-            a = 4 * n[0]
-            ends, rE = (T.LOS[:, 127:512:128], T.LOS[:, 575:768:64])[n[0]], ("LOS", 512 * n[0], 512 * n[0] + 512)
-            if t < ROUNDS:
-                op("v", tt(T.OFS[:, a:a + 4], ends, T.VC[:, 16 * a + 15:16 * a + 64:16], A.add), [rE, ("VC", 0, 128)], [("OFS", a, a + 4)])
-            else:
-                a += 8 * n[1]
-                op("v", tt(T.OFX[:, a:a + 4], ends, T.VE[:, a:a + 4], A.add), [rE, ("VE", a, a + 4)], [("OFX", a, a + 4)])
+            m = n[0]
+            a, b = 146 * m, 130 * m + 129
+            op("v", scan(T.OS[:, 129 * m:1032:8], T.EQ[:, a:b], T.KM[:, a:b], A.add, A.mult),
+               [("EQ", a, b), ("EQ.W", 0, 8), ("KM", 0, 1040), ("KM.W", 0, 8)], [rS[m]])
+        elif kind == "f":
+            a = 8 * n[0]
+            op("v", ts(T.OFX[:, a:a + 8], T.OS[:, 1024:1032], 4.0, float(n[0]), A.mult, A.add), rS, [("OFX", a, a + 8)])
         elif kind == "z":
             a, b = n
             op("v", cp(T.WIN[:, 0:1024].indirect(T.OU[:, 2048 + a:2048 + b]), T.IV[:, 16 * a:16 * b]),
                [("OU.%d" % c, 0, 1) for c in range(a, b)] + [("IV", 0, 128)], [("WIN", 0, 1024)])
         elif kind == "x":
             a = 128 * n[0]
-            op("v", cp(T["XP%d" % n[0]][:, 0:1024].indirect(T.OFS[:, 0:8]), T.NV[:, a:a + 128]),
-               [("OFS", 0, 8), ("NV", a, a + 128)], [("XP%d" % n[0], 0, 1024)])
+            op("v", cp(T["XP%d" % n[0]][:, 0:1024].indirect(T.OS[:, 1024:1032]), T.NV[:, a:a + 128]),
+               rS + [("NV", a, a + 128)], [("XP%d" % n[0], 0, 1024)])
         elif kind == "y":
             a = 256 * n[0]
             op("v", cp(T.XF[:, 0:4096].indirect(T.OFX[:, 16 * n[0]:16 * n[0] + 16]), T.NV[:, a:a + 256]),
@@ -290,12 +289,12 @@ def rank_program(g, core, T, topo):
         elif kind == "g":
             el, lo, hi = n
             if t == 0:
-                win = T.XI[:, 0:2048].indirect(T.OFH[:, 64 * el + lo // 16:64 * el + hi // 16])
+                win, by = T.XI[:, 0:2048].indirect(T.OFH[:, 64 * el + lo // 16:64 * el + hi // 16]), None
                 reads = [("XI", 0, 2048), ("OFH", 64 * el, 64 * el + 64)]
             else:
-                win = T["XP%d" % el][:, 0:512].indirect(T.OFP[:, lo // 16:hi // 16])
+                win, by = T["XP%d" % el][:, 0:512].indirect(T.OFP[:, lo // 16:hi // 16]), 1.0 / 64
                 reads = [("XP%d" % el, 0, 512), ("OFP", 0, 64)]
-            op(e, move(e, T.H[:, 4 * lo + el:4 * hi:4], win), reads, [("H.%d" % el, lo, hi)])
+            op(e, move(e, T.H[:, 4 * lo + el:4 * hi:4], win, by), reads, [("H.%d" % el, lo, hi)])
         elif kind == "q":
             a, b = n
             op("v", lambda: V.quantize_mx(QH[:, a:b], SH[:, a:b], T.H[:, 4 * a:4 * b]),
@@ -351,7 +350,8 @@ def rank_program(g, core, T, topo):
 
         def some(k, test):
             return [x for x in every if x[0] == k and x[1:2].isdigit() and test([int(y) for y in x[1:].split(".")])]
-        fixed = {"i": "u", "d": "Vb Vr", "h": "Vc", "E": "Vb", "Vb": "Va", "Vc": "Vb"}
+        sums = "o0 o1 o2 o3 o4 o5 o6 o7"
+        fixed = {"i": "u", "U": "u", "d": "Vb Vr", "h": "Vc", "W": "Vb", "Vb": "Va", "Vc": "Vb", "f": sums}
         if name in fixed or kind in fixed:
             return fixed.get(name, fixed.get(kind)).split()
         if kind == "t":
@@ -359,22 +359,20 @@ def rank_program(g, core, T, topo):
         if kind == "n":
             return some("t", lambda m: n[0] <= 128 * m[0] < n[1])
         if kind == "x":
-            return some("n", lambda m: m[0] <= 128 * n[0] < m[1]) + ["p0", "p1"]
+            return ["t" + name[1]] + sums.split()
         if kind == "y":
-            return some("n", lambda m: m[0] < 256 * n[0] + 256 and 256 * n[0] < m[1]) + some("p", lambda m: m[1] // 2 == n[0])
+            return some("n", lambda m: m[0] < 256 * n[0] + 256 and 256 * n[0] < m[1]) + some("f", lambda m: m[0] // 2 == n[0])
         if kind == "o":
-            return ["d%d" % (4 * n[0] + k) for k in range(4)]
-        if kind == "p":
-            return ["o" + name[1]] + ["E%d" % k for k in n[1:]]
+            return ["d" + name[1], "W0"]
         if kind == "g":
             return some("x", lambda m: m[0] == n[0])
         if kind == "q":
             return some("g", lambda m: m[1] < n[1] and n[0] < m[2])
         if kind == "r":
-            return some("q", lambda m: m[0] // 512 == n[0]) + [x for x in every if x in ("u", "i0")]
+            return some("q", lambda m: m[0] // 512 == n[0]) + [x for x in every if x in ("U0", "i0")]
         if kind == "c":
             return (some("q", lambda m: m[0] < 128 * n[0] + 128 and 128 * n[0] < m[1]) + some("t", lambda m: True)
-                    + [x for x in every if x in ("u", "i0")] + (["k0"] if n[0] > 3 else []))
+                    + [x for x in every if x in ("U0", "i0")] + (["k0"] if n[0] > 3 else []))
         if kind == "k":
             return ["c%d" % (4 * n[0] + k) for k in range(4)]
         if kind == "D":
@@ -407,15 +405,19 @@ def rank_program(g, core, T, topo):
         if t == 0:
             op("s", act(T.FVN[:], T.FVP[:].indirect(T.POSL[:, 0:64]), ACT.Copy),
                [("FVP.%d" % q, 0, 1024) for q in range(16)] + [("POSL", 0, 64)], [("FVN", 0, 1024)])
+            plane(0)
         nL = "LST%d" % t
         LST, rL = T[nL], [(nL + ".%d" % k, 0, 8) for k in range(4)]
         op("v", lambda: V.transpose(T.TT[:, 0:128], T.WIN[:, 896:1024]), [("WIN", 896, 1024)], [("TT", 0, 128)])
         op("v", lambda: V.transpose(T.TT[:, 128:288], T.WIN[:, 880:1040]), [("WIN", 880, 1040)], [("TT", 128, 288)])
-        op("v", cp(T.G0[:], T.TT[:].indirect(T.GL[:, 0:1])), [("TT", 0, 288), ("GL", 0, 1)], [("G0", 0, 16)])
-        op("v", tt(T.G1[0:64, :], T.G0[0:64, :], T.G0[64:128, :], A.add), [("G0", 0, 16)], [("G1", 0, 16)])
-        op("v", tt(T.G2[0:64, :], T.G1[0:64, 0:8], T.G1[0:64, 8:16], A.add), [("G1", 0, 16)], [("G2", 0, 8)])
+        if t == 0:
+            plane(1)
+        op("v", tt(T.G0[:], T.TT[:].indirect(T.GL[:, 0:2]), T.SG[:], A.mult), [("TT", 0, 288), ("GL", 0, 2), ("SG", 0, 32)], [("G0", 0, 32)])
+        if t == 0:
+            plane(2)
+        op("v", scan(T.G1[0:64, :], T.G0[0:64, :], T.G0[64:128, :], A.add, A.add), [("G0", 0, 32)], [("G1", 0, 32)])
         for k in range(4):
-            op("v", tt(LST[32 * k:32 * k + 32, :], T.G2[0:32, :], T.G2[32:64, :], A.add), [("G2", 0, 8)], [rL[k]])
+            op("v", tt(LST[32 * k:32 * k + 32, :], T.G1[0:32, 1:32:4], T.G1[32:64, 1:32:4], A.add), [("G1", 0, 32)], [rL[k]])
 
         send(t, T["LR%d" % t][:], LST[:], "arrL%d" % t, rL)
         pick_codes("SL%d" % t, "QH%d" % t, 1024, nL, rL)
@@ -434,22 +436,21 @@ def rank_program(g, core, T, topo):
         op("s", act(FLS[:], T.FR[:].indirect(T.REV[:, 0:8]), ACT.Copy), [("FR", 0, 128), ("REV", 0, 8)], [(nF, 0, 128)])
         dma("y", T.fl[t:t + 1, :], FLS[0:1, :], "dout", nout, [(nF, 0, 128)], [])
         if t == 0:
-            for e in range(4):
-                k = "s" if e == 3 else "v"
-                op(k, move(k, T["XP%d" % e][:, 0:512], T.XI[:, e:2048:4]), [("XI", 0, 2048)], [("XP%d" % e, 0, 512)])
+            plane(3)
             op("v", ts(T.MD[:], T.MD0[:], QF, None, A.is_equal), [("MD0", 0, 128)] + rP, [("MD", 0, 128)])
             op("v", ts(T.RM[:], T.MD0[:], 0.0, None, A.is_gt), [("MD0", 0, 128)], [("RM", 0, 128)])
             op("v", cp(T.OFP[:], T.FVT[:]), [("FVT", 0, 64)], [("OFP", 0, 64)])
-            for m, (a, j) in enumerate(segs):
-                op("v", ts(T.KM[:, a:a + 128 - j], T.PL0[:, j:128], T.QM[:, m:m + 1], None, A.is_gt),
-                   [("PL0", 0, 128), ("QM", 0, 8)], [("KM", a, a + 128 - j)])
+            op("v", ts(T.KM[:, 128:1040:130], T.PL0[:, 0:8], 0.0, 1.0, A.mult, A.add), [("PL0", 0, 128)], [("KM.W", 0, 8)])
+            for m in range(8):
+                op("v", ts(T.KM[:, 146 * m:130 * m + 128], T.PL0[:, 16 * m:128], T.QM[:, m:m + 1], None, A.is_gt),
+                   [("PL0", 0, 128), ("QM", 0, 8)], [("KM", 146 * m, 130 * m + 128)])
         if t + 1 < ROUNDS:
             pick_codes("QUR%d" % (t + 1), "QU", 128, "UO%d" % (t + 1), [("UO%d" % (t + 1), 0, 8)])
         if t == 1:
             op("v", lambda: V.quantize_mx(T.QWY[:, 0:128], T.SWY[:, 0:128], T.WYB[:, 0:512]), [("WYB", 0, 512)], [("QWY", 0, 128), ("SWY", 0, 128)])
         if t == 2:
             for e in range(4):
-                op("v", cp(T.XF[:, e:2048:4], T["XP%d" % e][:, 0:512]), [("XP%d" % e, 0, 512)], [("XF.%d" % e, 0, 4096)])
+                op("v", move("v", T.XF[:, e:2048:4], T["XP%d" % e][:, 0:512], 1.0 / 64), [("XP%d" % e, 0, 512)], [("XF.%d" % e, 0, 4096)])
     play(ROUNDS, LAST)
 
     for h in range(4):

from concourse.mybir import dt, AluOpType, ActivationFunctionType

ROUNDS = 3
UW = 1282

F32, BF, F16, I32, U16, CODE, U8 = "float32", "bfloat16", "float16", "int32", "uint16", "float8_e4m3fn_x4", "uint8"
SCRATCH = {
    "XI": ("sbuf", [128, 2048], BF), "XF": ("sbuf", [128, 4096], BF), "H": ("sbuf", [128, 4096], BF),
    "WQ": ("sbuf", [128, 512], CODE), "WSC": ("sbuf", [128, 512], U8),
    "UB": ("sbuf", [128, 512], BF), "QU": ("sbuf", [128, 128], CODE), "SU": ("sbuf", [128, 128], U8),
    "WYB": ("sbuf", [128, 512], BF), "QWY": ("sbuf", [128, 128], CODE), "SWY": ("sbuf", [128, 128], U8),
    "QX": ("sbuf", [128, 512], CODE), "SX": ("sbuf", [128, 512], U8),
    "FVT": ("sbuf", [128, 64], I32), "OFH": ("sbuf", [128, 256], U16), "OFP": ("sbuf", [128, 64], U16),
    "FVP": ("sbuf", [128, 1024], I32), "POSL": ("sbuf", [128, 64], U16), "FVN": ("sbuf", [128, 1024], F32),
    "CC": ("sbuf", [128, 8], F32), "AB": ("sbuf", [128, 8], F32), "UP": ("sbuf", [128, 8], F32),
    "UA": ("sbuf", [128, 8 * UW], U16), "CM": ("sbuf", [128, 1024], F32), "LT": ("sbuf", [128, 128], BF),
    "OU": ("sbuf", [128, 2056], U16), "WIN": ("sbuf", [128, 1040], F32), "TT": ("sbuf", [128, 288], F32),
    "GL": ("sbuf", [128, 2], U16), "SG": ("sbuf", [128, 32], F32), "G0": ("sbuf", [128, 32], F32), "G1": ("sbuf", [64, 32], F32),
    "P32": ("sbuf", [128, 1], I32), "PI": ("sbuf", [128, 8], I32), "PF": ("sbuf", [128, 16], F32),
    "IV0": ("sbuf", [128, 128], F32), "IV": ("sbuf", [128, 128], F32),
    "MD0": ("sbuf", [128, 128], F32), "MD": ("sbuf", [128, 128], F32), "RM": ("sbuf", [128, 128], F32),
    "KM": ("sbuf", [128, 1040], F16), "IOT": ("sbuf", [128, 1024], F32),
    "RV0": ("sbuf", [128, 8], F32), "QM": ("sbuf", [128, 8], F32), "REV": ("sbuf", [128, 8], U16),
    "PL0": ("sbuf", [128, 128], BF),
    "VRO": ("sbuf", [128, 128], F16), "VM": ("sbuf", [128, 128], F32), "VC": ("sbuf", [128, 128], F32),
    "EQ": ("sbuf", [128, 1040], F16), "OS": ("sbuf", [128, 1032], U16),
    "OFG": ("sbuf", [128, 8], U16), "OFX": ("sbuf", [128, 32], U16),
    "FR": ("sbuf", [128, 128], F32),
    "OLD": ("sbuf", [128, 512], F32), "TMP": ("sbuf", [128, 512], F32), "NV": ("sbuf", [128, 512], BF),
    "YS": ("sbuf", [128, 512], F32),
    "psR": ("psum", [128, 2048], F32), "psC": ("psum", [128, 2048], F32),
}
for _e in range(4):
    SCRATCH["XP%d" % _e] = ("sbuf", [128, 1024], BF)
for _t in range(ROUNDS):
    SCRATCH["UO%d" % _t] = ("sbuf", [128, 8], U16)
    SCRATCH["QUR%d" % _t] = ("sbuf", [128, 128], CODE)
    SCRATCH["SUR%d" % _t] = ("sbuf", [128, 128], U8)
    SCRATCH["QH%d" % _t] = ("sbuf", [128, 1024], CODE)
    SCRATCH["SH%d" % _t] = ("sbuf", [128, 1024], U8)
    SCRATCH["SL%d" % _t] = ("sbuf", [128, 128], CODE)
    SCRATCH["SS%d" % _t] = ("sbuf", [128, 128], U8)
    SCRATCH["LC%d" % _t] = ("sbuf", [128, 128], CODE)
    SCRATCH["LS%d" % _t] = ("sbuf", [128, 128], U8)
    SCRATCH["LR%d" % _t] = ("sbuf", [128, 8], U16)
    SCRATCH["LST%d" % _t] = ("sbuf", [128, 8], U16)
    SCRATCH["FLS%d" % _t] = ("sbuf", [128, 128], F32)

SEMAPHORES = ["cv", "cs", "ct", "cg", "dx", "dfv", "du", "dfp", "dw", "dwy", "dout", "sent"]
for _t in range(ROUNDS):
    SEMAPHORES += ["arrL%d" % _t, "arrC%d" % _t, "arrS%d" % _t]

FIRST = {"v": "g0.0.768 u g1.0.512 U0 q128.384 q0.128 q384.512 g1.512.896 k0 g1.896.1024 q512.768 q768.896 q896.1024 l2.384.512 D2 M0 "
              "e3 l1.256.512 k1 e1 l0.128.256 s6.0.512 s4.0.512 s1.0.128 D7 D4 a3 M1 e0 a5 a4 D6 e2 l5.768.1024 e6 l6.896.1024 s5.512.640 "
              "a2 a0 e5 a7 e4 a6 e7 b5 b3 a1 b0 b6 b7 b1 b2 b4 z0.8",
         "s": "g2.0.512 g3.0.512 i0 g3.512.1024 g2.512.1024 g0.768.1024 m0 s2.0.256 D3 D1 s3.0.384 D0 l0.256.512 m1 s7.0.512 s5.0.512 D5 "
              "s6.512.768 l1.512.1024 l3.512.1024 s7.512.896 l0.512.1024 l2.512.1024 l4.640.1024",
         "t": "c2 c1 c0 c3 r0.1 r0.0 c5 c4 c6 c7 r1.0 r1.1"}
LATER = {"v": "Va Vb d3 d1 d2 d4 d6 d5 d7 d0 o3 o1 o6 o5 o2 o4 o7 o0 t0 t3 x0 t2 t1 x3 x1 x2 g1.0.256 g2.0.256 g2.256.640 q0.256 q256.512 "
              "g1.512.896 g0.896.1024 k0 q512.640 q640.768 q768.896 q896.1024 M0 D2 l0.128.512 e3 e2 k1 s3.0.256 s5.0.512 a2 l1.256.384 e1 "
              "s6.0.512 D4 b2 e0 M1 a6 D7 a1 a5 s5.512.640 e7 e4 s7.512.896 a0 b1 a7 l6.896.1024 a4 e6 a3 e5 b7 b0 b3 b5 b6 b4 z0.8",
         "s": "Vr Vc W0 h0 h3 h2 h1 g0.0.896 g3.0.512 g1.256.512 g3.512.1024 g2.640.1024 g1.896.1024 m0 "
              "s2.0.256 D3 s3.256.384 s1.0.128 D0 l1.384.512 D1 l2.384.512 l1.512.1024 m1 l2.512.1024 s4.0.512 l0.512.1024 l5.768.1024 "
              "s7.0.512 D6 D5 l3.512.1024 s6.512.768 l4.640.1024",
         "t": "w0 w3 w2 w1 c0 c1 c2 c3 r0.1 r0.0 c4 c5 c6 c7 r1.1 r1.0"}
LAST = {"v": "Va Vb d4 d1 d0 d5 d2 d7 d6 d3 o4 o0 o2 o7 o5 o6 o1 o3 t0 t1 f0 f1 f2 f3 n128.256 t2 t3 y0 y1",
        "s": "Vr Vc W0 h0 h1 h2 h3 n0.128 n256.384 n384.512", "t": "w0 w1 w2 w3"}


def rank_program(g, core, T, topo):
    rank = T.rank_of(core)
    if rank is None:
        return
    A, ACT = AluOpType, ActivationFunctionType
    V, S, TE, SY = g.vector, g.scalar, g.tensor, g.sync
    queue = {"v": V, "s": S, "t": TE, "g": g, "y": SY}
    own = {"v": "cv", "s": "cs", "t": "ct", "g": "cg"}

    count = {k: 0 for k in own}
    known = {k: {} for k in queue}
    most, total = {}, {}
    wr, rd = {}, {}

    def need(e, tok):
        sem, n = tok
        if known[e].get(sem, 0) < n:
            queue[e].wait_ge(T.sem[sem], n)
            known[e][sem] = n
            most[sem] = max(most.get(sem, 0), n)

    def deps(e, reads, writes):
        want = {}
        for n, a, b in reads:
            for (x, y, tok, w) in wr.get(n, []):
                if x < b and a < y:
                    want[tok[0]] = max(want.get(tok[0], 0), tok[1])
        for n, a, b in writes:
            for (x, y, tok, w) in wr.get(n, []):
                if x < b and a < y:
                    want[tok[0]] = max(want.get(tok[0], 0), tok[1])
            for (x, y, tok, w) in rd.get(n, []):
                if x < b and a < y and w != e:
                    want[tok[0]] = max(want.get(tok[0], 0), tok[1])
        for sem in sorted(want):
            need(e, (sem, want[sem]))

    def note(e, tok, reads, writes):
        for n, a, b in writes:
            wr[n] = [r for r in wr.get(n, []) if not (a <= r[0] and r[1] <= b)] + [(a, b, tok, e)]
            rd[n] = [r for r in rd.get(n, []) if not (a <= r[0] and r[1] <= b)]
        for n, a, b in reads:
            rd[n] = [r for r in rd.get(n, []) if not (r[3] == e and a <= r[0] and r[1] <= b)] + [(a, b, tok, e)]

    def op(e, call, reads, writes):
        deps(e, reads, writes)
        count[e] += 1
        total[own[e]] = count[e]
        call().then_inc(T.sem[own[e]], 1)
        note(e, (own[e], count[e]), reads, writes)

    def dma(e, out, in_, sem, n, reads, writes):
        deps(e, reads, writes)
        total[sem] = total.get(sem, 0) + 16
        queue[e].dma_start(out, in_).then_inc(T.sem[sem], 16)
        note("d" + sem, (sem, 16 * n), reads, writes)

    def ts(out, in0, s1, s2, *ops):
        return lambda: V.tensor_scalar(out, in0, s1, s2, *ops)

    def tt(out, a, b, o):
        return lambda: V.tensor_tensor(out, a, b, o)

    def scan(out, a, b, o0, o1):
        return lambda: V.tensor_tensor_scan(out, a, b, 0.0, o0, o1)

    def cp(out, in_):
        return lambda: V.tensor_copy(out, in_)

    def ms(ap, c):
        return lambda: V.memset(ap, c)

    def act(out, in_, func, **kw):
        return lambda: S.activation(out, in_, func, **kw)

    def move(e, out, in_, by=None):
        if by is None:
            return cp(out, in_) if e == "v" else act(out, in_, ACT.Copy)
        return ts(out, in_, by, None, A.mult) if e == "v" else act(out, in_, ACT.Copy, scale=by)

    def mm(out, a, sa, b, sb):
        return lambda: TE.matmul_mx(out, a, sa, b, sb, True, True)

    def iota(name, pattern, base, cm, a, b):
        kw = {} if SCRATCH[name][2] == I32 else {"allow_small_or_imprecise_dtypes": True}
        op("g", lambda: g.iota(T[name][:, a:b], pattern, base, cm, **kw), [], [(name, a, b)])

    dma("y", T.XI[:], T.x[:], "dx", 1, [], [("XI", 0, 2048)])
    dma("s", T.FVT[:], T.fv[:], "dfv", 1, [], [("FVT", 0, 64)])
    dma("y", T.UB[:], T.u[:], "du", 1, [], [("UB", 0, 512)])
    need("y", ("dx", 16))
    for q in range(16):
        dma("y", T.FVP[q:128:16, :], T.fv[:], "dfp", 16, [], [("FVP.%d" % q, 0, 1024)])
    dma("y", T.WQ[:, 0:512].bitcast(dt.uint8), T.wc[:], "dw", 2, [], [("WQ", 0, 512)])
    dma("y", T.WSC[:, 0:512], T.ws[:], "dw", 2, [], [("WSC", 0, 512)])
    dma("y", T.WYB[:], T.wy[:], "dwy", 1, [], [("WYB", 0, 512)])

    iota("P32", [[0, 1]], 0, 1, 0, 1)
    iota("RV0", [[16, 8]], 0, 0, 0, 8)
    iota("PL0", [[1, 128]], 0, 0, 0, 128)
    iota("IV0", [[128, 8], [1, 16]], 0, 0, 0, 128)
    iota("MD0", [[0, 8], [1, 16]], 0, 0, 0, 128)
    iota("SG", [[0, 8], [-2, 2], [0, 2]], 1, 0, 0, 32)
    iota("WIN", [[0, 160]], 0, 0, 880, 1040)
    iota("IOT", [[1, 1024]], 0, 0, 0, 1024)
    op("v", ms(T.PF[:, 12:13], 2.0 ** -126), [], [("PF", 12, 13)])
    for t in range(ROUNDS):
        op("v", ms(T["UO%d" % t][:], t), [], [("UO%d" % t, 0, 8)])
    for k, a in enumerate([(15, None, A.bitwise_and), (112, None, A.bitwise_and), (4, 1, A.arith_shift_right, A.bitwise_and),
                           (2, 1, A.arith_shift_right, A.bitwise_and), (1, None, A.bitwise_and), (8, None, A.bitwise_and)]):
        op("v", ts(T.PI[:, k:k + 1], T.P32[:], *a), [("P32", 0, 1)], [("PI", k, k + 1)])
    op("v", cp(T.PF[:, 13:14], T.P32[:]), [("P32", 0, 1)], [("PF", 13, 14)])
    op("v", cp(T.PF[:, 0:6], T.PI[:, 0:6]), [("PI", 0, 6)], [("PF", 0, 6)])
    op("v", ts(T.LT[:], T.PL0[:], T.PF[:, 13:14], None, A.is_gt), [("PL0", 0, 128), ("PF", 13, 14)], [("LT", 0, 128)])
    op("v", ts(T.PF[:, 6:7], T.PF[:, 2:3], -32.0, 160.0, A.mult, A.add), [("PF", 0, 6)], [("PF", 6, 7)])
    op("v", ts(T.PF[:, 8:9], T.PF[:, 4:5], 4.0, T.PF[:, 5:6], A.mult, A.add), [("PF", 0, 6)], [("PF", 8, 9)])
    QF, GF, Q64 = T.PF[:, 0:1], T.PF[:, 1:2], T.PF[:, 10:11]
    rP = [("PF", 0, 2)]
    op("s", act(T.UA[:, 1280:8 * UW:UW], T.PL0[:, 0:8], ACT.Copy, scale=0.0), [("PL0", 0, 128)],
       [("UA", 1280 + UW * c, 1281 + UW * c) for c in range(8)])
    op("s", act(Q64, QF, ACT.Copy, scale=64.0), rP, [("PF", 10, 11)])
    op("s", act(T.QM[:], T.RV0[:], ACT.Identity, bias=QF), [("RV0", 0, 8)] + rP, [("QM", 0, 8)])
    op("s", act(T.IV[:], T.IV0[:], ACT.Identity, bias=GF), [("IV0", 0, 128)] + rP, [("IV", 0, 128)])
    op("s", act(T.POSL[:], T.PL0[:, 0:64], ACT.Identity, bias=Q64), [("PL0", 0, 128), ("PF", 10, 11)], [("POSL", 0, 64)])
    op("v", ts(T.PF[:, 7:8], T.PF[:, 3:4], T.PF[:, 2:3], T.PF[:, 6:7], A.not_equal, A.mult), [("PF", 0, 7)], [("PF", 7, 8)])
    op("v", ts(T.PF[:, 14:16], T.RV0[:, 0:2], T.PF[:, 8:9], 4.0, A.add, A.mult), [("RV0", 0, 8), ("PF", 8, 9)], [("PF", 14, 16)])
    for e in (0, 2, 3, 1):
        op("v", ts(T.OFH[:, 64 * e:64 * e + 64], T.FVT[:], 4.0, float(e), A.mult, A.add), [("FVT", 0, 64)], [("OFH", 64 * e, 64 * e + 64)])
    op("v", ts(T.GL[:], T.PF[:, 14:16], T.PF[:, 7:8], None, A.add), [("PF", 7, 8), ("PF", 14, 16)], [("GL", 0, 2)])
    op("v", ts(T.REV[:], T.QM[:], -1.0, 127.0, A.mult, A.add), [("QM", 0, 8)], [("REV", 0, 8)])

    def pick_codes(out, src, n, off, reads):
        op("v", cp(T[out][:, 0:128].bitcast(dt.uint32), T[src][:, 0:n].bitcast(dt.uint32).indirect(T[off][:, 0:8])),
           [(src, 0, n)] + reads, [(out, 0, 128)])

    def pick_scales(e, out, src, n, off, reads):
        op(e, move(e, T[out][:, 0:128], T[src][:, 0:n].indirect(T[off][:, 0:8])), [(src, 0, n)] + reads, [(out, 0, 128)])

    def plane(k):
        op("v", move("v", T["XP%d" % k][:, 0:512], T.XI[:, k:2048:4], 64.0), [("XI", 0, 2048)], [("XP%d" % k, 0, 512)])

    partners = [T.cores[rank ^ (1 << t)] for t in range(ROUNDS)]
    common = [e for e in topo.engines(core, partners[0]) if all(e in topo.engines(core, p) for p in partners)]
    mask, ne = sum(1 << e for e in common), len(common)
    nout = ROUNDS + 12
    rS = [("OS.%d" % m, 0, 1) for m in range(8)]

    def send(t, land, src, arr, reads):
        deps("g", reads, [])
        rid, pid = topo.addr(partners[t])[:2]
        total["sent"] = total.get("sent", 0) + ne
        g.remote_dma(land, src, T.sem[arr], T.sem.sent, pid, rid, mask)
        total[arr] = ne

    def step(t, e, name):
        kind, n = name[0], [int(x) for x in name[1:].split(".")] if name[1:2].isdigit() else []
        if t < ROUNDS:
            QH, SH, QUR, SUR = T["QH%d" % t], T["SH%d" % t], T["QUR%d" % t][:, 0:128], T["SUR%d" % t][:, 0:128]
            nQH, nSH = "QH%d" % t, "SH%d" % t
            ru = [("QUR%d" % t, 0, 128), ("SUR%d" % t, 0, 128)]
        if kind == "V":
            nR = "LR%d" % (t - 1)
            hit, rH = T.FVN[:].indirect(T[nR][:, 0:8]), [("FVN", 0, 1024), (nR, 0, 8)]
            if name == "Va":
                op("v", tt(T.VM[:], hit, T.MD[:], A.mult), rH + [("MD", 0, 128)], [("VM", 0, 128)])
            elif name == "Vr":
                op(e, move(e, T.VRO[:], hit), rH, [("VRO", 0, 128)])
            elif name == "Vb":
                op("v", scan(T.VC[:], T.RM[:], T.VM[:], A.mult, A.add), [("VM", 0, 128), ("RM", 0, 128)], [("VC", 0, 128)])
            else:
                op(e, move(e, T.OFG[:], T.VC[:, 15:128:16]), [("VC", 0, 128)], [("OFG", 0, 8)])
        elif kind == "W":
            op(e, move(e, T.EQ[:, 128:1040:130], T.VC[:, 15:128:16]), [("VC", 0, 128)], [("EQ.W", 0, 8)])
        elif name == "u":
            op("v", lambda: V.quantize_mx(T.QU[:, 0:128], T.SU[:, 0:128], T.UB[:, 0:512]), [("UB", 0, 512)], [("QU", 0, 128), ("SU", 0, 128)])
        elif kind == "U":
            pick_codes("QUR0", "QU", 128, "UO0", [("UO0", 0, 8)])
        elif kind == "i":
            pick_scales(e, "SUR0", "SU", 128, "UO0", [("UO0", 0, 8)])
        elif kind == "w":
            b = n[0]
            op("t", mm(T.psC[:, 512 * b:512 * b + 128], T.WQ[:, 128 * b:128 * b + 128], T.WSC[:, 128 * b:128 * b + 128],
                       T["LC%d" % (t - 1)][:, 0:128], T["LS%d" % (t - 1)][:, 0:128]),
               [("WQ", 0, 512), ("WSC", 0, 512), ("LC%d" % (t - 1), 0, 128), ("LS%d" % (t - 1), 0, 128)], [("psC", 512 * b, 512 * b + 512)])
        elif kind == "t":
            a, to = 128 * n[0], "NV" if t < ROUNDS else "TMP"
            op("v", tt(T[to][:, a:a + 128], T.psC[:, 4 * a:4 * a + 128], T.OLD[:, a:a + 128], A.add),
               [("psC", 4 * a, 4 * a + 128), ("OLD", a, a + 128)], [(to, a, a + 128)])
        elif kind == "n":
            a, b = n
            op(e, move(e, T.NV[:, a:b], T.TMP[:, a:b], 1.0 / 64), [("TMP", a, b)], [("NV", a, b)])
        elif kind == "h":
            a = 128 * n[0]
            op(e, move(e, T.OLD[:, a:a + 128], T["XP%d" % n[0]][:, 0:512].indirect(T.OFG[:, 0:8]), 0.5),
               [("XP%d" % n[0], 0, 512), ("OFG", 0, 8)], [("OLD", a, a + 128)])
        elif kind == "d":
            m = n[0]
            op("v", ts(T.EQ[:, 146 * m:130 * m + 128], T.VRO[:, 16 * m:128], T.VC[:, 16 * m + 15:16 * m + 16], 512.0, A.is_equal, A.mult),
               [("VRO", 0, 128), ("VC", 0, 128)], [("EQ", 146 * m, 130 * m + 128)])
        elif kind == "o":
            m = n[0]
            a, b = 146 * m, 130 * m + 129
            op("v", scan(T.OS[:, 129 * m:1032:8], T.EQ[:, a:b], T.KM[:, a:b], A.add, A.mult),
               [("EQ", a, b), ("EQ.W", 0, 8), ("KM", 0, 1040), ("KM.W", 0, 8)], [rS[m]])
        elif kind == "f":
            a = 8 * n[0]
            op("v", ts(T.OFX[:, a:a + 8], T.OS[:, 1024:1032], 4.0, float(n[0]), A.mult, A.add), rS, [("OFX", a, a + 8)])
        elif kind == "z":
            a, b = n
            op("v", cp(T.WIN[:, 0:1024].indirect(T.OU[:, 2048 + a:2048 + b]), T.IV[:, 16 * a:16 * b]),
               [("OU.%d" % c, 0, 1) for c in range(a, b)] + [("IV", 0, 128)], [("WIN", 0, 1024)])
        elif kind == "x":
            a = 128 * n[0]
            op("v", cp(T["XP%d" % n[0]][:, 0:1024].indirect(T.OS[:, 1024:1032]), T.NV[:, a:a + 128]),
               rS + [("NV", a, a + 128)], [("XP%d" % n[0], 0, 1024)])
        elif kind == "y":
            a = 256 * n[0]
            op("v", cp(T.XF[:, 0:4096].indirect(T.OFX[:, 16 * n[0]:16 * n[0] + 16]), T.NV[:, a:a + 256]),
               [("OFX", 16 * n[0], 16 * n[0] + 16), ("NV", a, a + 256)], [("XF.%d" % k, 0, 4096) for k in range(4)])
        elif kind == "g":
            el, lo, hi = n
            if t == 0:
                win, by = T.XI[:, 0:2048].indirect(T.OFH[:, 64 * el + lo // 16:64 * el + hi // 16]), None
                reads = [("XI", 0, 2048), ("OFH", 64 * el, 64 * el + 64)]
            else:
                win, by = T["XP%d" % el][:, 0:512].indirect(T.OFP[:, lo // 16:hi // 16]), 1.0 / 64
                reads = [("XP%d" % el, 0, 512), ("OFP", 0, 64)]
            op(e, move(e, T.H[:, 4 * lo + el:4 * hi:4], win, by), reads, [("H.%d" % el, lo, hi)])
        elif kind == "q":
            a, b = n
            op("v", lambda: V.quantize_mx(QH[:, a:b], SH[:, a:b], T.H[:, 4 * a:4 * b]),
               [("H.%d" % k, a, b) for k in range(4)], [(nQH, a, b), (nSH, a, b)])
        elif kind == "r":
            a = 512 * n[0]
            b = 1024 * n[1] + a
            op("t", mm(T.psR[:, b:b + 512], QUR, SUR, QH[:, a:a + 512], SH[:, a:a + 512]),
               ru + [(nQH, a, a + 512), (nSH, a, a + 512)], [("psR", b, b + 512)])
        elif kind == "c":
            a, k = 128 * n[0], 512 * (n[0] % 4)
            op("t", mm(T.psC[:, k:k + 128], QH[:, a:a + 128], SH[:, a:a + 128], QUR, SUR),
               ru + [(nQH, a, a + 128), (nSH, a, a + 128)], [("psC", k, k + 512)])
        elif kind == "k":
            a = 4 * n[0]
            op(e, move(e, T.CC[:, a:a + 4], T.psC[:, 0:2048:512]), [("psC", 0, 2048)], [("CC", a, a + 4)])
        elif kind == "m":
            a = 4 * n[0]
            op("s", act(T.AB[:, a:a + 4], T.CC[:, a:a + 4], ACT.Abs, scale=0.625 * 2.0 ** -23, bias=T.PF[:, 12:13]),
               [("CC", a, a + 4), ("PF", 12, 13)], [("AB", a, a + 4)])
        elif kind == "M":
            a = 4 * n[0]
            op("v", tt(T.UP[:, a:a + 4], T.CC[:, a:a + 4], T.AB[:, a:a + 4], A.add), [("CC", a, a + 4), ("AB", a, a + 4)], [("UP", a, a + 4)])
        elif kind in "sl":
            c, a, b = n
            d, j = UW * c + a + 256 * (a // 512), a + (1024 if e == "s" else 0)
            out, in_ = T.UA[:, d:d + b - a], T.psR[:, j:j + b - a]
            mine = "UP" if kind == "l" and e == "s" else "CC"
            if e == "s":
                call = act(out, in_, ACT.Sign, bias=T[mine][:, c:c + 1], scale=-1.0)
            else:
                call = ts(out, in_, T.CC[:, c:c + 1], None, A.is_lt if kind == "s" else A.is_le)
            op(e, call, [("psR", j, j + b - a), (mine, c, c + 1)], [("UA", d, d + b - a)])
        elif kind == "D":
            c = n[0]
            out, s1, s2 = T.CM[:, 128 * c:128 * c + 128], T.AB[:, c:c + 1], T.CC[:, c:c + 1]
            op(e, act(out, T.LT[:], ACT.Identity, scale=s1, bias=s2) if e == "s" else ts(out, T.LT[:], s1, s2, A.mult, A.add),
               [("LT", 0, 128), ("AB", c, c + 1), ("CC", c, c + 1)], [("CM", 128 * c, 128 * c + 128)])
        elif kind == "e":
            a = 128 * n[0]
            d = UW * n[0] + a + 256 * (a // 512)
            op("v", tt(T.UA[:, d:d + 128], T.psR[:, a:a + 128], T.CM[:, a:a + 128], A.is_lt), [("psR", a, a + 128), ("CM", a, a + 128)], [("UA", d, d + 128)])
        elif kind == "a":
            u = UW * n[0]
            op("v", scan(T.UA[:, u + 512:u + 768], T.UA[:, u:u + 256], T.UA[:, u + 256:u + 512], A.add, A.add), [("UA", u, u + 512)], [("UA", u + 512, u + 768)])
        elif kind == "b":
            u = UW * n[0] + 767
            op("v", scan(T.OU[:, n[0]:2056:8], T.UA[:, u:u + 257], T.UA[:, u + 257:u + 514], A.add, A.add), [("UA", u, u + 514)], [("OU.%d" % n[0], 0, 1)])

    def after(name, plan):
        kind, n = name[0], [int(x) for x in name[1:].split(".")] if name[1:2].isdigit() else []
        every = " ".join(plan.values()).split()

        def some(k, test):
            return [x for x in every if x[0] == k and x[1:2].isdigit() and test([int(y) for y in x[1:].split(".")])]
        sums = "o0 o1 o2 o3 o4 o5 o6 o7"
        fixed = {"i": "u", "U": "u", "d": "Vb Vr", "h": "Vc", "W": "Vb", "Vb": "Va", "Vc": "Vb", "f": sums}
        if name in fixed or kind in fixed:
            return fixed.get(name, fixed.get(kind)).split()
        if kind == "t":
            return ["w" + name[1], "h" + name[1]]
        if kind == "n":
            return some("t", lambda m: n[0] <= 128 * m[0] < n[1])
        if kind == "x":
            return ["t" + name[1]] + sums.split()
        if kind == "y":
            return some("n", lambda m: m[0] < 256 * n[0] + 256 and 256 * n[0] < m[1]) + some("f", lambda m: m[0] // 2 == n[0])
        if kind == "o":
            return ["d" + name[1], "W0"]
        if kind == "g":
            return some("x", lambda m: m[0] == n[0])
        if kind == "q":
            return some("g", lambda m: m[1] < n[1] and n[0] < m[2])
        if kind == "r":
            return some("q", lambda m: m[0] // 512 == n[0]) + [x for x in every if x in ("U0", "i0")]
        if kind == "c":
            return (some("q", lambda m: m[0] < 128 * n[0] + 128 and 128 * n[0] < m[1]) + some("t", lambda m: True)
                    + [x for x in every if x in ("U0", "i0")] + (["k0"] if n[0] > 3 else []))
        if kind == "k":
            return ["c%d" % (4 * n[0] + k) for k in range(4)]
        if kind == "D":
            return ["m%d" % (n[0] // 4)]
        if kind == "e":
            return ["D" + name[1], "r%d.0" % (n[0] // 4)]
        if kind in "mM":
            return [("k%d" if kind == "m" else "m%d") % n[0]]
        if kind in "sl":
            on = name in plan["s"].split()
            return [("M%d" if kind == "l" and on else "k%d") % (n[0] // 4), "r%d.%d" % (n[1] // 512, on)]
        if kind in "ab":
            h = "ab".index(kind)
            mine = some("s", lambda m: m[0] == n[0] and m[1] // 512 == h) + some("l", lambda m: m[0] == n[0] and m[1] // 512 == h)
            return mine + (["e" + name[1]] if n[0] // 4 == h else []) + (["a" + name[1]] if h else [])
        if kind == "z":
            return ["b%d" % c for c in range(n[0], n[1])]
        return []

    def play(t, plan):
        left, done = {e: plan[e].split() for e in plan}, set()
        while any(left.values()):
            ready = [e for e in left if left[e] and all(x in done for x in after(left[e][0], plan))]
            name = left[ready[0]].pop(0)
            step(t, ready[0], name)
            done.add(name)

    for t in range(ROUNDS):
        play(t, LATER if t else FIRST)
        if t == 0:
            op("s", act(T.FVN[:], T.FVP[:].indirect(T.POSL[:, 0:64]), ACT.Copy),
               [("FVP.%d" % q, 0, 1024) for q in range(16)] + [("POSL", 0, 64)], [("FVN", 0, 1024)])
            plane(0)
        nL = "LST%d" % t
        LST, rL = T[nL], [(nL + ".%d" % k, 0, 8) for k in range(4)]
        op("v", lambda: V.transpose(T.TT[:, 0:128], T.WIN[:, 896:1024]), [("WIN", 896, 1024)], [("TT", 0, 128)])
        op("v", lambda: V.transpose(T.TT[:, 128:288], T.WIN[:, 880:1040]), [("WIN", 880, 1040)], [("TT", 128, 288)])
        if t == 0:
            plane(1)
        op("v", tt(T.G0[:], T.TT[:].indirect(T.GL[:, 0:2]), T.SG[:], A.mult), [("TT", 0, 288), ("GL", 0, 2), ("SG", 0, 32)], [("G0", 0, 32)])
        if t == 0:
            plane(2)
        op("v", scan(T.G1[0:64, :], T.G0[0:64, :], T.G0[64:128, :], A.add, A.add), [("G0", 0, 32)], [("G1", 0, 32)])
        for k in range(4):
            op("v", tt(LST[32 * k:32 * k + 32, :], T.G1[0:32, 1:32:4], T.G1[32:64, 1:32:4], A.add), [("G1", 0, 32)], [rL[k]])

        send(t, T["LR%d" % t][:], LST[:], "arrL%d" % t, rL)
        pick_codes("SL%d" % t, "QH%d" % t, 1024, nL, rL)
        pick_scales("s", "SS%d" % t, "SH%d" % t, 1024, nL, rL)
        send(t, T["LC%d" % t][:, 0:128].bitcast(dt.uint8), T["SL%d" % t][:, 0:128].bitcast(dt.uint8), "arrC%d" % t, [("SL%d" % t, 0, 128)])
        send(t, T["LS%d" % t][:, 0:128], T["SS%d" % t][:, 0:128], "arrS%d" % t, [("SS%d" % t, 0, 128)])
        note("a", ("arrL%d" % t, ne), [], [("LR%d" % t, 0, 8)])
        note("a", ("arrC%d" % t, ne), [], [("LC%d" % t, 0, 128)])
        note("a", ("arrS%d" % t, ne), [], [("LS%d" % t, 0, 128)])
        if t + 1 < ROUNDS:
            iota("WIN", [[0, 128]], 0, 0, 896, 1024)
        FLS, nF = T["FLS%d" % t], "FLS%d" % t
        op("s", act(T.FR[:], T.IOT[:].indirect(LST[:, 0:8]), ACT.Copy), [("IOT", 0, 1024)] + rL, [("FR", 0, 128)])
        if t + 1 < ROUNDS:
            pick_scales("s", "SUR%d" % (t + 1), "SU", 128, "UO%d" % (t + 1), [("UO%d" % (t + 1), 0, 8)])
        op("s", act(FLS[:], T.FR[:].indirect(T.REV[:, 0:8]), ACT.Copy), [("FR", 0, 128), ("REV", 0, 8)], [(nF, 0, 128)])
        dma("y", T.fl[t:t + 1, :], FLS[0:1, :], "dout", nout, [(nF, 0, 128)], [])
        if t == 0:
            plane(3)
            op("v", ts(T.MD[:], T.MD0[:], QF, None, A.is_equal), [("MD0", 0, 128)] + rP, [("MD", 0, 128)])
            op("v", ts(T.RM[:], T.MD0[:], 0.0, None, A.is_gt), [("MD0", 0, 128)], [("RM", 0, 128)])
            op("v", cp(T.OFP[:], T.FVT[:]), [("FVT", 0, 64)], [("OFP", 0, 64)])
            op("v", ts(T.KM[:, 128:1040:130], T.PL0[:, 0:8], 0.0, 1.0, A.mult, A.add), [("PL0", 0, 128)], [("KM.W", 0, 8)])
            for m in range(8):
                op("v", ts(T.KM[:, 146 * m:130 * m + 128], T.PL0[:, 16 * m:128], T.QM[:, m:m + 1], None, A.is_gt),
                   [("PL0", 0, 128), ("QM", 0, 8)], [("KM", 146 * m, 130 * m + 128)])
        if t + 1 < ROUNDS:
            pick_codes("QUR%d" % (t + 1), "QU", 128, "UO%d" % (t + 1), [("UO%d" % (t + 1), 0, 8)])
        if t == 1:
            op("v", lambda: V.quantize_mx(T.QWY[:, 0:128], T.SWY[:, 0:128], T.WYB[:, 0:512]), [("WYB", 0, 512)], [("QWY", 0, 128), ("SWY", 0, 128)])
        if t == 2:
            for e in range(4):
                op("v", move("v", T.XF[:, e:2048:4], T["XP%d" % e][:, 0:512], 1.0 / 64), [("XP%d" % e, 0, 512)], [("XF.%d" % e, 0, 4096)])
    play(ROUNDS, LAST)

    for h in range(4):
        a, e = 128 * h, "s" if h < 3 else "v"
        op("v", lambda: V.quantize_mx(T.QX[:, a:a + 128], T.SX[:, a:a + 128], T.XF[:, 4 * a:4 * a + 512]),
           [("XF.%d" % k, 0, 4096) for k in range(4)], [("QX", a, a + 128), ("SX", a, a + 128)])
        op("t", mm(T.psR[:, 4 * a:4 * a + 128], T.QWY[:, 0:128], T.SWY[:, 0:128], T.QX[:, a:a + 128], T.SX[:, a:a + 128]),
           [("QWY", 0, 128), ("SWY", 0, 128), ("QX", a, a + 128), ("SX", a, a + 128)], [("psR", 4 * a, 4 * a + 512)])
        op(e, move(e, T.YS[:, a:a + 128], T.psR[:, 4 * a:4 * a + 128]), [("psR", 4 * a, 4 * a + 128)], [("YS", a, a + 128)])
    for k in "c0 c1 y0 c2 c3 y1 y2 y3".split():
        a = 128 * int(k[1])
        if k[0] == "c":
            dma("y", T.oc[:, 4 * a:4 * a + 512], T.QX[:, a:a + 128].bitcast(dt.uint8), "dout", nout, [("QX", a, a + 128)], [])
        else:
            dma("y", T.y[:, a:a + 128], T.YS[:, a:a + 128], "dout", nout, [("YS", a, a + 128)], [])
    for k in range(4):
        dma("s", T.osc[4 * k:4 * k + 4, :], T.SX[32 * k:32 * k + 4, 0:512], "dout", nout, [("SX", 0, 512)], [])
    for sem in sorted(total):
        if most.get(sem, 0) < total[sem]:
            need("g", (sem, total[sem]))
